import numpy as np, ml_dtypes
CORES = [24,25,26,27,28,29,30,31]
N = 8
import mx_ref
BF = ml_dtypes.bfloat16
def entries(a):
    return np.ascontiguousarray(a.T).reshape(-1)
def table(e):
    return np.ascontiguousarray(np.reshape(e, (-1, 16)).T).astype(np.int32)
def pick(q, e):
    c = np.concatenate([q[0].reshape(128, -1, 4), np.zeros((128, 1, 4), np.uint8)], axis=1); s = np.concatenate([q[1], np.ones((16, 1), np.uint8)], axis=1)
    return (np.ascontiguousarray(c[:, e].reshape(128, -1)), np.ascontiguousarray(s[:, e]))
def join(*qs):
    return (np.concatenate([q[0] for q in qs], axis=1), np.concatenate([q[1] for q in qs], axis=1))
def put(q, e, v):
    c, s = q[0].reshape(128, -1, 4).copy(), q[1].copy(); c[:, e] = v[0].reshape(128, -1, 4); s[:, e] = v[1]
    return (c.reshape(128, -1), s)
def pk(c, s):
    return (np.ascontiguousarray(c), mx_ref.live(s))
def emit(q):
    return q[0], q[1]
def cut(t, i, w=512):
    return t[:, w * i:w * i + w]
def f(rng, *shape):
    return mx_ref.flush((rng.standard_normal(shape, dtype=np.float32) * np.exp2(rng.integers(-2, 3, shape[:-1] + (1,)))).astype(BF))
def wide(rng, *shape, cols=0):
    v = rng.standard_normal(shape, dtype=np.float32) * np.exp2(rng.integers(-12, 13, shape)).astype(np.float32)
    if cols: v *= np.repeat(np.exp2(rng.integers(-cols, cols + 1, shape[:-2] + (1, shape[-1] // 4))) * (rng.random(shape[:-2] + (1, shape[-1] // 4)) > 0.0625), 4, axis=-1).astype(np.float32)
    return mx_ref.flush(v.astype(BF))
P, K, R, LC = 256, 32, 3, 48
def near(nb):
    return np.stack([entries(nb[r]).reshape(P, 3) for r in range(N)]).astype(np.int64)
def play(x, bb, nb, u, v, a):
    n = near(nb)
    X = join(*[mx_ref.quantize(np.ascontiguousarray(x[r])) for r in range(N)])
    qu, qv = mx_ref.quantize(np.ascontiguousarray(u[0])), mx_ref.quantize(np.ascontiguousarray(v[0]))
    qa = [[mx_ref.quantize(np.ascontiguousarray(cut(a[r], i))) for i in range(4)] for r in range(N)]
    fixed = [mx_ref.matmul(qv, mx_ref.quantize(np.ascontiguousarray(bb[r])))[0] for r in range(N)]
    b = bb.astype(np.float32).reshape(N, 128, P, 4)
    done, res, made = np.zeros((N, R, K), np.int64), [], []
    for t in range(R):
        e = mx_ref.matmul(qu, X)[0]
        new = []
        for r in range(N):
            z = ((e[n[r, :, 0]] + e[n[r, :, 1]]) + e[n[r, :, 2]]) - fixed[r]
            j = np.argsort(-np.abs(z), kind="stable")[:K]
            nbs = pick(X, n[r, j].T.reshape(-1))
            s = []
            for i in range(4):
                m = mx_ref.matmul(qa[r][i], nbs)
                s.append((m[:, :K] + m[:, K:2 * K]) + m[:, 2 * K:])
            g = np.float32(0.05) * np.stack(s, axis=2) + b[r][:, j]
            new.append(mx_ref.quantize(np.ascontiguousarray(g.reshape(128, -1).astype(BF))))
            done[r, t] = j
            res.append(z)
            made.append(g)
        X = put(X, np.concatenate([P * r + done[r, t] for r in range(N)]), join(*new))
    return X, done, np.stack(res), np.stack(made)
def fit(z, g):
    top = np.abs(g.astype(BF).astype(np.float32)).reshape(-1, 16, 8, K, 4).max(axis=(2, 4))
    g = np.abs(g)
    return bool(np.isfinite(z).all() and np.isfinite(g).all() and ((g == 0) | (g >= 2.0 ** -60) & (g <= 2.0 ** 60)).all() and ((top == 0) | (top >= 2.0 ** -30) & (top <= 2.0 ** 30)).all())
def bf(v):
    return mx_ref.flush(np.asarray(v, np.float32).astype(BF))
def lone(c):
    t = np.zeros((N, 128, 512), BF)
    t[:, :, :4] = c
    return t
def few(rng, q, n, free, most):
    p = rng.permutation(free)[:most]
    return q * P + rng.permutation(np.concatenate([p, p[rng.integers(0, p.size, P)]])[:n])
def graph(rng, src=None, free=None, most=LC):
    n = np.zeros((N, P, 3), np.int64)
    if free is None: free = [np.arange(P)] * N
    for r in range(N):
        n[r, :, :2] = r * P + rng.choice(free[r], (P, 2))
        s = (r + rng.integers(1, N, P)) % N if src is None else np.full(P, src[r])
        for q in range(N):
            i = np.flatnonzero(s == q)
            n[r, i, 2] = few(rng, q, i.size, free[q], most)
    return n
def stored(n):
    return np.stack([table(n[r].reshape(-1)) for r in range(N)])
def setup_inputs(rng):
    return {"x": f(rng, N, 128, 4 * P), "bb": f(rng, N, 128, 4 * P), "nb": stored(graph(rng)), "u": lone(f(rng, 128, 4)), "v": lone(f(rng, 128, 4)),
            "a": bf(f(rng, N, 128, 2048).astype(np.float32) * np.float32(2.0 ** -4)), "w": f(rng, N, 128, 512)}
def signs(rng):
    return 1.0 - 2.0 * rng.integers(0, 2, (128, 4))
def signed(rng, sg, size):
    return bf(((1 + rng.random((N, 128, P, 4))) * size[:, None, :, None] * sg[:, None, :] + 0.0).reshape(N, 128, 4 * P))
def single(rng, sg, size):
    return lone(bf((1 + rng.random((128, 4))) * sg * size))
def setup_inputs_again(rng):
    d, sg, size, m = setup_inputs(rng), signs(rng), np.zeros((N, P)), K // 8
    o = np.stack([rng.permutation(P) for r in range(N)])
    rest = np.sort(o[:, 7 * m:], axis=1)
    hold = np.stack([rng.permutation(rest[r, -5:]) for r in range(N)])
    n = graph(rng, free=rest[:, :-5], most=LC - 2)
    large, small = (1 + rng.random((128, 4))) * sg * 2.0 ** 20, (1 + rng.random((128, 4))) * sg * 2.0 ** -8
    top = np.arange(128)[:, None] < 64
    five = np.stack([large * top, large * ~top, -large, large, small], axis=1) + 0.0
    x = np.zeros((N, 128, P, 4))
    for r in range(N):
        x[r][:, hold[r]] = five
        h, left, both, alone = o[r, :4 * m], o[r, 4 * m:5 * m], o[r, 5 * m:6 * m], o[r, 6 * m:7 * m]
        size[r, h] = 64
        size[r, left] = 64
        n[r, h, 0] = r * P + rng.permutation(h)
        n[r, left, 0], n[r, left, 1] = r * P + hold[r, 0], r * P + hold[r, 1]
        n[r, both, 0], n[r, both, 1] = r * P + hold[r, 3], r * P + hold[r, 2]
        for i, k in ((left, 2), (both, 4), (alone, 4)):
            q = n[r, i, 2] // P
            n[r, i, 2] = q * P + hold[q, k]
    bb = signed(rng, sg, size).reshape(N, 128, P, 4)
    for r in range(N): bb[r][8:, o[r, 4 * m:5 * m]] = 0
    d.update(x=bf(x.reshape(N, 128, 4 * P)), bb=bb.reshape(N, 128, 4 * P), nb=stored(n), u=single(rng, sg, 1.0), v=single(rng, sg, 4.0))
    return d
def setup_inputs_far(rng):
    h = int(rng.integers(0, N))
    src = np.full(N, h)
    src[h] = (h + int(rng.integers(1, N))) % N
    d, n, sg, size = setup_inputs(rng), graph(rng, src), signs(rng), np.full((N, P), 2.0 ** 20)
    for r in range(N):
        first = np.unique(n[r, :, 2], return_index=True)[1]
        size[r, rng.permutation(first)[:K]] = 2.0 ** 26
    d.update(x=signed(rng, sg, np.full((N, P), 2.0 ** 20)), bb=signed(rng, sg, size), nb=stored(n), u=single(rng, sg, 2.0 ** 23), v=single(rng, sg, 2.0 ** 29))
    return d
def setup_inputs_moved(rng):
    d, n, sg, size = setup_inputs(rng), np.zeros((N, P, 3), np.int64), signs(rng), np.full((N, P), 2.0 ** -4)
    o = [rng.permutation(P) for r in range(N)]
    for r in range(N):
        size[r, o[r][:K]] = 64
        n[r, :, :2] = r * P + rng.choice(o[r][K:], (P, 2))
        m = np.zeros(P, bool)
        m[rng.permutation(P)[:K + K // 2]] = True
        s = (r + rng.integers(1, N, P)) % N
        for q in range(N):
            hot, cold = rng.permutation(o[q][:K])[:LC // 2], rng.permutation(o[q][K:])[:LC - LC // 2]
            i, k = np.flatnonzero((s == q) & m), np.flatnonzero((s == q) & ~m)
            n[r, i, 2] = q * P + rng.choice(hot, i.size)
            n[r, k, 2] = q * P + rng.choice(cold, k.size)
    d.update(x=signed(rng, sg, np.full((N, P), 2.0 ** -6)), bb=signed(rng, sg, size), nb=stored(n), u=single(rng, sg, 16.0), v=single(rng, sg, 1.0))
    return d
def setup_inputs_spread(rng):
    d = setup_inputs(rng)
    d["x"] = wide(rng, N, 128, 4 * P, cols=4)
    d["bb"] = wide(rng, N, 128, 4 * P, cols=4)
    return d
def setup_inputs_ties(rng):
    d, n = setup_inputs(rng), np.zeros((N, P, 3), np.int64)
    kind = np.stack([rng.permutation(np.arange(P) % 4) for r in range(N)])
    for k in ("x", "bb"):
        c = f(rng, 128, 8).astype(np.float32).reshape(128, 2, 4)
        d[k] = np.stack([bf((c[:, kind[r] >> 1] * (1 - 2 * (kind[r] & 1))[None, :, None]).reshape(128, -1)) for r in range(N)])
    for r in range(N):
        s = (r + rng.integers(1, N, P)) % N
        for k in range(4):
            i = np.flatnonzero(kind[r] == k)
            n[r, i, 0] = r * P + rng.choice(i, i.size)
            n[r, i, 1] = r * P + rng.choice(np.flatnonzero(kind[r] == (k ^ 2)), i.size)
            for q in range(N):
                j = i[s[i] == q]
                n[r, j, 2] = q * P + rng.choice(rng.permutation(np.flatnonzero(kind[q] == k))[:LC // 4], j.size)
    d["nb"] = stored(n)
    return d
def check_inputs(d):
    b = []
    for k in ("x", "bb", "u", "v", "a", "w"):
        t = np.abs(d[k].astype(np.float32))
        if not (np.isfinite(t).all() and ((t == 0) | (t >= 2.0 ** -30) & (t <= 2.0 ** 30)).all()): b.append("a value of " + k)
    for k in ("u", "v"):
        t = d[k].astype(np.float32)
        if (t[:, :, 4:] != 0).any(): b.append(k + " has numbers behind its column 0")
        if (t != t[:1]).any(): b.append(k + " isn't the same on all ranks")
    n = near(d["nb"])
    at, own = n // P, np.arange(N)[:, None, None]
    if n.min() < 0 or n.max() >= N * P or (at[:, :, :2] != own).any() or (at[:, :, 2] == own[:, :, 0]).any(): b.append("nb")
    elif any(np.unique(n[r, :, 2][at[r, :, 2] == q]).size > LC for r in range(N) for q in range(N)): b.append("nb names too many columns of one rank")
    if not b:
        try:
            with np.errstate(all="ignore"):
                X, done, z, g = play(d["x"], d["bb"], d["nb"], d["u"], d["v"], d["a"])
                good = fit(z, g)
        except Exception:
            good = False
        if not good: b.append("a number that the rounds make")
    return b
def reference(x, bb, nb, u, v, a, w):
    X, done, z, g = play(x, bb, nb, u, v, a)
    oc, osc, y = np.zeros((N, 128, 4 * P), np.uint8), np.zeros((N, 16, P), np.uint8), np.zeros((N, 128, P), np.float32)
    for r in range(N):
        q = pick(X, np.arange(P * r, P * r + P))
        oc[r], osc[r] = emit(q)
        y[r] = mx_ref.matmul(mx_ref.quantize(np.ascontiguousarray(w[r])), q)
    return {"oc": oc, "osc": osc, "nd": done.astype(np.float32), "y": y}

@@ -1,0 +1,687 @@
+import numpy as np
+from concourse.bass import DstId, RemoteDMATransfer
+from concourse.mybir import dt, AluOpType, AxisListType, ActivationFunctionType
+
+A = AluOpType
+F = ActivationFunctionType
+P, K, R, LC = 256, 32, 3, 48
+FAR0 = P
+NEW0 = P + 7 * LC
+C05 = 13421773 * 2.0 ** -28
+THIRD = float(np.float32(1.0) / np.float32(3.0))
+KC = 1024 * 255
+TINY = 2.0 ** -110
+CYC, HOLD, FLY, FIRST, LOAD = 0.001, 0.25, 2.4, 2.0, 2.2
+ORDER = """
+21 282 14 15 4 11 12 7 1 6 10 5 13 0 3 9 2 8 16 20 36 28 22 37 27 30 29 272 31 35 84 200 32 39 23 34 209 33 41 211 38 108 44 292 17 110
+46 124 40 127 45 50 18 291 47 42 288 135 256 109 125 48 19 43 111 128 289 112 287 49 290 210 126 188 129 113 52 51 136 114 53 55 56 116
+54 57 122 58 144 115 117 60 217 185 118 186 64 59 187 63 25 119 61 67 153 148 131 66 137 68 271 69 138 62 70 73 71v 72s 205 183 139 24
+74 75 195 65 79 218 184 77 189 81 76 78 190 83 86 132 147 82 80 130 145 85 93 146 87s 88v 90 89 206 94 92v 91s 95 401 98 97 101 99 102
+216 96 100 104 106 140 105 103 107 123 227 141 120 212 150 191 149 121 142 235 228 276 219 143 229 236 196 249 226v 202 151 284 230 199
+232 152 197 250 198 273 165 158s 251 166s 160s 233 167s 162 164s 163 161s 154 159 156s 155 168 234 157s 224 170 231 169 213 204 252 283
+201 220 172s 277 171 257 237 174 253 178 258 181s 26 259 175s 238 179s 254 177s 182 260 173s 180v 223 176v 203 261 214 264 263 262 304
+266 265 305 208 269 306s 239 221 312 308s 270 309 267 307 240 241s 314 310 268 274 311 242 313 316 322 245s 318 243s 315 244 225 323 246
+324 248 317 321 247s 319 207 255 325 320 275 298 133 222 326 280 134 327 279v 329 333 334 215 192 335s 336v 330 339 328 338 337 278 285
+340 193 332 331 341 347 344 345 346s 342 296 349 348s 343 360 359 399 351 350 281 353 361 352 293 363 354 528 286 368 362 357 355 358
+370 372 364 297 366 356 369 374 301 299 365 371 402 380 375 294 373 367 377 378 376 379 300 405 384 381 382 386 295 385 383 387 302 388
+303 406 194 389 394 398 400 391 390 392 407 403 408 529 417 409 410 414 527 413 421 526 393 411 404 422 397 423 395 416 424 425v 427s
+426s 412 428 530 415 429 436 432s 431 433v 430s 437 438 434s 440 435 445 420 439 441 442 418 446 448 447 443 419 449 444 450 451 454 452
+453 456 458v 457s 459s 460v 463 461 462 455 464 468s 470 469v 471v 465s 473v 472s 466 521 474 475 467 522 476 483 484 477 485 478 488
+479 482 481 396 523 492 486 489 480 495 487 496 493 501 490 494 503 497 498 499 510 491 500 502 504 506 511 508 505 507 509 512 513 517
+518 515 514 516 531 532 533 537 540 534 535 536 545 539 546 547 519 541 548 550 551s 549 538 542 552 544v 553 560 557 554s 555v 556s 562
+561 559 570 558s 563 543 569 571 572 566 565 564 573 567 574 568 575 578 576 577 580 582v 581s 583s 584v 579 587 585 586 592 594s 593v
+595 588 597 596 589 599 598 590 601 639 600 591 524 602 604 605 525 603 520 608 625 609 626 615 606 616 620 607 635 610 611 622 623 640
+624 613 612v 614 633 617 631 618 634 619 621 642 627 629 632 628 630 643 636 637 644 645 638 648 651 652 647 649 641 646 650 653
+"""
+CODE, U8, BF, F32, I32, U16 = "float8_e4m3fn_x4", "uint8", "bfloat16", "float32", "int32", "uint16"
+
+
+def _sbuf(dtype, **cols):
+    return {n: ("sbuf", [128, c], dtype) for n, c in cols.items()}
+
+
+SCRATCH = {"pe": ("psum", [128, 512], F32), "pf": ("psum", [128, 512], F32), "ps": ("psum", [128, 2048], F32), "py": ("psum", [128, 512], F32)}
+SCRATCH.update(_sbuf(F32, nbf=768, iot=2048, jr=256, jf=256, cf=64, jo=6, ka=256, kat=64, junk=2560, cq=1024, cz=512, ac=32, fa=28,
+                     sp=192, ex=768, cc=128, lo=16, ea=1104, fn=256, z=256, zt=64, dd=128, jj=128, zs=256, d0z=256, d1z=256, cx=320, cr=64,
+                     cl=256, sa_=4, sb_=8, sel=24, kk=264, ng=96, nt=96, nd_=12, bbs=128, sc4=512, nda0=16, nda1=16,
+                     np0=2048, ndv=512, nl=1536, db=192, dbz=192, dt_=192, dtz=192, ol=256, od=96, og=256, ogt=256, yt=256,
+                     ep=2, er=14, es=448, est=480, fz=256, d0r=448, d1r=448, zr=448, rl=32, rl2=96, lst=4, yw=352))
+SCRATCH.update(_sbuf(I32, nb32=48, ci=16, fi=16, frf=256, gi=128))
+SCRATCH.update(_sbuf(U16, nbt=48, far16=16, pm=16, rep=24, so=6, po=6, ndl=2, nai=16, bo=8, dbt=12, dnb=12, of=36, frt=36, d8=16, oo=16))
+SCRATCH.update(_sbuf(BF, xb=1024, bb_t=1024, at=2048, wt=512, u4=4, v4=4, ub=512, vb=512, mm_=640, xt=512))
+for _c, _s, _n in (("qx", "sx", 256), ("qb", "sb", 256), ("qu", "su", 128), ("qv", "sv", 128), ("qa", "sa", 512), ("qw", "sw", 128), ("slc", "sls", 336),
+                   ("g0", "h0", 592), ("g1", "h1", 944), ("g2", "h2", 1200), ("nq0", "ns0", 128), ("nq1", "ns1", 128), ("nq2", "ns2", 128),
+                   ("ow", "os_", 448), ("occ", "ocs", 256)):
+    SCRATCH.update({_c: ("sbuf", [128, _n], CODE), _s: ("sbuf", [128, _n], U8)})
+SEMAPHORES = ["cv", "cs", "ct", "cg"] + ["q%d" % i for i in range(60)] + ["aer", "arl", "ac0", "as0", "an0", "an1", "ac1", "as1", "ac2", "as2"]
+
+
+def r(name, c0, c1, step=1, p0=0, p1=128):
+    return (name, c0, c1, step, p0, p1)
+
+
+def rank_program(g, core, T, topo):
+    rank = T.rank_of(core)
+    if rank is None:
+        return
+    eng = {"v": g.vector, "s": g.scalar, "t": g.tensor, "g": g, "y": g.sync}
+    csem = {"v": "cv", "s": "cs", "t": "ct", "g": "cg"}
+    cnt, known, log, pool, snaps, ops = {}, {q: {} for q in eng}, {}, [0], {}, []
+
+    def ap(x):
+        return T[x[0]][x[4]:x[5], x[1]:x[2]:x[3]] if x[3] != 1 else T[x[0]][x[4]:x[5], x[1]:x[2]]
+
+    def span(x):
+        if SCRATCH[x[0]][0] == "psum":
+            return x[1] // 512 * 512, (x[2] + 511) // 512 * 512, 0, 128
+        return x[1], x[2], x[4], x[5]
+
+    def learn(q, tok):
+        k, (sem, c) = known[q], tok
+        if k.get(sem, 0) >= c:
+            return
+        k[sem] = c
+        for n, m in snaps.get(tok, {}).items():
+            if k.get(n, 0) < m:
+                k[n] = m
+
+    def clash(a, b):
+        return not (a[3] == b[3] and a[3] > 1 and (a[1] - b[1]) % a[3])
+
+    def meets(reads, writes, q):
+        deps = set()
+        for x, w in [(x, 0) for x in reads] + [(x, 1) for x in writes]:
+            s = span(x)
+            bank = SCRATCH[x[0]][0] == "psum"
+            for y, t, w2, i, q2 in log.get(x[0], []):
+                if (w or w2 or (bank and q2 != q)) and s[0] < t[1] and t[0] < s[1] and s[2] < t[3] and t[2] < s[3] and clash(x, y):
+                    deps.add(i)
+        return deps
+
+    def note(q, reads, writes, i):
+        for x in writes:
+            s = span(x)
+            if x[3] == 1:
+                log[x[0]] = [e for e in log.get(x[0], []) if not (s[0] <= e[1][0] and e[1][1] <= s[1] and s[2] <= e[1][2] and e[1][3] <= s[3])]
+            log.setdefault(x[0], []).append((x, s, 1, i, q))
+        for x in reads:
+            log.setdefault(x[0], []).append((x, span(x), 0, i, q))
+
+    def put(q, fn, reads, writes, cost, late=0.0, sem=None, inc=1, deps=(), alt=False):
+        i = len(ops)
+        ops.append({"q": q, "fn": fn, "deps": meets(reads, writes, q) | set(deps), "cost": cost, "late": late, "sem": sem, "inc": inc, "alt": alt, "peers": [i]})
+        note(q, reads, writes, i)
+        return i
+
+    def emit(q, fn, reads, writes, cycles, fixed=0.0, deps=(), alt=False):
+        put(q, fn, reads, writes, fixed + max(64, cycles) * CYC, deps=deps, alt=alt)
+
+    def width(x):
+        return -(-(x[2] - x[1]) // x[3])
+
+    def flush():
+        for i, o in enumerate(ops):
+            for k in list(o["deps"]):
+                o["deps"] |= set(ops[k]["peers"])
+            o["deps"].discard(i)
+        out = [int(x.rstrip("vs")) for x in ORDER.split()] or list(range(len(ops)))
+        for x in ORDER.split():
+            if x[-1] in "vs":
+                ops[int(x[:-1])]["q"] = x[-1]
+        tok = {}
+        for i in out:
+            o = ops[i]
+            q = o["q"]
+            need = {}
+            if q == "g" and o["sem"] is None and "cg" in cnt:
+                need["cg"] = cnt["cg"]
+            for k in o["deps"]:
+                need[tok[k][0]] = max(need.get(tok[k][0], 0), tok[k][1])
+            if q != "r":
+                for sem, c in sorted(need.items(), key=lambda e: -sum(snaps.get(e, {}).values())):
+                    if known[q].get(sem, 0) < c:
+                        eng[q].wait_ge(T.sem[sem], c)
+                        learn(q, (sem, c))
+            sem = o["sem"] or csem[q]
+            cnt[sem] = cnt.get(sem, 0) + 1 if o["sem"] is None else o["inc"]
+            tok[i] = (sem, cnt[sem])
+            if q != "r":
+                s = snaps.setdefault(tok[i], {})
+                for n, m in known[q].items():
+                    s[n] = max(s.get(n, 0), m)
+                c = o["fn"](q) if o["alt"] else o["fn"]()
+                if o["sem"] is None:
+                    c.then_inc(T.sem[sem], 1)
+
+    def newsem():
+        pool[0] += 1
+        return "q%d" % (pool[0] - 1)
+
+    def src(x):
+        if len(x) == 2:
+            return ap(x[0]).indirect(ap(x[1])), [x[0], x[1]]
+        return ap(x), [x]
+
+    def sc(x):
+        return (ap(x), [x]) if isinstance(x, tuple) else (x, [])
+
+    def by(in_):
+        return 1.5 if len(in_) == 2 else 1
+
+    def copy(q, out, in_):
+        i, rd = src(in_)
+        n = width(out) * by(in_)
+        names = [out[0]] + [x[0] for x in rd]
+        flex = all(SCRATCH[k][0] == "sbuf" and SCRATCH[k][2] in (F32, BF) for k in names[:2])
+        fns = {"v": lambda: g.vector.tensor_copy(ap(out), i), "s": lambda: g.scalar.activation(ap(out), i, F.Copy)}
+        emit(q, (lambda e: fns[e]()) if flex else fns[q], rd, [out], n, alt=flex)
+
+    def times(out, in_, c):
+        fns = {"v": lambda: g.vector.tensor_scalar(ap(out), ap(in_), ap(c), None, A.mult), "s": lambda: g.scalar.activation(ap(out), ap(in_), F.Copy, scale=ap(c))}
+        emit("v", lambda e: fns[e](), [in_, c], [out], width(out), alt=True)
+
+    def scatter(win, off, in_):
+        emit("v", lambda: g.vector.tensor_copy(ap(win).indirect(ap(off)), ap(in_)), [in_, off], [win], 3 * width(in_))
+
+    def act(out, in_, func, bias=0.0, scale=1.0, acc=None):
+        i, rd = src(in_)
+        b, rb = sc(bias)
+        s, rs = sc(scale)
+        n = width(out) * by(in_)
+        if acc is None:
+            emit("s", lambda: g.scalar.activation(ap(out), i, func, bias=b, scale=s), rd + rb + rs, [out], n)
+        else:
+            emit("s", lambda: g.scalar.activation(ap(out), i, func, bias=b, scale=s, accum_out=ap(acc)), rd + rb + rs, [out, acc], n)
+
+    def const(out, val):
+        act(out, r("iot", 0, width(out), 1, out[4], out[5]), F.Copy, bias=val, scale=0.0)
+
+    def lin(out, in_, scale, bias):
+        act(out, in_, F.Identity if isinstance(bias, tuple) else F.Copy, bias=bias, scale=scale)
+
+    def ts(out, in_, s1, op0, s2=None, op1=None):
+        i, rd = src(in_)
+        a, ra = sc(s1)
+        b, rb = sc(s2)
+        if op1 is None:
+            emit("v", lambda: g.vector.tensor_scalar(ap(out), i, a, None, op0), rd + ra, [out], width(out))
+        else:
+            emit("v", lambda: g.vector.tensor_scalar(ap(out), i, a, b, op0, op1), rd + ra + rb, [out], width(out))
+
+    def tt(out, in0, in1, op):
+        i, rd = src(in0)
+        emit("v", lambda: g.vector.tensor_tensor(ap(out), i, ap(in1), op), rd + [in1], [out], (1.5 if len(in0) == 2 else 2) * width(out))
+
+    def scan(out, d0, d1, initial, op0, op1):
+        a, ra = sc(initial)
+        emit("v", lambda: g.vector.tensor_tensor_scan(ap(out), ap(d0), ap(d1), a, op0, op1), [d0, d1] + ra, [out], width(out))
+
+    def least(out, in_):
+        emit("v", lambda: g.vector.tensor_reduce(ap(out), ap(in_), AxisListType.X, A.min, apply_absolute_value=True), [in_], [out], width(in_))
+
+    def tr(out, in_):
+        emit("v", lambda: g.vector.transpose(ap(out), ap(in_)), [in_], [out], width(out))
+
+    def fill(out, val):
+        emit("v", lambda: g.vector.memset(ap(out), val), [], [out], width(out))
+
+    def quant(q, s, in_):
+        emit("v", lambda: g.vector.quantize_mx(ap(q), ap(s), ap(in_)), [in_], [q, s], width(in_) // 4)
+
+    def mm(out, wq, ws, xq, xs):
+        emit("t", lambda: g.tensor.matmul_mx(ap(out), ap(wq), ap(ws), ap(xq), ap(xs), True, True), [wq, ws, xq, xs], [out], width(out))
+
+    def iota(out, pattern, base, cm, flag=True, after=()):
+        if flag:
+            emit("g", lambda: g.iota(ap(out), pattern, base, cm, allow_small_or_imprecise_dtypes=True), [], [out], 2 * width(out), 0.13, after)
+        else:
+            emit("g", lambda: g.iota(ap(out), pattern, base, cm), [], [out], 2 * width(out), 0.13, after)
+
+    def pick(qo, so, win, wins, off):
+        emit("v", lambda: g.vector.tensor_copy(ap(qo).bitcast(dt.uint32), ap(win).bitcast(dt.uint32).indirect(ap(off))), [win, off], [qo], 1.5 * width(qo))
+        emit("s", lambda: g.scalar.activation(ap(so), ap(wins).indirect(ap(off)), F.Copy), [wins, off], [so], 1.5 * width(so))
+
+    def side(x):
+        return ap(x).bitcast(dt.uint8) if SCRATCH[x[0]][2] == CODE else ap(x)
+
+    def dma(moves, late=LOAD):
+        sem = newsem()
+        made = []
+        for q, out, in_ in moves:
+            wr = [out] if isinstance(out, tuple) else []
+            rd = [in_] if isinstance(in_, tuple) else []
+            o, i = side(out) if wr else out, side(in_) if rd else in_
+            made.append(put(q, lambda q=q, o=o, i=i: eng[q].dma_start(o, i).then_inc(T.sem[sem], 16), rd, wr, 0.07, late, sem, 16 * len(moves)))
+        for k in made:
+            ops[k]["peers"] = made
+
+    peers = [(rank + 1 + i) % 8 for i in range(7)]
+    ids = {}
+    for d in peers:
+        rid, pid, _ = topo.addr(T.cores[d])
+        ids[d] = DstId(rid=rid, pnc=pid)
+    full = topo.engines(core, T.cores[peers[0]])
+    across = [d for d in peers if topo.die(T.cores[d]) != topo.die(core)]
+    masks = {}
+    for d in peers:
+        e = topo.engines(core, T.cores[d])
+        lane = e[0::2] if d in across else e[1::2]
+        k = (across if d in across else [s for s in peers if s not in across]).index(d)
+        masks[d] = sum(1 << x for x in lane[2 * k:2 * k + 2])
+
+    def issue(trs, reads, total):
+        sem = newsem()
+        return put("g", lambda: g.remote_dma_fused(trs, local_sem=T.sem[sem]), reads, [], HOLD, FLY - 0.5, sem, total)
+
+    def send_each(moves, arr, regions):
+        i = issue([RemoteDMATransfer(dst_ids=[ids[d]], dma_engine_mask=masks[d], remote_sem=T.sem[arr], srcs=[side(s)], dsts=[side(l)]) for d, s, l in moves],
+                  [m[1] for m in moves], 2 * len(moves))
+        put("r", None, [], regions, 0.0, 2.0, arr, 2 * 7, [i])
+
+    def send_all(s, land, arr, regions, more=0.0):
+        i = issue([RemoteDMATransfer(dst_ids=[ids[d] for d in peers], dma_engine_mask=sum(1 << x for x in full), remote_sem=T.sem[arr], srcs=[side(s)],
+                                     dsts=[side(land(d)) for d in peers])], [s], len(full))
+        put("r", None, [], regions, 0.0, 0.5 + more, arr, len(full) * 7, [i])
+        return i
+
+    def exchange(n, w=64, o=0):
+        for a in range(4):
+            b = (a + 1) % 4
+            copy("vs"[a % 2], r(n, o + w, o + 2 * w, 1, 32 * a, 32 * a + 32), r(n, o, o + w, 1, 32 * b, 32 * b + 32))
+        copy("v", r(n, o + 2 * w, o + 4 * w, 1, 0, 64), r(n, o, o + 2 * w, 1, 64, 128))
+        copy("s", r(n, o + 2 * w, o + 4 * w, 1, 64, 128), r(n, o, o + 2 * w, 1, 0, 64))
+
+    def col(n, c, w=1):
+        return r(n, c, c + w)
+
+    def blk(n, c0, c1, a):
+        return r(n, c0, c1, 1, 32 * a, 32 * a + 32)
+
+    def junk(i):
+        return r("junk", 256 * i, 256 * i + 256)
+
+    def total(i, x, c):
+        scan(r("cz", 128 * i, 128 * i + 128), r(x, c, c + 128), r(x, c + 128, c + 256), 0.0, A.add, A.add)
+        return col("cz", 128 * i + 127)
+
+    mv = []
+    for gr in range(8):
+        a = gr // 2
+        q = "ys"[gr % 2]
+        mv.append((q, r("nb32", 0, 48 - 12 * a, 1, 16 * gr, 16 * gr + 16), T.nb[:, 12 * a:48]))
+        if a:
+            mv.append((q, r("nb32", 48 - 12 * a, 48, 1, 16 * gr, 16 * gr + 16), T.nb[:, 0:12 * a]))
+    dma(mv)
+    dma([("y", r("xb", 0, 1024), T.x[:])])
+    dma([("s", r("u4", 0, 4), T.u[:, 0:4]), ("s", r("v4", 0, 4), T.v[:, 0:4])])
+    dma([("y", r("bb_t", 0, 1024), T.bb[:])])
+    dma([("y", r("at", 0, 2048), T.a[:])])
+    dma([("y", r("wt", 0, 512), T.w[:])])
+
+    C4096, CM128, C1024, CONE = r("cc", 0, 32), r("cc", 32, 64), r("cc", 64, 96), r("cc", 96, 128)
+    iota(r("ci", 0, 1), [[0, 1]], 0, 1, False)
+    iota(r("iot", 0, 256), [[1, 256]], 0, 0)
+    iota(r("kk", 24, 72), [[0, 16], [1, 3]], 0, 0)
+    iota(r("iot", 1536, 2048), [[1, 512]], 1536, 0)
+    iota(r("lo", 8, 11), [[4096, 3]], 0, 0)
+    iota(r("kk", 6, 18), [[1, 3], [96, 2], [0, 2]], 0, 0)
+    iota(r("kk", 0, 6), [[1, 3], [0, 2]], 768, 0)
+    ts(r("ci", 1, 2), r("ci", 0, 1), 31, A.bitwise_and)
+    ts(r("ci", 2, 3), r("ci", 0, 1), 15, A.bitwise_and)
+    copy("v", r("cf", 0, 3), r("ci", 0, 3))
+    ts(r("ci", 3, 4), r("ci", 2, 3), 11.0, A.mult)
+    ts(r("ci", 4, 5), r("ci", 3, 4), 5, A.arith_shift_right)
+    ts(col("cf", 40), r("ci", 4, 5), -3.0, A.mult, col("cf", 2), A.add)
+    ts(r("kk", 72, 120), r("kk", 24, 72), col("cf", 40), A.add, 2.0, A.is_equal)
+    ts(r("kk", 120, 168), r("kk", 24, 72), 0.5, A.is_gt)
+    ts(col("cf", 26), col("cf", 0), col("cf", 1), A.subtract, 2.0, A.mult)
+    ts(r("iot", 256, 512), r("iot", 0, 256), 256.0, A.add)
+    act(r("iot", 512, 1024), r("iot", 0, 512), F.Copy, bias=512.0)
+    act(r("iot", 1024, 1536), r("iot", 0, 512), F.Copy, bias=1024.0)
+    ts(r("frf", 0, 256), r("iot", 0, 256), col("cf", 26), A.add)
+    tt(col("jo", 0), col("cf", 26), col("cf", 1), A.add)
+    ts(r("frf", 0, 256), r("frf", 0, 256), 255, A.bitwise_and)
+    ts(col("jo", 1), col("jo", 0), 32.0, A.add)
+    ts(r("jo", 2, 4), r("jo", 0, 2), 1.0 / 512, A.mult)
+    copy("v", r("jr", 0, 256), r("frf", 0, 256))
+    lin(r("jf", 0, 256), r("jr", 0, 256), 1.0 / 512, 0.0)
+
+    tt(r("kk", 168, 216), r("nb32", 0, 48), r("kk", 72, 120), A.mult)
+    scan(r("kk", 216, 264), r("kk", 120, 168), r("kk", 168, 216), 0.0, A.mult, A.add)
+    copy("v", r("far16", 0, 16), r("kk", 218, 264, 3))
+    tt(r("ka", 0, 256), (r("iot", 0, 2048), r("far16", 0, 16)), r("jf", 0, 256), A.add)
+    fill(C4096, 4096.0)
+    fill(CM128, -128.0)
+    tr(r("kat", 0, 64), r("ka", 0, 64))
+    tt(r("jo", 4, 6), r("jo", 2, 4), r("kat", 0, 64, 32), A.subtract)
+    ts(junk(0), r("ka", 0, 256), col("jo", 4), A.add)
+    act(junk(6), r("ka", 0, 256), F.Sign, bias=col("kat", 32), scale=-1.0, acc=col("ac", 1))
+    ts(col("ac", 17), col("kat", 32), -0.5, A.add)
+    act(junk(8), r("ka", 0, 256), F.Sign, bias=col("ac", 17), scale=-1.0, acc=col("ac", 18))
+    ts(r("fa", 0, 2), r("jo", 4, 6), -1.0, A.mult)
+    ts(r("fa", 2, 4), r("jo", 4, 6), 0.5, A.add)
+    least(col("ac", 0), junk(0))
+    copy("v", r("fi", 0, 2), r("fa", 0, 2))
+    ts(r("fi", 2, 4), r("fi", 0, 2), 255, A.bitwise_and)
+    tt(col("ac", 6), col("ac", 0), col("jo", 2), A.not_equal)
+    ts(col("ac", 7), col("ac", 1), col("ac", 18), A.subtract, 1.0, A.not_equal)
+    copy("v", r("fa", 4, 6), r("fi", 2, 4))
+    ts(r("sp", 0, 32), C4096, col("ac", 6), A.mult, col("fa", 0), A.add)
+    act(r("sp", 32, 64), C4096, F.Identity, bias=col("fa", 1), scale=col("ac", 7))
+    ts(col("cf", 17), col("cf", 0), col("cf", 2), A.subtract, 16.0, A.mult)
+    tr(r("ex", 0, 64), r("sp", 0, 64))
+    exchange("ex", 64, 0)
+    FR, CR2, FL = r("ex", 0, 256), r("ex", 256, 512), r("ex", 512, 768)
+    for h in range(2):
+        act(junk(1 + h), FR, F.Sign, bias=col("fa", 2 + h), acc=col("ac", 4 + h))
+    ts(r("cq", 768, 1024), FR, col("cf", 17), A.is_ge)
+    ts(r("fa", 6, 8), r("ac", 6, 8), 1048576.0, A.mult)
+    below = total(3, "cq", 768)
+    tt(r("fa", 8, 10), r("fa", 6, 8), r("fa", 4, 6), A.add)
+    ts(r("sp", 64, 96), CM128, col("ac", 4), A.mult, col("fa", 8), A.add)
+    act(r("sp", 96, 128), CM128, F.Identity, bias=col("fa", 9), scale=col("ac", 5))
+    ts(col("cf", 18), col("cf", 2), 256.0, A.mult)
+    tr(r("ex", 256, 320), r("sp", 64, 128))
+    ts(r("lo", 0, 3), r("lo", 8, 11), col("cf", 18), A.add, 32768.0, A.add)
+    exchange("ex", 64, 256)
+    ts(col("cf", 19), below, -256.0, A.mult)
+    ts(r("lo", 3, 6), r("lo", 0, 3), col("cf", 19), A.add)
+    ts(r("lo", 11, 14), r("lo", 3, 6), 256.0, A.add)
+    ts(r("cf", 21, 24), r("lo", 3, 6), -255.0, A.mult, -32512.0, A.add)
+    ts(col("lo", 14), col("lo", 3), -1.0, A.mult)
+    ts(col("lo", 15), col("lo", 3), 33024.0, A.add)
+    act(junk(5), CR2, F.Relu, bias=col("lo", 14))
+    act(r("cq", 0, 256), junk(5), F.Relu, bias=256.0, scale=-1.0, acc=col("ac", 16))
+    for c in (1, 2):
+        ts(r("cq", 256 * c, 256 * c + 256), CR2, col("lo", 3 + c), A.max, col("lo", 11 + c), A.min)
+    act(col("lst", 0), col("ac", 16), F.Identity, bias=col("lo", 15), scale=-1.0)
+    for c in (1, 2):
+        ts(col("lst", c), total(c, "cq", 256 * c), col("cf", 21 + c), A.add)
+
+    def slot(d, w, base=0):
+        q = base + w * ((rank - d - 1) % 8)
+        return q, q + w
+
+    quant(r("qx", 0, 256), r("sx", 0, 256), r("xb", 0, 1024))
+    for i in range(4):
+        act(r("ub", i, 512, 4), r("iot", 0, 128), F.Identity, bias=col("u4", i), scale=0.0)
+    quant(r("qu", 0, 128), r("su", 0, 128), r("ub", 0, 512))
+    for h in range(2):
+        mm(r("ps", 512 * h, 512 * h + 128), r("qx", 128 * h, 128 * h + 128), r("sx", 128 * h, 128 * h + 128), r("qu", 0, 128), r("su", 0, 128))
+        copy("s", col("ep", h), col("ps", 512 * h))
+    send_all(r("ep", 0, 2), lambda d: r("er", *slot(d, 2)), "aer", [r("er", 0, 14)], FIRST)
+    asked = send_all(r("lst", 0, 3), lambda d: r("rl", *slot(d, 3)), "arl", [r("rl", 0, 21)])
+    mm(r("pe", 0, 256), r("qu", 0, 128), r("su", 0, 128), r("qx", 0, 256), r("sx", 0, 256))
+    copy("s", r("ea", 0, 256), r("pe", 0, 256))
+    dma([("y", r("g0", 0, 256), r("qx", 0, 256)), ("y", r("h0", 0, 256), r("sx", 0, 256))])
+    dma([("y", r("ow", 0, 256), r("qx", 0, 256)), ("y", r("os_", 0, 256), r("sx", 0, 256))])
+
+    copy("v", r("nbt", 0, 48), r("nb32", 0, 48))
+    for i in range(0, 48, 12):
+        copy("s", r("nbf", 16 * i, 16 * i + 192), (r("iot", 0, 2048), r("nbt", i, i + 12)))
+    ts(col("cf", 25), col("cf", 1), 3.0, A.mult)
+    ts(r("dbt", 0, 12), r("kk", 6, 18), col("cf", 25), A.add)
+    ts(r("ci", 7, 8), r("ci", 3, 4), 10.0, A.add)
+    ts(r("ci", 8, 9), r("ci", 7, 8), 15, A.bitwise_and)
+    copy("v", col("cf", 43), r("ci", 8, 9))
+    ts(col("cf", 45), col("cf", 1), col("cf", 2), A.subtract, col("cf", 43), A.add)
+    lin(col("cf", 46), col("cf", 45), 3.0, 0.0)
+    ts(r("frt", 12, 20), r("kk", 6, 14), col("cf", 46), A.add)
+    copy("v", r("dbz", 0, 128), (r("nbf", 0, 768), r("frt", 12, 20)))
+    tr(r("dtz", 0, 128), r("dbz", 0, 128))
+    ts(r("of", 0, 8), r("dtz", 0, 128, 16), -256.0 * rank, A.add)
+    ts(r("gi", 0, 16), r("kk", 218, 264, 3), 2048.0 - 256.0 * (rank + 1), A.add)
+    ts(r("gi", 16, 32), r("gi", 0, 16), 2, A.arith_shift_right, 480, A.bitwise_and)
+    ts(r("gi", 32, 48), r("gi", 0, 16), 31, A.bitwise_and)
+    ts(r("gi", 48, 64), r("gi", 0, 16), 96, A.bitwise_and)
+    lin(col("cf", 49), col("cf", 26), 0.5, 0.0)
+    tt(r("gi", 64, 80), r("gi", 16, 32), r("gi", 32, 48), A.add)
+    ts(r("gi", 80, 96), r("gi", 48, 64), col("cf", 49), A.not_equal, 1024.0, A.mult)
+    tt(r("gi", 96, 112), r("gi", 64, 80), r("gi", 80, 96), A.add)
+    ts(r("frt", 20, 36), r("gi", 96, 112), 448.0, A.min)
+
+    fill(CONE, 1.0)
+    for c in range(14):
+        o = r("es", 32 * c, 32 * c + 32)
+        times(o, CONE, col("er", c))
+    const(r("est", 448, 480), 0.0)
+    for h in range(0, 448, 224):
+        tr(r("est", h, h + 224), r("es", h, h + 224))
+    copy("s", r("d1r", 2, 448, 7), (r("est", 0, 480), r("frt", 20, 24)))
+    copy("v", r("fz", 64, 256), (r("est", 0, 480), r("frt", 24, 36)))
+    for d in (1, 3):
+        for a in range(4):
+            copy("vs"[a % 2], r("d1r", 2 + d, 448, 7, 32 * a, 32 * a + 32), blk("fz", 64 * (4 - d), 64 * (4 - d) + 64, (a + d) % 4))
+    copy("v", r("d1r", 4, 448, 7, 0, 64), r("fz", 128, 192, 1, 64, 128))
+    copy("s", r("d1r", 4, 448, 7, 64, 128), r("fz", 128, 192, 1, 0, 64))
+
+    for h in range(2):
+        quant(r("qb", 128 * h, 128 * h + 128), r("sb", 128 * h, 128 * h + 128), r("bb_t", 512 * h, 512 * h + 512))
+    for i in range(4):
+        act(r("vb", i, 512, 4), r("iot", 0, 128), F.Identity, bias=col("v4", i), scale=0.0)
+    quant(r("qv", 0, 128), r("sv", 0, 128), r("vb", 0, 512))
+    mm(r("pf", 0, 256), r("qv", 0, 128), r("sv", 0, 128), r("qb", 0, 256), r("sb", 0, 256))
+    copy("s", r("fn", 0, 256), r("pf", 0, 256))
+    ts(col("cf", 27), col("cf", 26), col("cf", 2), A.add)
+    ts(r("frt", 0, 4), r("iot", 0, 64, 16), col("cf", 27), A.add)
+    act(r("d1z", 3, 256, 4), (r("fn", 0, 256), r("frt", 0, 4)), F.Copy, scale=-1.0)
+    lin(col("cf", 47), col("cf", 43), 1.0, col("cf", 26))
+    ts(r("frt", 4, 8), r("iot", 0, 64, 16), col("cf", 47), A.add)
+    act(r("d1r", 6, 448, 7), (r("fn", 0, 256), r("frt", 4, 8)), F.Copy, scale=-1.0)
+    copy("s", r("d1r", 0, 448, 7), (r("ea", 0, 256), r("of", 0, 4)))
+    copy("v", r("d1r", 1, 448, 7), (r("ea", 0, 256), r("of", 4, 8)))
+    const(r("d0r", 0, 448), 1.0)
+    act(r("d0r", 0, 448, 7), r("iot", 0, 64), F.Copy, scale=0.0)
+    const(r("d0z", 0, 256), 1.0)
+    act(r("d0z", 0, 256, 4), r("iot", 0, 64), F.Copy, scale=0.0)
+    for i in range(4):
+        const(r("mm_", 160 * i + 128, 160 * i + 160), 0.0)
+    const(col("cf", 35), 1024.0)
+    const(r("cf", 32, 35), 0.0)
+    const(r("cf", 32, 33, 1, 96, 128), -TINY)
+    const(r("cf", 33, 34, 1, 64, 128), -TINY)
+    const(r("cf", 34, 35, 1, 64, 128), -TINY)
+    const(r("cf", 34, 35, 1, 32, 64), -TINY)
+    lin(col("cf", 4), col("cf", 1), 1.0, 1.0)
+    lin(col("cf", 6), col("cf", 2), 1.0, 1.0)
+    lin(col("cf", 7), col("cf", 2), -1.0, -16.0)
+    lin(col("cf", 12), col("cf", 1), -float(KC), -float(KC))
+    lin(r("cf", 15, 17), r("jo", 0, 2), 3.0 / 1024, 0.0)
+    ts(r("jj", 0, 64), r("jr", 0, 64), col("jo", 0), A.is_lt, -TINY, A.mult)
+    ts(r("jj", 64, 128), r("jr", 0, 64), col("jo", 1), A.is_lt, TINY, A.mult)
+    lin(col("cf", 28), col("cf", 26), -3.0, col("cf", 12))
+    SOC = r("kk", 0, 6)
+    lin(SOC, SOC, 1.0, col("cf", 28))
+    lin(col("cf", 29), col("cf", 2), -float(KC), 768.0 * rank - KC)
+    lin(col("cf", 30), col("cf", 2), 1024.0, 768.0 * rank + 17 * 1024)
+    lin(r("kk", 18, 22), r("iot", 0, 4), 0.25, 0.0)
+    copy("s", r("ol", 0, 256), r("iot", 0, 256))
+
+    ts(r("fi", 4, 6), r("fi", 0, 2), 8, A.arith_shift_right)
+    copy("v", r("fa", 10, 12), r("fi", 4, 6))
+    ts(r("fa", 12, 14), r("fa", 10, 12), -256.0, A.mult, 0.5, A.add)
+    for h in range(2):
+        act(junk(3 + h), FR, F.Sign, bias=col("fa", 12 + h), acc=col("ac", 8 + h))
+    ts(r("fi", 6, 8), r("fi", 4, 6), float(7 - rank), A.add)
+    ts(r("fi", 8, 10), r("fi", 6, 8), 7, A.bitwise_and)
+    ts(r("fa", 14, 16), r("fi", 8, 10), float(LC), A.mult, float(FAR0), A.add)
+    for k in range(2):
+        lin(r("nl", k, 768, 3), r("nbf", k, 768, 3), 1.0, -256.0 * rank)
+    tt(r("ac", 10, 12), r("ac", 8, 10), r("ac", 4, 6), A.subtract)
+    ts(r("ac", 12, 14), r("ac", 10, 12), 0.5, A.mult)
+    tt(r("ac", 14, 16), r("ac", 12, 14), r("fa", 14, 16), A.add)
+    for h in range(2):
+        times(r("sp", 128 + 32 * h, 160 + 32 * h), CONE, col("ac", 14 + h))
+    tr(r("ex", 512, 576), r("sp", 128, 192))
+    exchange("ex", 64, 512)
+    ts(r("ci", 5, 6), r("ci", 2, 3), 3.0, A.mult, 2.0, A.add)
+    ts(r("ci", 6, 7), r("ci", 5, 6), 15, A.bitwise_and)
+    copy("v", col("cf", 41), r("ci", 6, 7))
+    lin(col("cf", 48), col("cf", 41), 7.0, 6.0)
+    ts(r("frt", 8, 12), r("iot", 0, 448, 112), col("cf", 48), A.add)
+    ts(r("pm", 0, 16), r("iot", 0, 256, 16), col("cf", 41), A.add)
+    copy("s", r("nl", 2, 768, 3), (FL, r("pm", 0, 16)))
+
+    dma([("y", r("rl", 21, 32), r("iot", 0, 11))])
+    tr(r("rl2", 0, 32), r("rl", 0, 32))
+    o = 16 * (rank % 2)
+    for i in (32, 48):
+        ts(r("rl2", i, i + 16), r("rl2", o, o + 16), 255.0, A.min)
+    tr(r("rl2", 64, 96), r("rl2", 32, 64))
+    for a in range(4):
+        copy("v", blk("rep", 0, 21, a), blk("rl2", 64, 85, rank // 2))
+    pick(r("slc", 0, 336), r("sls", 0, 336), r("qx", 0, 256), r("sx", 0, 256), r("rep", 0, 21))
+    for s, l, arr in (("slc", "g0", "ac0"), ("sls", "h0", "as0")):
+        send_each([(d, r(s, LC * i, LC * i + LC), r(l, *slot(d, LC, FAR0))) for i, d in enumerate(peers)], arr, [r(l, FAR0, NEW0)])
+    w0 = 32 * ((rank + 1) % 8)
+    w1 = w0 or 128
+    iota(r("ndv", w1, 256), [[1, 256 - w1]], NEW0 + w1 - w0, 0)
+    iota(r("ndv", 0, w1), [[1, w1]], NEW0 + (256 - w0) % 256, 0)
+    for i in range(4):
+        iota(r("np0", 512 * i, 512 * i + 512), [[0, 512]], 0, 0, after=[asked])
+    iota(r("od", 0, 96), [[1, 96]], P, 0)
+
+    for i in range(0, 768, 256):
+        copy("s", r("nl", 768 + i, 1024 + i), r("nl", i, i + 256))
+    copy("v", r("db", 0, 192), (r("nl", 0, 768), r("dbt", 0, 12)))
+    fill(r("xt", 0, 512), 0.0)
+    for b in range(4):
+        quant(r("qa", 128 * b, 128 * b + 128), r("sa", 128 * b, 128 * b + 128), r("at", 512 * b, 512 * b + 512))
+    dma([("y", r(n % t, 96, 128), r(s, 0, 32)) for t in range(3) for n, s in (("nq%d", "qx"), ("ns%d", "sx"))])
+    quant(r("qw", 0, 128), r("sw", 0, 128), r("wt", 0, 512))
+    mm(r("py", 0, 256), r("qw", 0, 128), r("sw", 0, 128), r("qx", 0, 256), r("sx", 0, 256))
+    copy("s", r("yw", 0, 256), r("py", 0, 256))
+    for k in range(3):
+        tr(r("dt_", 64 * k, 64 * k + 64), r("nbf", k, 192, 3))
+    copy("v", r("dnb", 0, 12), r("dt_", 0, 192, 16))
+
+    def places(t):
+        copy("v", r("ndl", 0, 2), r("nd_", 0, 2))
+        scatter(r("ol", 0, 256), r("ndl", 0, 2), r("od", 32 * t, 32 * t + 32))
+
+    def q32(i, b):
+        return r("sc4", 128 * i + 32 * b, 128 * i + 32 * b + 32)
+
+    for t in range(R):
+        gq, gs, W, oz = "g%d" % t, "h%d" % t, NEW0 + 256 * t, 12 * t
+        e0, e1 = (W - 256, W) if t else (FAR0, NEW0)
+        em = (e0 + e1) // 2
+        mm(r("pe", 0, em - e0), r("qu", 0, 128), r("su", 0, 128), r(gq, e0, em), r(gs, e0, em))
+        mm(r("pf", 0, e1 - em), r("qu", 0, 128), r("su", 0, 128), r(gq, em, e1), r(gs, em, e1))
+        copy("v" if t else "s", r("ea", e0, em), r("pe", 0, em - e0))
+        copy("s", r("ea", em, e1), r("pf", 0, e1 - em))
+        if t:
+            for k in range(3):
+                copy("svv"[k], r("d1z", k, 256, 4), (r("ea", 0, W), r("of", oz + 4 * k, oz + 4 * k + 4)))
+            scan(r("zs", 0, 256), r("d0z", 0, 256), r("d1z", 0, 256), 0.0, A.mult, A.add)
+            act(r("z", 0, 64), r("zs", 3, 256, 4), F.Abs)
+        else:
+            scan(r("zr", 0, 448), r("d0r", 0, 448), r("d1r", 0, 448), 0.0, A.mult, A.add)
+            act(r("z", 0, 64), (r("zr", 0, 448), r("frt", 8, 12)), F.Abs)
+        exchange("z")
+        tr(r("zt", 0, 64), r("z", 0, 64))
+        ts(r("dd", 0, 64), r("z", 0, 64), col("zt", 0), A.subtract)
+        act(r("dd", 64, 128), r("z", 0, 64), F.Identity, bias=col("zt", 32), scale=-1.0)
+        for h in range(2):
+            o = 320 * h
+            tt(r("mm_", o, o + 64), r("dd", 64 * h, 64 * h + 64), r("jj", 64 * h, 64 * h + 64), A.is_lt if h else A.is_gt)
+            for d in range(1, 4):
+                o2 = o + (0, 64, 160, 224)[d]
+                ts(r("mm_", o2, o2 + 64), r("z", 64 * d, 64 * d + 64), col("zt", 32 * h), A.subtract, col("cf", 31 + d), A.is_gt)
+            scan(r("cx", 160 * h, 160 * h + 160), r("mm_", o, o + 160), r("mm_", o + 160, o + 320), col("cf", 15 + h), A.add, A.add)
+            tr(r("cr", 32 * h, 32 * h + 32), r("cx", 160 * h + 128, 160 * h + 160))
+        ts(r("cl", 0, 64), r("cr", 0, 64), col("cf", 1), A.max, col("cf", 4), A.min)
+        ts(r("cl", 64, 128), r("cr", 0, 64), col("cf", 2), A.max, col("cf", 6), A.min)
+        act(r("junk", 1792, 1856), r("cl", 0, 64), F.Copy, scale=1024.0, acc=col("sa_", 0))
+        act(r("cl", 128, 192), r("cr", 0, 64), F.Relu, bias=col("cf", 7))
+        act(r("junk", 1856, 1920), r("cl", 64, 128), F.Copy, scale=1024.0, acc=col("sb_", 0))
+        act(r("cl", 192, 256), r("cl", 128, 192), F.Relu, bias=col("cf", 35), scale=-1024.0, acc=col("sb_", 1))
+        for a in range(4):
+            copy("vs"[a % 2], blk("sa_", 1, 2, a), blk("sa_", 0, 1, (a + 1) % 4))
+        PRE = r("sel", 16, 22)
+        ts(PRE, SOC, col("sa_", 0), A.add, col("sa_", 1), A.add)
+        act(r("sa_", 2, 3, 1, 0, 64), r("sa_", 0, 1, 1, 64, 128), F.Identity, bias=r("sa_", 1, 2, 1, 64, 128))
+        ts(r("sa_", 2, 3, 1, 64, 128), r("sa_", 0, 1, 1, 0, 64), r("sa_", 1, 2, 1, 0, 64), A.add)
+        ts(r("so", 0, 6), PRE, col("sa_", 2), A.add)
+        copy("v", r("ng", 0, 96), (r("nl", 0, 1536), r("so", 0, 6)))
+        tr(r("nt", 0, 96), r("ng", 0, 96))
+        copy("v", r("po", 0, 6), r("nt", 0, 96, 16))
+        exchange("sb_", 2)
+        act(r("sel", 4, 8), r("sb_", 0, 8, 2), F.Copy, acc=col("sel", 1))
+        act(r("sel", 8, 12), r("sb_", 1, 8, 2), F.Copy, acc=col("sel", 2))
+        act(col("sel", 12), col("sel", 1), F.Identity, bias=col("cf", 29))
+        act(col("sel", 13), col("sel", 2), F.Identity, bias=col("cf", 30), scale=-1.0)
+        nd, na = r("nd_", 4 + 2 * (t % 2), 6 + 2 * (t % 2)), "nda%d" % t
+        act(nd, r("sel", 12, 14), F.Copy, scale=THIRD)
+        if t < 2:
+            send_all(nd, lambda d: r(na, 2 * rank, 2 * rank + 2), "an%d" % t, [r(na, 2 * s, 2 * s + 2) for s in peers])
+            dma([("y", r(na, 2 * rank, 2 * rank + 2), nd)])
+        act(r("nd_", 0, 2), nd, F.Copy, bias=-256.0 * rank)
+        nq, ns = "nq%d" % t, "ns%d" % t
+        pick(r(nq, 0, 96), r(ns, 0, 96), r(gq, 0, W), r(gs, 0, W), r("po", 0, 6))
+        for b in range(4):
+            mm(r("ps", 512 * b, 512 * b + 128), r("qa", 128 * b, 128 * b + 128), r("sa", 128 * b, 128 * b + 128), r(nq, 0, 128), r(ns, 0, 128))
+        for c in range(2):
+            ts(r("bo", c, 8, 2), r("kk", 18, 22), col("nd_", c), A.add, 4.0, A.mult)
+        copy("s", r("bbs", 0, 128), (r("bb_t", 0, 1024), r("bo", 0, 8)))
+        for b in range(4):
+            copy("s", q32(0, b), r("ps", 512 * b, 512 * b + 32))
+        for k, b in ((1, 0), (1, 1), (2, 0), (1, 2), (2, 1), (1, 3), (2, 2), (2, 3)):
+            tt(q32(k, b), q32(k - 1, b), r("ps", 512 * b + 32 * k, 512 * b + 32 * k + 32), A.add)
+        if t == 2:
+            places(t)
+        for b in range(4):
+            act(q32(3, b), q32(2, b), F.Copy, scale=C05)
+            tt(r("xt", b, 128, 4), q32(3, b), r("bbs", 32 * b, 32 * b + 32), A.add)
+        if t == 2:
+            copy("s", r("og", 0, 256), (r("ol", 0, 256), r("d8", 0, 16)))
+        o0 = P + 32 * t
+        if t < 2:
+            nq, ns, at = "g%d" % (t + 1), "h%d" % (t + 1), W + 224
+            quant(r(nq, at, at + 128), r(ns, at, at + 128), r("xt", 0, 512))
+            for n, arr in ((nq, "ac%d" % (t + 1)), (ns, "as%d" % (t + 1))):
+                send_all(r(n, at, at + 32), lambda d: r(n, *slot(d, 32, W)), arr, [r(n, W, at)], 1.2)
+            dma([("y", r("ow", o0, o0 + 32), r(nq, at, at + 32)), ("y", r("os_", o0, o0 + 32), r(ns, at, at + 32))])
+        else:
+            nq, ns, at = "ow", "os_", o0
+            quant(r(nq, at, at + 128), r(ns, at, at + 128), r("xt", 0, 512))
+        mm(r("py", 0, 128), r("qw", 0, 128), r("sw", 0, 128), r(nq, at, at + 128), r(ns, at, at + 128))
+        copy("s", r("yw", o0, o0 + 32), r("py", 0, 32))
+        if t == 0:
+            dma([("y", r("g1", 0, NEW0), r("g0", 0, NEW0)), ("y", r("h1", 0, NEW0), r("h0", 0, NEW0))])
+            dma([("y", r("g2", 0, NEW0), r("g0", 0, NEW0)), ("y", r("h2", 0, NEW0), r("h0", 0, NEW0))])
+            lin(r("ndv", 256, 512), r("ndv", 0, 256), 1.0, 256.0)
+        ts(col("sel", 0), col("sa_", 0), col("sa_", 1), A.add, col("sa_", 2), A.add)
+        ts(col("nd_", 8 + t), col("sel", 0), col("cf", 12), A.add, THIRD, A.mult)
+        dma([("y", T.nd[t:t + 1, 0:32], r("nd_", 8 + t, 9 + t, 1, 0, 32))])
+        if t < 2:
+            places(t)
+        if t == 1:
+            dma([("y", r("g2", NEW0, NEW0 + 256), r("g1", NEW0, NEW0 + 256)), ("y", r("h2", NEW0, NEW0 + 256), r("h1", NEW0, NEW0 + 256))])
+            ts(r("frf", 0, 16), r("iot", 0, 256, 16), 0.0, A.add)
+            ts(r("frf", 0, 16), r("frf", 0, 16), 224, A.bitwise_and)
+            ts(r("d8", 0, 16), r("frf", 0, 16), col("cf", 1), A.add)
+        if t < 2:
+            npn = r("np0", 0, 2048)
+            copy("v", r("nai", 0, 16), r(na, 0, 16))
+            scatter(npn, r("nai", 0, 16), r("ndv", 256 * t, 256 * t + 256))
+            tt(r("db", 0, 192), (npn, r("dnb", 0, 12)), r("db", 0, 192), A.max)
+            tr(r("dt_", 0, 192), r("db", 0, 192))
+            copy("v", r("of", 12 * t + 12, 12 * t + 24), r("dt_", 0, 192, 16))
+            for i in range(0, 48, 8):
+                tt(r("nl", 16 * i, 16 * i + 128), (npn, r("nbt", i, i + 8)), r("nl", 16 * i, 16 * i + 128), A.max)
+            for i in range(0, 768, 256):
+                copy("s", r("nl", 768 + i, 1024 + i), r("nl", i, i + 256))
+
+    tr(r("ogt", 0, 256), r("og", 0, 256))
+    copy("v", r("oo", 0, 16), r("ogt", 0, 256, 16))
+    pick(r("occ", 0, 256), r("ocs", 0, 256), r("ow", 0, 352), r("os_", 0, 352), r("oo", 0, 16))
+    dma([("y", T.oc[:], r("occ", 0, 256))])
+    dma([("y", T.osc[4 * k:4 * k + 4, :], r("ocs", 0, 256, 1, 32 * k, 32 * k + 4)) for k in range(4)])
+    copy("v", r("yt", 0, 128), (r("yw", 0, 352), r("oo", 0, 8)))
+    copy("s", r("yt", 128, 256), (r("yw", 0, 352), r("oo", 8, 16)))
+    dma([("s", T.y[:], r("yt", 0, 256))])
+    flush()
+    for sem, c in cnt.items():
+        if known["g"].get(sem, 0) < c:
+            g.wait_ge(T.sem[sem], c)

@@ -8,30 +8,26 @@ P, K, R, LC = 256, 32, 3, 48
 FAR0 = P
 NEW0 = P + 7 * LC
 C05 = 13421773 * 2.0 ** -28
-THIRD = float(np.float32(1.0) / np.float32(3.0))
-KC = 1024 * 255
 TINY = 2.0 ** -110
 CYC, HOLD, FLY, FIRST, LOAD = 0.001, 0.25, 2.4, 2.0, 2.2
 ORDER = """
-21 282 14 15 4 11 12 7 1 6 10 5 13 0 3 9 2 8 16 20 36 28 22 37 27 30 29 272 31 35 84 200 32 39 23 34 209 33 41 211 38 108 44 292 17 110
-46 124 40 127 45 50 18 291 47 42 288 135 256 109 125 48 19 43 111 128 289 112 287 49 290 210 126 188 129 113 52 51 136 114 53 55 56 116
-54 57 122 58 144 115 117 60 217 185 118 186 64 59 187 63 25 119 61 67 153 148 131 66 137 68 271 69 138 62 70 73 71v 72s 205 183 139 24
-74 75 195 65 79 218 184 77 189 81 76 78 190 83 86 132 147 82 80 130 145 85 93 146 87s 88v 90 89 206 94 92v 91s 95 401 98 97 101 99 102
-216 96 100 104 106 140 105 103 107 123 227 141 120 212 150 191 149 121 142 235 228 276 219 143 229 236 196 249 226v 202 151 284 230 199
-232 152 197 250 198 273 165 158s 251 166s 160s 233 167s 162 164s 163 161s 154 159 156s 155 168 234 157s 224 170 231 169 213 204 252 283
-201 220 172s 277 171 257 237 174 253 178 258 181s 26 259 175s 238 179s 254 177s 182 260 173s 180v 223 176v 203 261 214 264 263 262 304
-266 265 305 208 269 306s 239 221 312 308s 270 309 267 307 240 241s 314 310 268 274 311 242 313 316 322 245s 318 243s 315 244 225 323 246
-324 248 317 321 247s 319 207 255 325 320 275 298 133 222 326 280 134 327 279v 329 333 334 215 192 335s 336v 330 339 328 338 337 278 285
-340 193 332 331 341 347 344 345 346s 342 296 349 348s 343 360 359 399 351 350 281 353 361 352 293 363 354 528 286 368 362 357 355 358
-370 372 364 297 366 356 369 374 301 299 365 371 402 380 375 294 373 367 377 378 376 379 300 405 384 381 382 386 295 385 383 387 302 388
-303 406 194 389 394 398 400 391 390 392 407 403 408 529 417 409 410 414 527 413 421 526 393 411 404 422 397 423 395 416 424 425v 427s
-426s 412 428 530 415 429 436 432s 431 433v 430s 437 438 434s 440 435 445 420 439 441 442 418 446 448 447 443 419 449 444 450 451 454 452
-453 456 458v 457s 459s 460v 463 461 462 455 464 468s 470 469v 471v 465s 473v 472s 466 521 474 475 467 522 476 483 484 477 485 478 488
-479 482 481 396 523 492 486 489 480 495 487 496 493 501 490 494 503 497 498 499 510 491 500 502 504 506 511 508 505 507 509 512 513 517
-518 515 514 516 531 532 533 537 540 534 535 536 545 539 546 547 519 541 548 550 551s 549 538 542 552 544v 553 560 557 554s 555v 556s 562
-561 559 570 558s 563 543 569 571 572 566 565 564 573 567 574 568 575 578 576 577 580 582v 581s 583s 584v 579 587 585 586 592 594s 593v
-595 588 597 596 589 599 598 590 601 639 600 591 524 602 604 605 525 603 520 608 625 609 626 615 606 616 620 607 635 610 611 622 623 640
-624 613 612v 614 633 617 631 618 634 619 621 642 627 629 632 628 630 643 636 637 644 645 638 648 651 652 647 649 641 646 650 653
+6 13 20 2 49 149 4 21 22 5 27 26 29 28 30 34 131 31 39 38 12 1 67 8 3 9 15 132 0 16 40 150 24 83s 234 33 10 129s 144 43 41 11 35s 32
+154 23 37 50 25 42 151 7 45 127 36 44 108 172 19 17 109 14 46 107 111 47 140 48 110 186 112 115 51 173 133 266 52 113 134 241 54 55 53
+141 257 121 57 114 116 59 60 56 63 62 171 142 61 65 128 66 78 64 68 85 80 174 70v 122 72v 69s 71s 181 170 74v 175 58s 73s 188 77 169 79
+76 75 176 143 227 82 117 81 92 214 135 84 145 89v 187 93s 88s 87v 86s 94s 91 97s 256 118 96 90 235 95 100 98 101 177 103 99 105 136
+104s 106 218 102 182 189 137s 146 219 152 153 202 138 220s 147 119 183 205 155 148 120 221 196 190 156 139 222 157 124 184 223 158 185s
+224 204 168 166 228 159s 164 236 163s 18 160v 165s 161s 237 167 125 203 200 194 193 162v 225 239 207 242 226 285 215 306 229s 244 243
+192 206 238 191 245 230 286 249 231s 123 232s 247 288 246 248 293 213 289s 130 251 295 290 210 233 287s 291s 250 294 292 208 240 254
+209 267s 301 270 268 302 216 297 197 198 252 258 296 304 303 260 195 253 259 298 299 263 178s 305 300 308 211 201 307 275 309 212 312
+310 255 311 313 272 314s 322 316v 323 320 321s 319 324v 315 318v 317s 273 325 264 274 326 328 333 331 271 332 327 336 338 334 335 372
+199 339 280 281 371 262 343 329 337 265 341 340 330 342 369 344 347 217 345 261 346 348 411 279 349 283 377 179 353 350 284 351 354 352
+355 282 378 180 362 479 379 269 356 380 357 363 375 384 381 276 387v 388 358 383 386 385 389 390 480 376 391 398 394s 395v 392 399 393
+402 407 400 396s 397 360 406 374 401 404 403 277 409 408 405 410 382 412 413 368 414 361 417 418 416 278 359 415 428 424s 423v 425 426
+365 421v 419s 429v 422s 478 427v 420s 430 431 432 437 433 438 439 436 442 443 444 481 445 446 449 440 441 516 447 448 453 450 451 434
+452 435 454 455 458 456 459 473 460 457 482 366 461 483 484 370 467 462 468 485 486 492 469 493 489 488 491 490 494 495 496 503 499s
+477 497s 500v 463 498 505 475 504 501s 373 512 502 507 487 506 511 508 464 509 513 514 364 510 515 517 518 519 367 521 523 522 520 525
+528 531s 465 524 533v 466 534 126 530 532v 526 529 527s 476 535 536 470 537 538 471 547 545 539 544 542 548 540 541 543 551 546 549 550
+552 553 555 554 556 557 472 563 558 564 565 561 562 559 474 566 570 568 567 571 569 560 573 572 574
 """
 CODE, U8, BF, F32, I32, U16 = "float8_e4m3fn_x4", "uint8", "bfloat16", "float32", "int32", "uint16"
 
@@ -40,24 +36,27 @@ def _sbuf(dtype, **cols):
     return {n: ("sbuf", [128, c], dtype) for n, c in cols.items()}
 
 
-SCRATCH = {"pe": ("psum", [128, 512], F32), "pf": ("psum", [128, 512], F32), "ps": ("psum", [128, 2048], F32), "py": ("psum", [128, 512], F32)}
-SCRATCH.update(_sbuf(F32, nbf=768, iot=2048, jr=256, jf=256, cf=64, jo=6, ka=256, kat=64, junk=2560, cq=1024, cz=512, ac=32, fa=28,
-                     sp=192, ex=768, cc=128, lo=16, ea=1104, fn=256, z=256, zt=64, dd=128, jj=128, zs=256, d0z=256, d1z=256, cx=320, cr=64,
-                     cl=256, sa_=4, sb_=8, sel=24, kk=264, ng=96, nt=96, nd_=12, bbs=128, sc4=512, nda0=16, nda1=16,
-                     np0=2048, ndv=512, nl=1536, db=192, dbz=192, dt_=192, dtz=192, ol=256, od=96, og=256, ogt=256, yt=256,
-                     ep=2, er=14, es=448, est=480, fz=256, d0r=448, d1r=448, zr=448, rl=32, rl2=96, lst=4, yw=352))
+SCRATCH = {"pe": ("psum", [128, 512], F32), "pf": ("psum", [128, 512], F32), "ps": ("psum", [128, 2048], F32), "py": ("psum", [128, 512], F32),
+           "px": ("psum", [128, 512], F32)}
+SCRATCH.update(_sbuf(F32, nbf=192, iot=2048, jr=256, jf=256, cf=64, jo=6, ka=256, kat=64, junk=2560, cq=1024, cz=512, ac=32, fa=28,
+                     sp=192, ex=576, cc=128, lo=16, ea=1104, fn=256, z=256, zt=64, dd=128, jj=128, zs=256, d1z=64, cx=256, c4=288,
+                     wn=1088, wt_=576, dv=128, sel=48, kk=264, nd_=48, bbs=128, sc4=512, nda0=16, nda1=16,
+                     np0=2048, ndv=512, nl=192, db=192, dbz=192, dt_=192, dtz=192, ol=256, od=96, og=256, ogt=256, yt=256,
+                     ep=12, er=32, es=448, est=480, fz=256, d0r=448, d1r=448, zr=448, rl=32, rl2=96, lst=4, yw=352))
 SCRATCH.update(_sbuf(I32, nb32=48, ci=16, fi=16, frf=256, gi=128))
-SCRATCH.update(_sbuf(U16, nbt=48, far16=16, pm=16, rep=24, so=6, po=6, ndl=2, nai=16, bo=8, dbt=12, dnb=12, of=36, frt=36, d8=16, oo=16))
-SCRATCH.update(_sbuf(BF, xb=1024, bb_t=1024, at=2048, wt=512, u4=4, v4=4, ub=512, vb=512, mm_=640, xt=512))
+SCRATCH.update(_sbuf(U16, nbt=12, far16=16, pm=4, rep=24, so=8, po=16, dvo=36, ndl=2, nai=16, bo=8, dbt=12, dnb=12, of=36, frt=36, d8=16, oo=16))
+SCRATCH.update(_sbuf(BF, xb=1024, bb_t=1024, at=2048, wt=512, u4=4, v4=4, ub=512, vb=512, mm_=512, xt=512))
 for _c, _s, _n in (("qx", "sx", 256), ("qb", "sb", 256), ("qu", "su", 128), ("qv", "sv", 128), ("qa", "sa", 512), ("qw", "sw", 128), ("slc", "sls", 336),
                    ("g0", "h0", 592), ("g1", "h1", 944), ("g2", "h2", 1200), ("nq0", "ns0", 128), ("nq1", "ns1", 128), ("nq2", "ns2", 128),
                    ("ow", "os_", 448), ("occ", "ocs", 256)):
     SCRATCH.update({_c: ("sbuf", [128, _n], CODE), _s: ("sbuf", [128, _n], U8)})
-SEMAPHORES = ["cv", "cs", "ct", "cg"] + ["q%d" % i for i in range(60)] + ["aer", "arl", "ac0", "as0", "an0", "an1", "ac1", "as1", "ac2", "as2"]
+SEMAPHORES = ["cv", "cs", "ct", "cg"] + ["q%d" % i for i in range(70)] + ["aer", "arl", "ac0", "as0", "an0", "an1", "ae0", "ae1", "ac1", "as1", "ac2", "as2"]
+PARTS = {"wm": ("c4", 128), "fr_": ("c4", 224), "wx": ("wt_", 384), "sm": ("wt_", 480), "fo": ("dvo", 6), "spo": ("dvo", 8)}
 
 
 def r(name, c0, c1, step=1, p0=0, p1=128):
-    return (name, c0, c1, step, p0, p1)
+    name, o = PARTS.get(name, (name, 0))
+    return (name, c0 + o, c1 + o, step, p0, p1)
 
 
 def rank_program(g, core, T, topo):
@@ -203,7 +202,13 @@ def rank_program(g, core, T, topo):
         i, rd = src(in_)
         a, ra = sc(s1)
         b, rb = sc(s2)
-        if op1 is None:
+        if all(SCRATCH[x[0]][2] == F32 for x in rd + [out]) and (op0, op1) in ((A.add, None), (A.mult, None), (A.mult, A.add)):
+            mul, add = (1.0, a) if op0 == A.add else (a, 0.0 if op1 is None else b)
+            fn = F.Copy if isinstance(add, float) else F.Identity
+            fns = {"v": lambda: g.vector.tensor_scalar(ap(out), i, a, b, op0, *([] if op1 is None else [op1])),
+                   "s": lambda: g.scalar.activation(ap(out), i, fn, bias=add, scale=mul)}
+            emit("v", lambda e: fns[e](), rd + ra + rb, [out], width(out), alt=True)
+        elif op1 is None:
             emit("v", lambda: g.vector.tensor_scalar(ap(out), i, a, None, op0), rd + ra, [out], width(out))
         else:
             emit("v", lambda: g.vector.tensor_scalar(ap(out), i, a, b, op0, op1), rd + ra + rb, [out], width(out))
@@ -325,7 +330,6 @@ def rank_program(g, core, T, topo):
     iota(r("iot", 1536, 2048), [[1, 512]], 1536, 0)
     iota(r("lo", 8, 11), [[4096, 3]], 0, 0)
     iota(r("kk", 6, 18), [[1, 3], [96, 2], [0, 2]], 0, 0)
-    iota(r("kk", 0, 6), [[1, 3], [0, 2]], 768, 0)
     ts(r("ci", 1, 2), r("ci", 0, 1), 31, A.bitwise_and)
     ts(r("ci", 2, 3), r("ci", 0, 1), 15, A.bitwise_and)
     copy("v", r("cf", 0, 3), r("ci", 0, 3))
@@ -371,7 +375,7 @@ def rank_program(g, core, T, topo):
     ts(col("cf", 17), col("cf", 0), col("cf", 2), A.subtract, 16.0, A.mult)
     tr(r("ex", 0, 64), r("sp", 0, 64))
     exchange("ex", 64, 0)
-    FR, CR2, FL = r("ex", 0, 256), r("ex", 256, 512), r("ex", 512, 768)
+    FR, CR2, FL = r("ex", 0, 256), r("ex", 256, 512), r("ex", 512, 576)
     for h in range(2):
         act(junk(1 + h), FR, F.Sign, bias=col("fa", 2 + h), acc=col("ac", 4 + h))
     ts(r("cq", 768, 1024), FR, col("cf", 17), A.is_ge)
@@ -410,15 +414,14 @@ def rank_program(g, core, T, topo):
         mm(r("ps", 512 * h, 512 * h + 128), r("qx", 128 * h, 128 * h + 128), r("sx", 128 * h, 128 * h + 128), r("qu", 0, 128), r("su", 0, 128))
         copy("s", col("ep", h), col("ps", 512 * h))
     send_all(r("ep", 0, 2), lambda d: r("er", *slot(d, 2)), "aer", [r("er", 0, 14)], FIRST)
-    asked = send_all(r("lst", 0, 3), lambda d: r("rl", *slot(d, 3)), "arl", [r("rl", 0, 21)])
+    send_all(r("lst", 0, 3), lambda d: r("rl", *slot(d, 3)), "arl", [r("rl", 0, 21)])
     mm(r("pe", 0, 256), r("qu", 0, 128), r("su", 0, 128), r("qx", 0, 256), r("sx", 0, 256))
     copy("s", r("ea", 0, 256), r("pe", 0, 256))
     dma([("y", r("g0", 0, 256), r("qx", 0, 256)), ("y", r("h0", 0, 256), r("sx", 0, 256))])
     dma([("y", r("ow", 0, 256), r("qx", 0, 256)), ("y", r("os_", 0, 256), r("sx", 0, 256))])
 
-    copy("v", r("nbt", 0, 48), r("nb32", 0, 48))
-    for i in range(0, 48, 12):
-        copy("s", r("nbf", 16 * i, 16 * i + 192), (r("iot", 0, 2048), r("nbt", i, i + 12)))
+    copy("v", r("nbt", 0, 12), r("nb32", 0, 12))
+    copy("s", r("nbf", 0, 192), (r("iot", 0, 2048), r("nbt", 0, 12)))
     ts(col("cf", 25), col("cf", 1), 3.0, A.mult)
     ts(r("dbt", 0, 12), r("kk", 6, 18), col("cf", 25), A.add)
     ts(r("ci", 7, 8), r("ci", 3, 4), 10.0, A.add)
@@ -427,7 +430,7 @@ def rank_program(g, core, T, topo):
     ts(col("cf", 45), col("cf", 1), col("cf", 2), A.subtract, col("cf", 43), A.add)
     lin(col("cf", 46), col("cf", 45), 3.0, 0.0)
     ts(r("frt", 12, 20), r("kk", 6, 14), col("cf", 46), A.add)
-    copy("v", r("dbz", 0, 128), (r("nbf", 0, 768), r("frt", 12, 20)))
+    copy("v", r("dbz", 0, 128), (r("nbf", 0, 192), r("frt", 12, 20)))
     tr(r("dtz", 0, 128), r("dbz", 0, 128))
     ts(r("of", 0, 8), r("dtz", 0, 128, 16), -256.0 * rank, A.add)
     ts(r("gi", 0, 16), r("kk", 218, 264, 3), 2048.0 - 256.0 * (rank + 1), A.add)
@@ -441,9 +444,10 @@ def rank_program(g, core, T, topo):
     ts(r("frt", 20, 36), r("gi", 96, 112), 448.0, A.min)
 
     fill(CONE, 1.0)
-    for c in range(14):
-        o = r("es", 32 * c, 32 * c + 32)
-        times(o, CONE, col("er", c))
+    for j in range(2):
+        copy("v", r("spo", j, 28, 2), r("iot", 0, 14))
+    copy("v", r("es", 0, 224), (r("er", 0, 14), r("spo", 0, 14)))
+    copy("s", r("es", 224, 448), (r("er", 0, 14), r("spo", 14, 28)))
     const(r("est", 448, 480), 0.0)
     for h in range(0, 448, 224):
         tr(r("est", h, h + 224), r("es", h, h + 224))
@@ -464,7 +468,7 @@ def rank_program(g, core, T, topo):
     copy("s", r("fn", 0, 256), r("pf", 0, 256))
     ts(col("cf", 27), col("cf", 26), col("cf", 2), A.add)
     ts(r("frt", 0, 4), r("iot", 0, 64, 16), col("cf", 27), A.add)
-    act(r("d1z", 3, 256, 4), (r("fn", 0, 256), r("frt", 0, 4)), F.Copy, scale=-1.0)
+    act(r("d1z", 0, 64), (r("fn", 0, 256), r("frt", 0, 4)), F.Copy, scale=-1.0)
     lin(col("cf", 47), col("cf", 43), 1.0, col("cf", 26))
     ts(r("frt", 4, 8), r("iot", 0, 64, 16), col("cf", 47), A.add)
     act(r("d1r", 6, 448, 7), (r("fn", 0, 256), r("frt", 4, 8)), F.Copy, scale=-1.0)
@@ -472,29 +476,31 @@ def rank_program(g, core, T, topo):
     copy("v", r("d1r", 1, 448, 7), (r("ea", 0, 256), r("of", 4, 8)))
     const(r("d0r", 0, 448), 1.0)
     act(r("d0r", 0, 448, 7), r("iot", 0, 64), F.Copy, scale=0.0)
-    const(r("d0z", 0, 256), 1.0)
-    act(r("d0z", 0, 256, 4), r("iot", 0, 64), F.Copy, scale=0.0)
-    for i in range(4):
-        const(r("mm_", 160 * i + 128, 160 * i + 160), 0.0)
-    const(col("cf", 35), 1024.0)
     const(r("cf", 32, 35), 0.0)
     const(r("cf", 32, 33, 1, 96, 128), -TINY)
     const(r("cf", 33, 34, 1, 64, 128), -TINY)
     const(r("cf", 34, 35, 1, 64, 128), -TINY)
     const(r("cf", 34, 35, 1, 32, 64), -TINY)
-    lin(col("cf", 4), col("cf", 1), 1.0, 1.0)
-    lin(col("cf", 6), col("cf", 2), 1.0, 1.0)
-    lin(col("cf", 7), col("cf", 2), -1.0, -16.0)
-    lin(col("cf", 12), col("cf", 1), -float(KC), -float(KC))
-    lin(r("cf", 15, 17), r("jo", 0, 2), 3.0 / 1024, 0.0)
     ts(r("jj", 0, 64), r("jr", 0, 64), col("jo", 0), A.is_lt, -TINY, A.mult)
     ts(r("jj", 64, 128), r("jr", 0, 64), col("jo", 1), A.is_lt, TINY, A.mult)
-    lin(col("cf", 28), col("cf", 26), -3.0, col("cf", 12))
-    SOC = r("kk", 0, 6)
-    lin(SOC, SOC, 1.0, col("cf", 28))
-    lin(col("cf", 29), col("cf", 2), -float(KC), 768.0 * rank - KC)
-    lin(col("cf", 30), col("cf", 2), 1024.0, 768.0 * rank + 17 * 1024)
     lin(r("kk", 18, 22), r("iot", 0, 4), 0.25, 0.0)
+    lin(r("kk", 0, 4), r("iot", 0, 4), 0.25, 16.0)
+    const(r("c4", 0, 128), 1.0)
+    const(r("c4", 2, 128, 4), C05)
+    const(r("c4", 3, 128, 4), 0.0)
+    const(r("wm", 0, 96), 1.0)
+    const(r("wm", 0, 96, 8), 0.0)
+    const(r("fr_", 0, 32), 7.0)
+    for c, u in ((0, 0), (1, 5), (16, 4), (17, 0)):
+        lin(r("fr_", c, c + 8 - c % 2, 2), r("iot", 0, 4), 8.0, 8.0 * u + 7)
+    for c, u in ((8, 9), (9, 11), (24, 10), (25, 9)):
+        const(col("fr_", c), 8.0 * u + 7)
+    tr(r("fr_", 32, 64), r("fr_", 0, 32))
+    copy("v", r("fo", 0, 2), r("fr_", 32, 34))
+    ts(r("dvo", 0, 6), r("iot", 0, 192, 32), col("cf", 2), A.add)
+    lin(col("cf", 4), col("cf", 2), -1.0, col("jo", 0))
+    for h in range(2):
+        lin(r("dv", 96 + 16 * h, 112 + 16 * h), r("iot", 32 * h, 32 * h + 16), 1.0, col("cf", 4))
     copy("s", r("ol", 0, 256), r("iot", 0, 256))
 
     ts(r("fi", 4, 6), r("fi", 0, 2), 8, A.arith_shift_right)
@@ -506,21 +512,20 @@ def rank_program(g, core, T, topo):
     ts(r("fi", 8, 10), r("fi", 6, 8), 7, A.bitwise_and)
     ts(r("fa", 14, 16), r("fi", 8, 10), float(LC), A.mult, float(FAR0), A.add)
     for k in range(2):
-        lin(r("nl", k, 768, 3), r("nbf", k, 768, 3), 1.0, -256.0 * rank)
+        lin(r("nl", k, 192, 3), r("nbf", k, 192, 3), 1.0, -256.0 * rank)
     tt(r("ac", 10, 12), r("ac", 8, 10), r("ac", 4, 6), A.subtract)
     ts(r("ac", 12, 14), r("ac", 10, 12), 0.5, A.mult)
     tt(r("ac", 14, 16), r("ac", 12, 14), r("fa", 14, 16), A.add)
     for h in range(2):
         times(r("sp", 128 + 32 * h, 160 + 32 * h), CONE, col("ac", 14 + h))
     tr(r("ex", 512, 576), r("sp", 128, 192))
-    exchange("ex", 64, 512)
     ts(r("ci", 5, 6), r("ci", 2, 3), 3.0, A.mult, 2.0, A.add)
     ts(r("ci", 6, 7), r("ci", 5, 6), 15, A.bitwise_and)
     copy("v", col("cf", 41), r("ci", 6, 7))
     lin(col("cf", 48), col("cf", 41), 7.0, 6.0)
     ts(r("frt", 8, 12), r("iot", 0, 448, 112), col("cf", 48), A.add)
-    ts(r("pm", 0, 16), r("iot", 0, 256, 16), col("cf", 41), A.add)
-    copy("s", r("nl", 2, 768, 3), (FL, r("pm", 0, 16)))
+    ts(r("pm", 0, 4), r("iot", 0, 64, 16), col("cf", 41), A.add)
+    copy("s", r("nl", 2, 192, 3), (FL, r("pm", 0, 4)))
 
     dma([("y", r("rl", 21, 32), r("iot", 0, 11))])
     tr(r("rl2", 0, 32), r("rl", 0, 32))
@@ -537,17 +542,17 @@ def rank_program(g, core, T, topo):
     w1 = w0 or 128
     iota(r("ndv", w1, 256), [[1, 256 - w1]], NEW0 + w1 - w0, 0)
     iota(r("ndv", 0, w1), [[1, w1]], NEW0 + (256 - w0) % 256, 0)
-    for i in range(4):
-        iota(r("np0", 512 * i, 512 * i + 512), [[0, 512]], 0, 0, after=[asked])
+    const(r("np0", 0, 256), 0.0)
+    dma([("y", r("np0", 256 * i, 256 * i + 256), r("np0", 0, 256)) for i in range(1, 8)])
     iota(r("od", 0, 96), [[1, 96]], P, 0)
 
-    for i in range(0, 768, 256):
-        copy("s", r("nl", 768 + i, 1024 + i), r("nl", i, i + 256))
-    copy("v", r("db", 0, 192), (r("nl", 0, 768), r("dbt", 0, 12)))
+    copy("v", r("db", 0, 192), (r("nl", 0, 192), r("dbt", 0, 12)))
+    copy("s", r("dv", 0, 96), (r("db", 0, 192), r("dvo", 0, 6)))
+    dma([("y", r("junk", 0, 256), r("ea", 0, 256))])
+    const(r("ea", NEW0 + 224, NEW0 + 256), 0.0)
     fill(r("xt", 0, 512), 0.0)
     for b in range(4):
         quant(r("qa", 128 * b, 128 * b + 128), r("sa", 128 * b, 128 * b + 128), r("at", 512 * b, 512 * b + 512))
-    dma([("y", r(n % t, 96, 128), r(s, 0, 32)) for t in range(3) for n, s in (("nq%d", "qx"), ("ns%d", "sx"))])
     quant(r("qw", 0, 128), r("sw", 0, 128), r("wt", 0, 512))
     mm(r("py", 0, 256), r("qw", 0, 128), r("sw", 0, 128), r("qx", 0, 256), r("sx", 0, 256))
     copy("s", r("yw", 0, 256), r("py", 0, 256))
@@ -556,25 +561,26 @@ def rank_program(g, core, T, topo):
     copy("v", r("dnb", 0, 12), r("dt_", 0, 192, 16))
 
     def places(t):
-        copy("v", r("ndl", 0, 2), r("nd_", 0, 2))
+        copy("v", r("ndl", 0, 2), r("nd_", 16 * t + 8, 16 * t + 10))
         scatter(r("ol", 0, 256), r("ndl", 0, 2), r("od", 32 * t, 32 * t + 32))
-
-    def q32(i, b):
-        return r("sc4", 128 * i + 32 * b, 128 * i + 32 * b + 32)
 
     for t in range(R):
         gq, gs, W, oz = "g%d" % t, "h%d" % t, NEW0 + 256 * t, 12 * t
-        e0, e1 = (W - 256, W) if t else (FAR0, NEW0)
-        em = (e0 + e1) // 2
-        mm(r("pe", 0, em - e0), r("qu", 0, 128), r("su", 0, 128), r(gq, e0, em), r(gs, e0, em))
-        mm(r("pf", 0, e1 - em), r("qu", 0, 128), r("su", 0, 128), r(gq, em, e1), r(gs, em, e1))
-        copy("v" if t else "s", r("ea", e0, em), r("pe", 0, em - e0))
-        copy("s", r("ea", em, e1), r("pf", 0, e1 - em))
         if t:
-            for k in range(3):
-                copy("svv"[k], r("d1z", k, 256, 4), (r("ea", 0, W), r("of", oz + 4 * k, oz + 4 * k + 4)))
-            scan(r("zs", 0, 256), r("d0z", 0, 256), r("d1z", 0, 256), 0.0, A.mult, A.add)
-            act(r("z", 0, 64), r("zs", 3, 256, 4), F.Abs)
+            win = r("er", 8 + 8 * t, 15 + 8 * t)
+            copy("v", r("es", 0, 128), (win, r("spo", 0, 8)))
+            copy("s", r("es", 128, 224), (win, r("spo", 8, 14)))
+            tr(r("ea", W - 256, W - 128), r("es", 0, 128))
+            tr(r("ea", W - 128, W - 32), r("es", 128, 224))
+        else:
+            mm(r("px", 0, 336), r("qu", 0, 128), r("su", 0, 128), r(gq, FAR0, NEW0), r(gs, FAR0, NEW0))
+            copy("s", r("ea", FAR0, NEW0), r("px", 0, 336))
+        if t:
+            copy("s", r("zs", 0, 64), (r("junk", 0, W), r("of", oz, oz + 4)))
+            tt(r("zs", 64, 128), (r("junk", 0, W), r("of", oz + 4, oz + 8)), r("zs", 0, 64), A.add)
+            tt(r("zs", 128, 192), (r("ea", 0, W - 32), r("of", oz + 8, oz + 12)), r("zs", 64, 128), A.add)
+            tt(r("zs", 192, 256), r("zs", 128, 192), r("d1z", 0, 64), A.add)
+            act(r("z", 0, 64), r("zs", 192, 256), F.Abs)
         else:
             scan(r("zr", 0, 448), r("d0r", 0, 448), r("d1r", 0, 448), 0.0, A.mult, A.add)
             act(r("z", 0, 64), (r("zr", 0, 448), r("frt", 8, 12)), F.Abs)
@@ -583,64 +589,62 @@ def rank_program(g, core, T, topo):
         ts(r("dd", 0, 64), r("z", 0, 64), col("zt", 0), A.subtract)
         act(r("dd", 64, 128), r("z", 0, 64), F.Identity, bias=col("zt", 32), scale=-1.0)
         for h in range(2):
-            o = 320 * h
+            o = 256 * h
             tt(r("mm_", o, o + 64), r("dd", 64 * h, 64 * h + 64), r("jj", 64 * h, 64 * h + 64), A.is_lt if h else A.is_gt)
             for d in range(1, 4):
-                o2 = o + (0, 64, 160, 224)[d]
-                ts(r("mm_", o2, o2 + 64), r("z", 64 * d, 64 * d + 64), col("zt", 32 * h), A.subtract, col("cf", 31 + d), A.is_gt)
-            scan(r("cx", 160 * h, 160 * h + 160), r("mm_", o, o + 160), r("mm_", o + 160, o + 320), col("cf", 15 + h), A.add, A.add)
-            tr(r("cr", 32 * h, 32 * h + 32), r("cx", 160 * h + 128, 160 * h + 160))
-        ts(r("cl", 0, 64), r("cr", 0, 64), col("cf", 1), A.max, col("cf", 4), A.min)
-        ts(r("cl", 64, 128), r("cr", 0, 64), col("cf", 2), A.max, col("cf", 6), A.min)
-        act(r("junk", 1792, 1856), r("cl", 0, 64), F.Copy, scale=1024.0, acc=col("sa_", 0))
-        act(r("cl", 128, 192), r("cr", 0, 64), F.Relu, bias=col("cf", 7))
-        act(r("junk", 1856, 1920), r("cl", 64, 128), F.Copy, scale=1024.0, acc=col("sb_", 0))
-        act(r("cl", 192, 256), r("cl", 128, 192), F.Relu, bias=col("cf", 35), scale=-1024.0, acc=col("sb_", 1))
-        for a in range(4):
-            copy("vs"[a % 2], blk("sa_", 1, 2, a), blk("sa_", 0, 1, (a + 1) % 4))
-        PRE = r("sel", 16, 22)
-        ts(PRE, SOC, col("sa_", 0), A.add, col("sa_", 1), A.add)
-        act(r("sa_", 2, 3, 1, 0, 64), r("sa_", 0, 1, 1, 64, 128), F.Identity, bias=r("sa_", 1, 2, 1, 64, 128))
-        ts(r("sa_", 2, 3, 1, 64, 128), r("sa_", 0, 1, 1, 0, 64), r("sa_", 1, 2, 1, 0, 64), A.add)
-        ts(r("so", 0, 6), PRE, col("sa_", 2), A.add)
-        copy("v", r("ng", 0, 96), (r("nl", 0, 1536), r("so", 0, 6)))
-        tr(r("nt", 0, 96), r("ng", 0, 96))
-        copy("v", r("po", 0, 6), r("nt", 0, 96, 16))
-        exchange("sb_", 2)
-        act(r("sel", 4, 8), r("sb_", 0, 8, 2), F.Copy, acc=col("sel", 1))
-        act(r("sel", 8, 12), r("sb_", 1, 8, 2), F.Copy, acc=col("sel", 2))
-        act(col("sel", 12), col("sel", 1), F.Identity, bias=col("cf", 29))
-        act(col("sel", 13), col("sel", 2), F.Identity, bias=col("cf", 30), scale=-1.0)
-        nd, na = r("nd_", 4 + 2 * (t % 2), 6 + 2 * (t % 2)), "nda%d" % t
-        act(nd, r("sel", 12, 14), F.Copy, scale=THIRD)
+                ts(r("mm_", o + 64 * d, o + 64 * d + 64), r("z", 64 * d, 64 * d + 64), col("zt", 32 * h), A.subtract, col("cf", 31 + d), A.is_gt)
+            scan(r("cx", 128 * h, 128 * h + 128), r("mm_", o, o + 128), r("mm_", o + 128, o + 256), 0.0, A.add, A.add)
+        const(r("wn", 0, 256), 0.0)
+        for h in range(2):
+            ts(r("so", h, 8, 2), r("kk", 0, 4), col("cx", 128 * h + 127), A.add, 4.0, A.mult)
+        scatter(r("wn", 0, 1088), r("so", 0, 8), r("dv", 0, 128))
+        tr(r("wt_", 0, 128), r("wn", 64, 192))
+        tr(r("wt_", 128, 288), r("wn", 48, 208))
+        tr(r("wt_", 288, 320), r("wn", 67, 192, 4))
+        tr(r("wt_", 320, 384), r("wn", 3, 256, 4))
+        copy("v", r("wx", 0, 96, 4), r("wt_", 0, 384, 16))
+        for d in (1, 3):
+            for a in range(4):
+                b = (a + d) % 4
+                copy("vs"[a % 2], r("wx", d, 96, 4, 32 * a, 32 * a + 32), r("wt_", 0, 384, 16, 32 * b, 32 * b + 32))
+        copy("s", r("wx", 2, 96, 4, 0, 64), r("wt_", 0, 384, 16, 64, 128))
+        copy("s", r("wx", 2, 96, 4, 64, 128), r("wt_", 0, 384, 16, 0, 64))
+        scan(r("sm", 0, 96), r("wm", 0, 96), r("wx", 0, 96), 0.0, A.mult, A.add)
+        copy("v", r("po", 0, 16), (r("sm", 0, 96), r("fo", 0, 1)))
+        nd, na, n0 = r("sel", 16 * t + 8, 16 * t + 10), "nda%d" % t, 16 * t + 8
+        act(r("nd_", 16 * t, 16 * t + 16), (r("sm", 0, 96), r("fo", 0, 1)), F.Copy)
         if t < 2:
+            act(r("sel", 16 * t, 16 * t + 16), (r("sm", 0, 96), r("fo", 0, 1)), F.Copy, bias=256.0 * rank)
             send_all(nd, lambda d: r(na, 2 * rank, 2 * rank + 2), "an%d" % t, [r(na, 2 * s, 2 * s + 2) for s in peers])
             dma([("y", r(na, 2 * rank, 2 * rank + 2), nd)])
-        act(r("nd_", 0, 2), nd, F.Copy, bias=-256.0 * rank)
         nq, ns = "nq%d" % t, "ns%d" % t
-        pick(r(nq, 0, 96), r(ns, 0, 96), r(gq, 0, W), r(gs, 0, W), r("po", 0, 6))
+        pick(r(nq, 0, 128), r(ns, 0, 128), r(gq, 0, W), r(gs, 0, W), r("po", 0, 8))
         for b in range(4):
             mm(r("ps", 512 * b, 512 * b + 128), r("qa", 128 * b, 128 * b + 128), r("sa", 128 * b, 128 * b + 128), r(nq, 0, 128), r(ns, 0, 128))
         for c in range(2):
-            ts(r("bo", c, 8, 2), r("kk", 18, 22), col("nd_", c), A.add, 4.0, A.mult)
+            ts(r("bo", c, 8, 2), r("kk", 18, 22), col("nd_", n0 + c), A.add, 4.0, A.mult)
         copy("s", r("bbs", 0, 128), (r("bb_t", 0, 1024), r("bo", 0, 8)))
-        for b in range(4):
-            copy("s", q32(0, b), r("ps", 512 * b, 512 * b + 32))
-        for k, b in ((1, 0), (1, 1), (2, 0), (1, 2), (2, 1), (1, 3), (2, 2), (2, 3)):
-            tt(q32(k, b), q32(k - 1, b), r("ps", 512 * b + 32 * k, 512 * b + 32 * k + 32), A.add)
         if t == 2:
             places(t)
         for b in range(4):
-            act(q32(3, b), q32(2, b), F.Copy, scale=C05)
-            tt(r("xt", b, 128, 4), q32(3, b), r("bbs", 32 * b, 32 * b + 32), A.add)
+            scan(r("sc4", 128 * b, 128 * b + 128), r("ps", 512 * b, 512 * b + 128), r("c4", 0, 128), 0.0, A.add, A.mult)
+        for b in range(4):
+            tt(r("xt", b, 128, 4), r("sc4", 128 * b + 2, 128 * b + 128, 4), r("bbs", 32 * b, 32 * b + 32), A.add)
         if t == 2:
             copy("s", r("og", 0, 256), (r("ol", 0, 256), r("d8", 0, 16)))
         o0 = P + 32 * t
         if t < 2:
             nq, ns, at = "g%d" % (t + 1), "h%d" % (t + 1), W + 224
             quant(r(nq, at, at + 128), r(ns, at, at + 128), r("xt", 0, 512))
+            for i, bank in enumerate(("pe", "pf")):
+                mm(r(bank, 0, 128), r(nq, at, at + 128), r(ns, at, at + 128), r("qu", 0, 128), r("su", 0, 128))
+                for a in (2 * i, 2 * i + 1):
+                    copy("vs"[i], blk("ep", 4 + 4 * t, 5 + 4 * t, a), blk(bank, 0, 1, 0))
+            send_all(col("ep", 4 + 4 * t), lambda d: r("er", *slot(d, 1, 16 + 8 * t)), "ae%d" % t, [r("er", 16 + 8 * t, 23 + 8 * t)])
             for n, arr in ((nq, "ac%d" % (t + 1)), (ns, "as%d" % (t + 1))):
-                send_all(r(n, at, at + 32), lambda d: r(n, *slot(d, 32, W)), arr, [r(n, W, at)], 1.2)
+                send_all(r(n, at, at + 32), lambda d: r(n, *slot(d, 32, W)), arr, [r(n, W, at)], 1.5)
+            mm(r("px", 0, 128), r("qu", 0, 128), r("su", 0, 128), r(nq, at, at + 128), r(ns, at, at + 128))
+            copy("s", r("junk", at, at + 32), r("px", 0, 32))
             dma([("y", r("ow", o0, o0 + 32), r(nq, at, at + 32)), ("y", r("os_", o0, o0 + 32), r(ns, at, at + 32))])
         else:
             nq, ns, at = "ow", "os_", o0
@@ -651,9 +655,7 @@ def rank_program(g, core, T, topo):
             dma([("y", r("g1", 0, NEW0), r("g0", 0, NEW0)), ("y", r("h1", 0, NEW0), r("h0", 0, NEW0))])
             dma([("y", r("g2", 0, NEW0), r("g0", 0, NEW0)), ("y", r("h2", 0, NEW0), r("h0", 0, NEW0))])
             lin(r("ndv", 256, 512), r("ndv", 0, 256), 1.0, 256.0)
-        ts(col("sel", 0), col("sa_", 0), col("sa_", 1), A.add, col("sa_", 2), A.add)
-        ts(col("nd_", 8 + t), col("sel", 0), col("cf", 12), A.add, THIRD, A.mult)
-        dma([("y", T.nd[t:t + 1, 0:32], r("nd_", 8 + t, 9 + t, 1, 0, 32))])
+        dma([("y", T.nd[t:t + 1, 16 * c:16 * c + 16], r("nd_", n0 + c, n0 + c + 1, 1, 0, 16)) for c in range(2)])
         if t < 2:
             places(t)
         if t == 1:
@@ -668,10 +670,7 @@ def rank_program(g, core, T, topo):
             tt(r("db", 0, 192), (npn, r("dnb", 0, 12)), r("db", 0, 192), A.max)
             tr(r("dt_", 0, 192), r("db", 0, 192))
             copy("v", r("of", 12 * t + 12, 12 * t + 24), r("dt_", 0, 192, 16))
-            for i in range(0, 48, 8):
-                tt(r("nl", 16 * i, 16 * i + 128), (npn, r("nbt", i, i + 8)), r("nl", 16 * i, 16 * i + 128), A.max)
-            for i in range(0, 768, 256):
-                copy("s", r("nl", 768 + i, 1024 + i), r("nl", i, i + 256))
+            copy("s", r("dv", 0, 96), (r("db", 0, 192), r("dvo", 0, 6)))
 
     tr(r("ogt", 0, 256), r("og", 0, 256))
     copy("v", r("oo", 0, 16), r("ogt", 0, 256, 16))

@@ -1,33 +1,29 @@
-import numpy as np
 from concourse.bass import DstId, RemoteDMATransfer
 from concourse.mybir import dt, AluOpType, AxisListType, ActivationFunctionType
 
 A = AluOpType
 F = ActivationFunctionType
 P, K, R, LC = 256, 32, 3, 48
-FAR0 = P
-NEW0 = P + 7 * LC
+OWN0, FAR0, LAND0 = 256, 448, 784
+UP = 4096.0
 C05 = 13421773 * 2.0 ** -28
 TINY = 2.0 ** -110
-CYC, HOLD, FLY, FIRST, LOAD = 0.001, 0.25, 2.4, 2.0, 2.2
 ORDER = """
-6 13 20 2 49 149 4 21 22 5 27 26 29 28 30 34 131 31 39 38 12 1 67 8 3 9 15 132 0 16 40 150 24 83s 234 33 10 129s 144 43 41 11 35s 32
-154 23 37 50 25 42 151 7 45 127 36 44 108 172 19 17 109 14 46 107 111 47 140 48 110 186 112 115 51 173 133 266 52 113 134 241 54 55 53
-141 257 121 57 114 116 59 60 56 63 62 171 142 61 65 128 66 78 64 68 85 80 174 70v 122 72v 69s 71s 181 170 74v 175 58s 73s 188 77 169 79
-76 75 176 143 227 82 117 81 92 214 135 84 145 89v 187 93s 88s 87v 86s 94s 91 97s 256 118 96 90 235 95 100 98 101 177 103 99 105 136
-104s 106 218 102 182 189 137s 146 219 152 153 202 138 220s 147 119 183 205 155 148 120 221 196 190 156 139 222 157 124 184 223 158 185s
-224 204 168 166 228 159s 164 236 163s 18 160v 165s 161s 237 167 125 203 200 194 193 162v 225 239 207 242 226 285 215 306 229s 244 243
-192 206 238 191 245 230 286 249 231s 123 232s 247 288 246 248 293 213 289s 130 251 295 290 210 233 287s 291s 250 294 292 208 240 254
-209 267s 301 270 268 302 216 297 197 198 252 258 296 304 303 260 195 253 259 298 299 263 178s 305 300 308 211 201 307 275 309 212 312
-310 255 311 313 272 314s 322 316v 323 320 321s 319 324v 315 318v 317s 273 325 264 274 326 328 333 331 271 332 327 336 338 334 335 372
-199 339 280 281 371 262 343 329 337 265 341 340 330 342 369 344 347 217 345 261 346 348 411 279 349 283 377 179 353 350 284 351 354 352
-355 282 378 180 362 479 379 269 356 380 357 363 375 384 381 276 387v 388 358 383 386 385 389 390 480 376 391 398 394s 395v 392 399 393
-402 407 400 396s 397 360 406 374 401 404 403 277 409 408 405 410 382 412 413 368 414 361 417 418 416 278 359 415 428 424s 423v 425 426
-365 421v 419s 429v 422s 478 427v 420s 430 431 432 437 433 438 439 436 442 443 444 481 445 446 449 440 441 516 447 448 453 450 451 434
-452 435 454 455 458 456 459 473 460 457 482 366 461 483 484 370 467 462 468 485 486 492 469 493 489 488 491 490 494 495 496 503 499s
-477 497s 500v 463 498 505 475 504 501s 373 512 502 507 487 506 511 508 464 509 513 514 364 510 515 517 518 519 367 521 523 522 520 525
-528 531s 465 524 533v 466 534 126 530 532v 526 529 527s 476 535 536 470 537 538 471 547 545 539 544 542 548 540 541 543 551 546 549 550
-552 553 555 554 556 557 472 563 558 564 565 561 562 559 474 566 570 568 567 571 569 560 573 572 574
+22 7 17s 21 8y 5 12y 4 2 15 9y 3s 23 28 11 1 27 13y 6s 10 16 0 19s 14 29 18 30 20 35 87s 31 128 52v 24 39 32 176v 36 25 34 33 71 178 38 46 40
+37v 217s 47 41 129 188 114 48 113 112v 43s 151 44s 49 42s 115v 45s 50 116 189 51 26 169 72s 165 153 190 55 130 154 58 56 195 59 111 57s 138 53v
+140 61s 124 126 60 63 117 199 54 125 64 67 66 65 141s 70v 118 69s 127s 83s 182 73 68 119 76s 75v 74s 77v 84 62s 120 142 152 78 79 187 89s 202
+167 139v 81 194 179 168v 80 236 206 155 82 86v 237 159 157 207 85s 148 170v 143 131 203 88 96s 181 166 198 93 97 90s 91v 92s 144 180s 98s 134
+94s 95v 150 145 204 160 100 105 102 104 101s 99s 171 103 109 107 172 110 106 108 205 215 147 146 122 149 135 132 162 200 173 240 209 208 196 234
+174 161 232 185 241 239 136 121 175 177s 210s 238 242 212s 243 244 245 247 235 123 246 248 211s 213s 218 249 220 250s 219 253 137 251 252s 221
+262 191 256 214 254s 222 223 255 224 225 133 263 227 258 266 264 259 260 257 265 226 193 216 230 186 183 261 267 228 268 269 164 270 201 271 273
+274 272 184v 163 282s 275 283 279v 277 276 281 280 284 285v 278 231 192 156 286 158 287 233 293 289 290 288 197 325 324s 229 292 299 298 296 294
+300 295 304 297 362 302 303 305 308 306 307 291 309 310 301 311 321 333 312 326 313 319 317 315 320 327 334 329 328 335 330 332 314 336 331 338
+337 341 318 339 342 340 343 347 346 356v 345 344 350 348s 357 349 352 358 322 316 351 354 360 353 359 355 361 363 364 365 367 369 366 368 377s
+379v 370s 376v 378 371 380 375 373s 374v 457 372v 381 382 383 384 388 387 385 394 393 389 390 395 392 397 391 419s 398 400 399 401 404 402 403
+405 396 406 416 407 386 414 408 428 412 410 421 415 422 429 424 423 430 409 431 426 425 432 433 434 413 436 427 435 437 420s 438 442 441 445 440v
+439s 451v 443s 446 444 447 453 452 448 454 449 455 450 456 458 459 460 411 462 464 461 463 471 465 472 469 473 467v 470s 468 474 466 475 323 476
+477 478v 480 479 501 488 417 502s 485 484 486 481 418 503 482 492 483 489 490 487 491 504 496 494 493 495 505 497 506 498 499 507 500 508 513y
+509s 511 510 512
 """
 CODE, U8, BF, F32, I32, U16 = "float8_e4m3fn_x4", "uint8", "bfloat16", "float32", "int32", "uint16"
 
@@ -38,20 +34,19 @@ def _sbuf(dtype, **cols):
 
 SCRATCH = {"pe": ("psum", [128, 512], F32), "pf": ("psum", [128, 512], F32), "ps": ("psum", [128, 2048], F32), "py": ("psum", [128, 512], F32),
            "px": ("psum", [128, 512], F32)}
-SCRATCH.update(_sbuf(F32, nbf=192, iot=2048, jr=256, jf=256, cf=64, jo=6, ka=256, kat=64, junk=2560, cq=1024, cz=512, ac=32, fa=28,
-                     sp=192, ex=576, cc=128, lo=16, ea=1104, fn=256, z=256, zt=64, dd=128, jj=128, zs=256, d1z=64, cx=256, c4=288,
-                     wn=1088, wt_=576, dv=128, sel=48, kk=264, nd_=48, bbs=128, sc4=512, nda0=16, nda1=16,
-                     np0=2048, ndv=512, nl=192, db=192, dbz=192, dt_=192, dtz=192, ol=256, od=96, og=256, ogt=256, yt=256,
-                     ep=12, er=32, es=448, est=480, fz=256, d0r=448, d1r=448, zr=448, rl=32, rl2=96, lst=4, yw=352))
-SCRATCH.update(_sbuf(I32, nb32=48, ci=16, fi=16, frf=256, gi=128))
-SCRATCH.update(_sbuf(U16, nbt=12, far16=16, pm=4, rep=24, so=8, po=16, dvo=36, ndl=2, nai=16, bo=8, dbt=12, dnb=12, of=36, frt=36, d8=16, oo=16))
-SCRATCH.update(_sbuf(BF, xb=1024, bb_t=1024, at=2048, wt=512, u4=4, v4=4, ub=512, vb=512, mm_=512, xt=512))
+SCRATCH.update(_sbuf(F32, nbf=192, iot=2048, jf=256, cf=64, jo=8, ka=256, kat=64, junk=2304, cq=768, cz=384, ac=32, fa=28, sp=256, ex=576, cc=128,
+                     lo=16, fn=256, z=256, dd=128, jj=128, c4=288, wn=1088, wt_=576, dv=128, kk=288, nd_=48, bbs=128, sc4=512, ndv=448, od=96,
+                     og=256, ogt=256, yt=256, ept=256, ep=8, ec=64, er=72, rl=32, rl2=96, lst=4, et=256, ol=256, mk=128, tg=64, lg=64, dz=132,
+                     fz=72, zo=80, ok=4, rel=128, jr=64, ft=128, lp=256, d16=128, nw=64, pat=64))
+SCRATCH.update(_sbuf(I32, nb32=48, ci=16, fi=16, gi=16, fr=256))
+SCRATCH.update(_sbuf(U16, nbt=12, far16=16, rep=24, so=8, po=48, sel=4, an=32, bo=8, frt=4, cl=8, dl=4, ll=4, c01=8, flp=2, fl2=2, jo16=2, fo=2,
+                     d8=16, oo=16))
+SCRATCH.update(_sbuf(BF, xb=1024, bb_t=1024, at=2048, wt=512, u4=4, v4=4, ub=512, vb=512, mm_=512, xt=512, cx=256, zb=128))
 for _c, _s, _n in (("qx", "sx", 256), ("qb", "sb", 256), ("qu", "su", 128), ("qv", "sv", 128), ("qa", "sa", 512), ("qw", "sw", 128), ("slc", "sls", 336),
-                   ("g0", "h0", 592), ("g1", "h1", 944), ("g2", "h2", 1200), ("nq0", "ns0", 128), ("nq1", "ns1", 128), ("nq2", "ns2", 128),
-                   ("ow", "os_", 448), ("occ", "ocs", 256)):
+                   ("gq", "gs", 1232), ("nq0", "ns0", 128), ("nq1", "ns1", 128), ("nq2", "ns2", 128), ("occ", "ocs", 256)):
     SCRATCH.update({_c: ("sbuf", [128, _n], CODE), _s: ("sbuf", [128, _n], U8)})
-SEMAPHORES = ["cv", "cs", "ct", "cg"] + ["q%d" % i for i in range(70)] + ["aer", "arl", "ac0", "as0", "an0", "an1", "ae0", "ae1", "ac1", "as1", "ac2", "as2"]
-PARTS = {"wm": ("c4", 128), "fr_": ("c4", 224), "wx": ("wt_", 384), "sm": ("wt_", 480), "fo": ("dvo", 6), "spo": ("dvo", 8)}
+SEMAPHORES = ["cv", "cs", "ct", "cg"] + ["q%d" % i for i in range(40)] + ["aer", "arl", "ac0", "as0", "an0", "an1", "ae0", "ae1", "ac1", "as1", "ac2", "as2"]
+PARTS = {"wm": ("c4", 128), "fr_": ("c4", 224), "wx": ("wt_", 384), "sm": ("wt_", 480)}
 
 
 def r(name, c0, c1, step=1, p0=0, p1=128):
@@ -106,14 +101,11 @@ def rank_program(g, core, T, topo):
         for x in reads:
             log.setdefault(x[0], []).append((x, span(x), 0, i, q))
 
-    def put(q, fn, reads, writes, cost, late=0.0, sem=None, inc=1, deps=(), alt=False):
+    def put(q, fn, reads, writes, sem=None, inc=1, deps=(), alt=""):
         i = len(ops)
-        ops.append({"q": q, "fn": fn, "deps": meets(reads, writes, q) | set(deps), "cost": cost, "late": late, "sem": sem, "inc": inc, "alt": alt, "peers": [i]})
+        ops.append({"q": q, "fn": fn, "deps": meets(reads, writes, q) | set(deps), "sem": sem, "inc": inc, "alt": alt, "peers": [i]})
         note(q, reads, writes, i)
         return i
-
-    def emit(q, fn, reads, writes, cycles, fixed=0.0, deps=(), alt=False):
-        put(q, fn, reads, writes, fixed + max(64, cycles) * CYC, deps=deps, alt=alt)
 
     def width(x):
         return -(-(x[2] - x[1]) // x[3])
@@ -123,9 +115,9 @@ def rank_program(g, core, T, topo):
             for k in list(o["deps"]):
                 o["deps"] |= set(ops[k]["peers"])
             o["deps"].discard(i)
-        out = [int(x.rstrip("vs")) for x in ORDER.split()] or list(range(len(ops)))
+        out = [int(x.rstrip("vsy")) for x in ORDER.split()] or list(range(len(ops)))
         for x in ORDER.split():
-            if x[-1] in "vs":
+            if x[-1] in "vsy":
                 ops[int(x[:-1])]["q"] = x[-1]
         tok = {}
         for i in out:
@@ -148,7 +140,7 @@ def rank_program(g, core, T, topo):
                 s = snaps.setdefault(tok[i], {})
                 for n, m in known[q].items():
                     s[n] = max(s.get(n, 0), m)
-                c = o["fn"](q) if o["alt"] else o["fn"]()
+                c = o["fn"](q)
                 if o["sem"] is None:
                     c.then_inc(T.sem[sem], 1)
 
@@ -164,99 +156,72 @@ def rank_program(g, core, T, topo):
     def sc(x):
         return (ap(x), [x]) if isinstance(x, tuple) else (x, [])
 
-    def by(in_):
-        return 1.5 if len(in_) == 2 else 1
-
     def copy(q, out, in_):
         i, rd = src(in_)
-        n = width(out) * by(in_)
-        names = [out[0]] + [x[0] for x in rd]
-        flex = all(SCRATCH[k][0] == "sbuf" and SCRATCH[k][2] in (F32, BF) for k in names[:2])
-        fns = {"v": lambda: g.vector.tensor_copy(ap(out), i), "s": lambda: g.scalar.activation(ap(out), i, F.Copy)}
-        emit(q, (lambda e: fns[e]()) if flex else fns[q], rd, [out], n, alt=flex)
-
-    def times(out, in_, c):
-        fns = {"v": lambda: g.vector.tensor_scalar(ap(out), ap(in_), ap(c), None, A.mult), "s": lambda: g.scalar.activation(ap(out), ap(in_), F.Copy, scale=ap(c))}
-        emit("v", lambda e: fns[e](), [in_, c], [out], width(out), alt=True)
+        flex = all(SCRATCH[k][2] in (F32, BF) for k in (out[0], rd[0][0])) and SCRATCH[rd[0][0]][0] == "sbuf"
+        put(q, lambda e: g.vector.tensor_copy(ap(out), i) if e == "v" else g.scalar.activation(ap(out), i, F.Copy), rd, [out], alt="vs" if flex else "")
 
     def scatter(win, off, in_):
-        emit("v", lambda: g.vector.tensor_copy(ap(win).indirect(ap(off)), ap(in_)), [in_, off], [win], 3 * width(in_))
+        put("v", lambda e: g.vector.tensor_copy(ap(win).indirect(ap(off)), ap(in_)), [in_, off], [win])
 
     def act(out, in_, func, bias=0.0, scale=1.0, acc=None):
         i, rd = src(in_)
         b, rb = sc(bias)
         s, rs = sc(scale)
-        n = width(out) * by(in_)
-        if acc is None:
-            emit("s", lambda: g.scalar.activation(ap(out), i, func, bias=b, scale=s), rd + rb + rs, [out], n)
-        else:
-            emit("s", lambda: g.scalar.activation(ap(out), i, func, bias=b, scale=s, accum_out=ap(acc)), rd + rb + rs, [out, acc], n)
+        put("s", lambda e: g.scalar.activation(ap(out), i, func, bias=b, scale=s, accum_out=acc and ap(acc)), rd + rb + rs, [out] + ([acc] if acc else []))
 
     def const(out, val):
-        act(out, r("iot", 0, width(out), 1, out[4], out[5]), F.Copy, bias=val, scale=0.0)
+        i = r("zb", 0, width(out), 1, out[4], out[5])
+        put("s", lambda e: g.vector.memset(ap(out), val) if e == "v" else g.scalar.activation(ap(out), ap(i), F.Copy, bias=val, scale=0.0), [i], [out], alt="vs")
 
-    def lin(out, in_, scale, bias):
-        act(out, in_, F.Identity if isinstance(bias, tuple) else F.Copy, bias=bias, scale=scale)
-
-    def ts(out, in_, s1, op0, s2=None, op1=None):
+    def ts(out, in_, s1, op0, s2=None, op1=None, q="v"):
         i, rd = src(in_)
         a, ra = sc(s1)
         b, rb = sc(s2)
-        if all(SCRATCH[x[0]][2] == F32 for x in rd + [out]) and (op0, op1) in ((A.add, None), (A.mult, None), (A.mult, A.add)):
-            mul, add = (1.0, a) if op0 == A.add else (a, 0.0 if op1 is None else b)
-            fn = F.Copy if isinstance(add, float) else F.Identity
-            fns = {"v": lambda: g.vector.tensor_scalar(ap(out), i, a, b, op0, *([] if op1 is None else [op1])),
-                   "s": lambda: g.scalar.activation(ap(out), i, fn, bias=add, scale=mul)}
-            emit("v", lambda e: fns[e](), rd + ra + rb, [out], width(out), alt=True)
-        elif op1 is None:
-            emit("v", lambda: g.vector.tensor_scalar(ap(out), i, a, None, op0), rd + ra, [out], width(out))
-        else:
-            emit("v", lambda: g.vector.tensor_scalar(ap(out), i, a, b, op0, op1), rd + ra + rb, [out], width(out))
+        both = all(SCRATCH[x[0]][2] in (F32, BF) for x in (out, rd[0])) and (op0, op1) in ((A.add, None), (A.mult, None), (A.mult, A.add))
+        mul, add = (1.0, a) if op0 == A.add else (a, 0.0 if op1 is None else b)
+        put(q, lambda e: g.vector.tensor_scalar(ap(out), i, a, b, op0, *([] if op1 is None else [op1])) if e == "v" else
+            g.scalar.activation(ap(out), i, F.Copy if isinstance(add, float) else F.Identity, bias=add, scale=mul), rd + ra + rb, [out], alt="vs" if both else "")
 
     def tt(out, in0, in1, op):
         i, rd = src(in0)
-        emit("v", lambda: g.vector.tensor_tensor(ap(out), i, ap(in1), op), rd + [in1], [out], (1.5 if len(in0) == 2 else 2) * width(out))
+        put("v", lambda e: g.vector.tensor_tensor(ap(out), i, ap(in1), op), rd + [in1], [out])
 
     def scan(out, d0, d1, initial, op0, op1):
         a, ra = sc(initial)
-        emit("v", lambda: g.vector.tensor_tensor_scan(ap(out), ap(d0), ap(d1), a, op0, op1), [d0, d1] + ra, [out], width(out))
-
-    def least(out, in_):
-        emit("v", lambda: g.vector.tensor_reduce(ap(out), ap(in_), AxisListType.X, A.min, apply_absolute_value=True), [in_], [out], width(in_))
+        put("v", lambda e: g.vector.tensor_tensor_scan(ap(out), ap(d0), ap(d1), a, op0, op1), [d0, d1] + ra, [out])
 
     def tr(out, in_):
-        emit("v", lambda: g.vector.transpose(ap(out), ap(in_)), [in_], [out], width(out))
+        put("v", lambda e: g.vector.transpose(ap(out), ap(in_)), [in_], [out])
 
     def fill(out, val):
-        emit("v", lambda: g.vector.memset(ap(out), val), [], [out], width(out))
+        put("v", lambda e: g.vector.memset(ap(out), val), [], [out])
 
-    def quant(q, s, in_):
-        emit("v", lambda: g.vector.quantize_mx(ap(q), ap(s), ap(in_)), [in_], [q, s], width(in_) // 4)
+    def quant(q, s, c0, c1, in_):
+        put("v", lambda e: g.vector.quantize_mx(ap(r(q, c0, c1)), ap(r(s, c0, c1)), ap(in_)), [in_], [r(q, c0, c1), r(s, c0, c1)])
 
-    def mm(out, wq, ws, xq, xs):
-        emit("t", lambda: g.tensor.matmul_mx(ap(out), ap(wq), ap(ws), ap(xq), ap(xs), True, True), [wq, ws, xq, xs], [out], width(out))
+    def mm(bank, at, w, x):
+        out, rd = r(bank, at, at + x[3] - x[2]), [r(w[0], w[2], w[3]), r(w[1], w[2], w[3]), r(x[0], x[2], x[3]), r(x[1], x[2], x[3])]
+        put("t", lambda e: g.tensor.matmul_mx(ap(out), ap(rd[0]), ap(rd[1]), ap(rd[2]), ap(rd[3]), True, True), rd, [out])
 
-    def iota(out, pattern, base, cm, flag=True, after=()):
-        if flag:
-            emit("g", lambda: g.iota(ap(out), pattern, base, cm, allow_small_or_imprecise_dtypes=True), [], [out], 2 * width(out), 0.13, after)
-        else:
-            emit("g", lambda: g.iota(ap(out), pattern, base, cm), [], [out], 2 * width(out), 0.13, after)
+    def iota(out, pattern, base, cm=0):
+        put("g", lambda e: g.iota(ap(out), pattern, base, cm, allow_small_or_imprecise_dtypes=SCRATCH[out[0]][2] != I32), [], [out])
 
     def pick(qo, so, win, wins, off):
-        emit("v", lambda: g.vector.tensor_copy(ap(qo).bitcast(dt.uint32), ap(win).bitcast(dt.uint32).indirect(ap(off))), [win, off], [qo], 1.5 * width(qo))
-        emit("s", lambda: g.scalar.activation(ap(so), ap(wins).indirect(ap(off)), F.Copy), [wins, off], [so], 1.5 * width(so))
+        put("v", lambda e: g.vector.tensor_copy(ap(qo).bitcast(dt.uint32), ap(win).bitcast(dt.uint32).indirect(ap(off))), [win, off], [qo])
+        put("s", lambda e: g.scalar.activation(ap(so), ap(wins).indirect(ap(off)), F.Copy), [wins, off], [so])
 
     def side(x):
         return ap(x).bitcast(dt.uint8) if SCRATCH[x[0]][2] == CODE else ap(x)
 
-    def dma(moves, late=LOAD):
+    def dma(moves):
         sem = newsem()
         made = []
         for q, out, in_ in moves:
             wr = [out] if isinstance(out, tuple) else []
             rd = [in_] if isinstance(in_, tuple) else []
             o, i = side(out) if wr else out, side(in_) if rd else in_
-            made.append(put(q, lambda q=q, o=o, i=i: eng[q].dma_start(o, i).then_inc(T.sem[sem], 16), rd, wr, 0.07, late, sem, 16 * len(moves)))
+            made.append(put(q, lambda e, o=o, i=i: eng[e].dma_start(o, i).then_inc(T.sem[sem], 16), rd, wr, sem, 16 * len(moves), alt="ys"))
         for k in made:
             ops[k]["peers"] = made
 
@@ -276,28 +241,32 @@ def rank_program(g, core, T, topo):
 
     def issue(trs, reads, total):
         sem = newsem()
-        return put("g", lambda: g.remote_dma_fused(trs, local_sem=T.sem[sem]), reads, [], HOLD, FLY - 0.5, sem, total)
+        return put("g", lambda e: g.remote_dma_fused(trs, local_sem=T.sem[sem]), reads, [], sem, total)
 
-    def send_each(moves, arr, regions):
+    def send_each(moves, arr, region):
         i = issue([RemoteDMATransfer(dst_ids=[ids[d]], dma_engine_mask=masks[d], remote_sem=T.sem[arr], srcs=[side(s)], dsts=[side(l)]) for d, s, l in moves],
                   [m[1] for m in moves], 2 * len(moves))
-        put("r", None, [], regions, 0.0, 2.0, arr, 2 * 7, [i])
+        put("r", None, [], [region], arr, 2 * 7, [i])
 
-    def send_all(s, land, arr, regions, more=0.0):
+    def send_all(s, name, base, arr):
+        w = width(s)
         i = issue([RemoteDMATransfer(dst_ids=[ids[d] for d in peers], dma_engine_mask=sum(1 << x for x in full), remote_sem=T.sem[arr], srcs=[side(s)],
-                                     dsts=[side(land(d)) for d in peers])], [s], len(full))
-        put("r", None, [], regions, 0.0, 0.5 + more, arr, len(full) * 7, [i])
-        return i
+                                     dsts=[side(r(name, *slot(d, w, base))) for d in peers])], [s], len(full))
+        put("r", None, [], [r(name, base, base + 7 * w)], arr, len(full) * 7, [i])
 
-    def exchange(n, w=64, o=0):
+    def slot(d, w, base):
+        q = base + w * ((rank - d - 1) % 8)
+        return q, q + w
+
+    def exchange(n, o=0, w=64):
         for a in range(4):
             b = (a + 1) % 4
             copy("vs"[a % 2], r(n, o + w, o + 2 * w, 1, 32 * a, 32 * a + 32), r(n, o, o + w, 1, 32 * b, 32 * b + 32))
         copy("v", r(n, o + 2 * w, o + 4 * w, 1, 0, 64), r(n, o, o + 2 * w, 1, 64, 128))
         copy("s", r(n, o + 2 * w, o + 4 * w, 1, 64, 128), r(n, o, o + 2 * w, 1, 0, 64))
 
-    def col(n, c, w=1):
-        return r(n, c, c + w)
+    def col(n, c):
+        return r(n, c, c + 1)
 
     def blk(n, c0, c1, a):
         return r(n, c0, c1, 1, 32 * a, 32 * a + 32)
@@ -305,9 +274,8 @@ def rank_program(g, core, T, topo):
     def junk(i):
         return r("junk", 256 * i, 256 * i + 256)
 
-    def total(i, x, c):
-        scan(r("cz", 128 * i, 128 * i + 128), r(x, c, c + 128), r(x, c + 128, c + 256), 0.0, A.add, A.add)
-        return col("cz", 128 * i + 127)
+    QX, QU, QV, QW, QB = ("qx", "sx", 0, 256), ("qu", "su", 0, 128), ("qv", "sv", 0, 128), ("qw", "sw", 0, 128), ("qb", "sb", 0, 256)
+    IOT = r("iot", 0, 2048)
 
     mv = []
     for gr in range(8):
@@ -318,77 +286,81 @@ def rank_program(g, core, T, topo):
             mv.append((q, r("nb32", 48 - 12 * a, 48, 1, 16 * gr, 16 * gr + 16), T.nb[:, 0:12 * a]))
     dma(mv)
     dma([("y", r("xb", 0, 1024), T.x[:])])
-    dma([("s", r("u4", 0, 4), T.u[:, 0:4]), ("s", r("v4", 0, 4), T.v[:, 0:4])])
+    dma([("s", r("u4", 0, 4), T.u[:, 0:4])])
+    dma([("s", r("v4", 0, 4), T.v[:, 0:4])])
     dma([("y", r("bb_t", 0, 1024), T.bb[:])])
-    dma([("y", r("at", 0, 2048), T.a[:])])
+    for h in range(2):
+        dma([("y", r("at", 1024 * h, 1024 * h + 1024), T.a[:, 1024 * h:1024 * h + 1024])])
     dma([("y", r("wt", 0, 512), T.w[:])])
 
-    C4096, CM128, C1024, CONE = r("cc", 0, 32), r("cc", 32, 64), r("cc", 64, 96), r("cc", 96, 128)
-    iota(r("ci", 0, 1), [[0, 1]], 0, 1, False)
-    iota(r("iot", 0, 256), [[1, 256]], 0, 0)
-    iota(r("kk", 24, 72), [[0, 16], [1, 3]], 0, 0)
-    iota(r("iot", 1536, 2048), [[1, 512]], 1536, 0)
-    iota(r("lo", 8, 11), [[4096, 3]], 0, 0)
-    iota(r("kk", 6, 18), [[1, 3], [96, 2], [0, 2]], 0, 0)
-    ts(r("ci", 1, 2), r("ci", 0, 1), 31, A.bitwise_and)
-    ts(r("ci", 2, 3), r("ci", 0, 1), 15, A.bitwise_and)
+    C4096, CM128, CONE = r("cc", 0, 32), r("cc", 32, 64), r("cc", 96, 128)
+    PP, P32, P16, B64, PI, PO = col("cf", 0), col("cf", 1), col("cf", 2), col("cf", 26), col("cf", 43), col("cf", 45)
+    fill(r("zb", 0, 128), 0.0)
+    iota(col("ci", 0), [[0, 1]], 0, 1)
+    iota(r("iot", 0, 256), [[1, 256]], 0)
+    iota(r("kk", 24, 72), [[0, 16], [1, 3]], 0)
+    iota(r("iot", 1536, 2048), [[1, 512]], 1536)
+    iota(r("lo", 8, 11), [[4096, 3]], 0)
+    ts(col("ci", 1), col("ci", 0), 31, A.bitwise_and)
+    ts(col("ci", 2), col("ci", 0), 15, A.bitwise_and)
     copy("v", r("cf", 0, 3), r("ci", 0, 3))
-    ts(r("ci", 3, 4), r("ci", 2, 3), 11.0, A.mult)
-    ts(r("ci", 4, 5), r("ci", 3, 4), 5, A.arith_shift_right)
-    ts(col("cf", 40), r("ci", 4, 5), -3.0, A.mult, col("cf", 2), A.add)
+    ts(col("ci", 3), col("ci", 2), 11.0, A.mult)
+    ts(col("ci", 4), col("ci", 3), 5, A.arith_shift_right)
+    ts(col("cf", 40), col("ci", 4), -3.0, A.mult, P16, A.add)
     ts(r("kk", 72, 120), r("kk", 24, 72), col("cf", 40), A.add, 2.0, A.is_equal)
-    ts(r("kk", 120, 168), r("kk", 24, 72), 0.5, A.is_gt)
-    ts(col("cf", 26), col("cf", 0), col("cf", 1), A.subtract, 2.0, A.mult)
+    act(r("kk", 120, 168), r("kk", 24, 72), F.Sign)
+    ts(B64, PP, P32, A.subtract, 2.0, A.mult)
     ts(r("iot", 256, 512), r("iot", 0, 256), 256.0, A.add)
-    act(r("iot", 512, 1024), r("iot", 0, 512), F.Copy, bias=512.0)
-    act(r("iot", 1024, 1536), r("iot", 0, 512), F.Copy, bias=1024.0)
-    ts(r("frf", 0, 256), r("iot", 0, 256), col("cf", 26), A.add)
-    tt(col("jo", 0), col("cf", 26), col("cf", 1), A.add)
-    ts(r("frf", 0, 256), r("frf", 0, 256), 255, A.bitwise_and)
-    ts(col("jo", 1), col("jo", 0), 32.0, A.add)
-    ts(r("jo", 2, 4), r("jo", 0, 2), 1.0 / 512, A.mult)
-    copy("v", r("jr", 0, 256), r("frf", 0, 256))
-    lin(r("jf", 0, 256), r("jr", 0, 256), 1.0 / 512, 0.0)
+    ts(r("iot", 512, 1024), r("iot", 0, 512), 512.0, A.add, q="s")
+    ts(r("iot", 1024, 1536), r("iot", 0, 512), 1024.0, A.add, q="s")
+    ts(r("gi", 8, 12), r("iot", 0, 256, 64), B64, A.add)
+    ts(r("gi", 12, 16), r("gi", 8, 12), 255, A.bitwise_and)
+    ts(r("cf", 28, 32), r("gi", 12, 16), 1.0 / 512, A.mult)
+    for d in range(4):
+        ts(r("jf", 64 * d, 64 * d + 64), r("iot", 0, 64), 1.0 / 512, A.mult, col("cf", 28 + d), A.add)
+    ts(col("cf", 3), PP, 2.0, A.mult, P32, A.subtract)
+    ts(r("jo", 2, 4), r("iot", 0, 64, 32), col("cf", 3), A.add, 1.0 / 512, A.mult)
 
     tt(r("kk", 168, 216), r("nb32", 0, 48), r("kk", 72, 120), A.mult)
     scan(r("kk", 216, 264), r("kk", 120, 168), r("kk", 168, 216), 0.0, A.mult, A.add)
     copy("v", r("far16", 0, 16), r("kk", 218, 264, 3))
-    tt(r("ka", 0, 256), (r("iot", 0, 2048), r("far16", 0, 16)), r("jf", 0, 256), A.add)
-    fill(C4096, 4096.0)
-    fill(CM128, -128.0)
+    tt(r("ka", 0, 256), (IOT, r("far16", 0, 16)), r("jf", 0, 256), A.add)
+    const(C4096, 4096.0)
+    const(CM128, -128.0)
+    const(CONE, 1.0)
     tr(r("kat", 0, 64), r("ka", 0, 64))
     tt(r("jo", 4, 6), r("jo", 2, 4), r("kat", 0, 64, 32), A.subtract)
     ts(junk(0), r("ka", 0, 256), col("jo", 4), A.add)
     act(junk(6), r("ka", 0, 256), F.Sign, bias=col("kat", 32), scale=-1.0, acc=col("ac", 1))
     ts(col("ac", 17), col("kat", 32), -0.5, A.add)
-    act(junk(8), r("ka", 0, 256), F.Sign, bias=col("ac", 17), scale=-1.0, acc=col("ac", 18))
+    act(junk(7), r("ka", 0, 256), F.Sign, bias=col("ac", 17), scale=-1.0, acc=col("ac", 18))
     ts(r("fa", 0, 2), r("jo", 4, 6), -1.0, A.mult)
     ts(r("fa", 2, 4), r("jo", 4, 6), 0.5, A.add)
-    least(col("ac", 0), junk(0))
+    put("v", lambda e: g.vector.tensor_reduce(ap(col("ac", 0)), ap(junk(0)), AxisListType.X, A.min, apply_absolute_value=True), [junk(0)], [col("ac", 0)])
     copy("v", r("fi", 0, 2), r("fa", 0, 2))
     ts(r("fi", 2, 4), r("fi", 0, 2), 255, A.bitwise_and)
-    tt(col("ac", 6), col("ac", 0), col("jo", 2), A.not_equal)
+    ts(col("ac", 6), col("ac", 0), col("jo", 2), A.not_equal)
     ts(col("ac", 7), col("ac", 1), col("ac", 18), A.subtract, 1.0, A.not_equal)
     copy("v", r("fa", 4, 6), r("fi", 2, 4))
-    ts(r("sp", 0, 32), C4096, col("ac", 6), A.mult, col("fa", 0), A.add)
-    act(r("sp", 32, 64), C4096, F.Identity, bias=col("fa", 1), scale=col("ac", 7))
-    ts(col("cf", 17), col("cf", 0), col("cf", 2), A.subtract, 16.0, A.mult)
+    for h in range(2):
+        ts(r("sp", 32 * h, 32 * h + 32), C4096, col("ac", 6 + h), A.mult, col("fa", h), A.add, q="vs"[h])
+    ts(col("cf", 17), PP, P16, A.subtract, -16.0, A.mult)
+    ts(col("cf", 16), col("cf", 17), 0.5, A.add)
     tr(r("ex", 0, 64), r("sp", 0, 64))
-    exchange("ex", 64, 0)
+    exchange("ex")
     FR, CR2, FL = r("ex", 0, 256), r("ex", 256, 512), r("ex", 512, 576)
     for h in range(2):
         act(junk(1 + h), FR, F.Sign, bias=col("fa", 2 + h), acc=col("ac", 4 + h))
-    ts(r("cq", 768, 1024), FR, col("cf", 17), A.is_ge)
+    act(junk(8), FR, F.Sign, bias=col("cf", 16), acc=col("ac", 19))
     ts(r("fa", 6, 8), r("ac", 6, 8), 1048576.0, A.mult)
-    below = total(3, "cq", 768)
     tt(r("fa", 8, 10), r("fa", 6, 8), r("fa", 4, 6), A.add)
-    ts(r("sp", 64, 96), CM128, col("ac", 4), A.mult, col("fa", 8), A.add)
-    act(r("sp", 96, 128), CM128, F.Identity, bias=col("fa", 9), scale=col("ac", 5))
-    ts(col("cf", 18), col("cf", 2), 256.0, A.mult)
+    for h in range(2):
+        ts(r("sp", 64 + 32 * h, 96 + 32 * h), CM128, col("ac", 4 + h), A.mult, col("fa", 8 + h), A.add, q="vs"[h])
+    ts(col("cf", 18), P16, 256.0, A.mult)
     tr(r("ex", 256, 320), r("sp", 64, 128))
-    ts(r("lo", 0, 3), r("lo", 8, 11), col("cf", 18), A.add, 32768.0, A.add)
-    exchange("ex", 64, 256)
-    ts(col("cf", 19), below, -256.0, A.mult)
+    ts(r("lo", 0, 3), r("lo", 8, 11), col("cf", 18), A.add)
+    exchange("ex", 256)
+    ts(col("cf", 19), col("ac", 19), -128.0, A.mult)
     ts(r("lo", 3, 6), r("lo", 0, 3), col("cf", 19), A.add)
     ts(r("lo", 11, 14), r("lo", 3, 6), 256.0, A.add)
     ts(r("cf", 21, 24), r("lo", 3, 6), -255.0, A.mult, -32512.0, A.add)
@@ -398,136 +370,114 @@ def rank_program(g, core, T, topo):
     act(r("cq", 0, 256), junk(5), F.Relu, bias=256.0, scale=-1.0, acc=col("ac", 16))
     for c in (1, 2):
         ts(r("cq", 256 * c, 256 * c + 256), CR2, col("lo", 3 + c), A.max, col("lo", 11 + c), A.min)
-    act(col("lst", 0), col("ac", 16), F.Identity, bias=col("lo", 15), scale=-1.0)
+    ts(col("lst", 0), col("ac", 16), -1.0, A.mult, col("lo", 15), A.add, q="s")
     for c in (1, 2):
-        ts(col("lst", c), total(c, "cq", 256 * c), col("cf", 21 + c), A.add)
+        scan(r("cz", 128 * c, 128 * c + 128), r("cq", 256 * c, 256 * c + 128), r("cq", 256 * c + 128, 256 * c + 256), 0.0, A.add, A.add)
+        ts(col("lst", c), col("cz", 128 * c + 127), col("cf", 21 + c), A.add)
 
-    def slot(d, w, base=0):
-        q = base + w * ((rank - d - 1) % 8)
-        return q, q + w
-
-    quant(r("qx", 0, 256), r("sx", 0, 256), r("xb", 0, 1024))
+    quant("qx", "sx", 0, 256, r("xb", 0, 1024))
     for i in range(4):
-        act(r("ub", i, 512, 4), r("iot", 0, 128), F.Identity, bias=col("u4", i), scale=0.0)
-    quant(r("qu", 0, 128), r("su", 0, 128), r("ub", 0, 512))
-    for h in range(2):
-        mm(r("ps", 512 * h, 512 * h + 128), r("qx", 128 * h, 128 * h + 128), r("sx", 128 * h, 128 * h + 128), r("qu", 0, 128), r("su", 0, 128))
-        copy("s", col("ep", h), col("ps", 512 * h))
-    send_all(r("ep", 0, 2), lambda d: r("er", *slot(d, 2)), "aer", [r("er", 0, 14)], FIRST)
-    send_all(r("lst", 0, 3), lambda d: r("rl", *slot(d, 3)), "arl", [r("rl", 0, 21)])
-    mm(r("pe", 0, 256), r("qu", 0, 128), r("su", 0, 128), r("qx", 0, 256), r("sx", 0, 256))
-    copy("s", r("ea", 0, 256), r("pe", 0, 256))
-    dma([("y", r("g0", 0, 256), r("qx", 0, 256)), ("y", r("h0", 0, 256), r("sx", 0, 256))])
-    dma([("y", r("ow", 0, 256), r("qx", 0, 256)), ("y", r("os_", 0, 256), r("sx", 0, 256))])
+        ts(r("ub", i, 512, 4), r("zb", 0, 128), col("u4", i), A.add, q="s")
+    quant("qu", "su", 0, 128, r("ub", 0, 512))
+    mm("pe", 0, QU, QX)
+    tr(r("ept", 0, 256), r("pe", 0, 256))
+    copy("s", r("ep", 0, 8), r("ept", 0, 256, 32))
+    send_all(r("ep", 0, 8), "er", 0, "aer")
+    send_all(r("lst", 0, 3), "rl", 0, "arl")
+    mm("px", 0, QU, QX)
+    copy("s", r("et", 0, 256), r("px", 0, 256))
+    dma([("y", r("gq", 0, 256), r("qx", 0, 256)), ("y", r("gs", 0, 256), r("sx", 0, 256))])
 
+    ts(col("ci", 7), col("ci", 3), 10.0, A.add)
+    ts(col("ci", 8), col("ci", 7), 15, A.bitwise_and)
+    copy("v", PI, col("ci", 8))
+    ts(PO, P32, P16, A.subtract, PI, A.add)
+    ts(r("jo", 0, 2), r("iot", 0, 64, 32), B64, A.add, PO, A.add)
+    copy("v", r("jo16", 0, 2), r("jo", 0, 2))
+    ts(r("frt", 0, 4), r("iot", 0, 64, 16), B64, A.add, PI, A.add)
+    copy("s", r("jr", 0, 64), (IOT, r("frt", 0, 4)))
+    for h in range(2):
+        ts(r("jj", 64 * h, 64 * h + 64), r("jr", 0, 64), col("jo", h), A.is_lt, TINY, A.mult)
     copy("v", r("nbt", 0, 12), r("nb32", 0, 12))
-    copy("s", r("nbf", 0, 192), (r("iot", 0, 2048), r("nbt", 0, 12)))
-    ts(col("cf", 25), col("cf", 1), 3.0, A.mult)
-    ts(r("dbt", 0, 12), r("kk", 6, 18), col("cf", 25), A.add)
-    ts(r("ci", 7, 8), r("ci", 3, 4), 10.0, A.add)
-    ts(r("ci", 8, 9), r("ci", 7, 8), 15, A.bitwise_and)
-    copy("v", col("cf", 43), r("ci", 8, 9))
-    ts(col("cf", 45), col("cf", 1), col("cf", 2), A.subtract, col("cf", 43), A.add)
-    lin(col("cf", 46), col("cf", 45), 3.0, 0.0)
-    ts(r("frt", 12, 20), r("kk", 6, 14), col("cf", 46), A.add)
-    copy("v", r("dbz", 0, 128), (r("nbf", 0, 192), r("frt", 12, 20)))
-    tr(r("dtz", 0, 128), r("dbz", 0, 128))
-    ts(r("of", 0, 8), r("dtz", 0, 128, 16), -256.0 * rank, A.add)
-    ts(r("gi", 0, 16), r("kk", 218, 264, 3), 2048.0 - 256.0 * (rank + 1), A.add)
-    ts(r("gi", 16, 32), r("gi", 0, 16), 2, A.arith_shift_right, 480, A.bitwise_and)
-    ts(r("gi", 32, 48), r("gi", 0, 16), 31, A.bitwise_and)
-    ts(r("gi", 48, 64), r("gi", 0, 16), 96, A.bitwise_and)
-    lin(col("cf", 49), col("cf", 26), 0.5, 0.0)
-    tt(r("gi", 64, 80), r("gi", 16, 32), r("gi", 32, 48), A.add)
-    ts(r("gi", 80, 96), r("gi", 48, 64), col("cf", 49), A.not_equal, 1024.0, A.mult)
-    tt(r("gi", 96, 112), r("gi", 64, 80), r("gi", 80, 96), A.add)
-    ts(r("frt", 20, 36), r("gi", 96, 112), 448.0, A.min)
-
-    fill(CONE, 1.0)
-    for j in range(2):
-        copy("v", r("spo", j, 28, 2), r("iot", 0, 14))
-    copy("v", r("es", 0, 224), (r("er", 0, 14), r("spo", 0, 14)))
-    copy("s", r("es", 224, 448), (r("er", 0, 14), r("spo", 14, 28)))
-    const(r("est", 448, 480), 0.0)
-    for h in range(0, 448, 224):
-        tr(r("est", h, h + 224), r("es", h, h + 224))
-    copy("s", r("d1r", 2, 448, 7), (r("est", 0, 480), r("frt", 20, 24)))
-    copy("v", r("fz", 64, 256), (r("est", 0, 480), r("frt", 24, 36)))
-    for d in (1, 3):
-        for a in range(4):
-            copy("vs"[a % 2], r("d1r", 2 + d, 448, 7, 32 * a, 32 * a + 32), blk("fz", 64 * (4 - d), 64 * (4 - d) + 64, (a + d) % 4))
-    copy("v", r("d1r", 4, 448, 7, 0, 64), r("fz", 128, 192, 1, 64, 128))
-    copy("s", r("d1r", 4, 448, 7, 64, 128), r("fz", 128, 192, 1, 0, 64))
+    copy("s", r("nbf", 0, 192), (IOT, r("nbt", 0, 12)))
+    iota(r("pat", 0, 8), [[1, 2], [96, 2], [48, 2]], 0)
+    ts(col("cf", 46), PI, 3.0, A.mult)
+    ts(r("cl", 0, 8), r("pat", 0, 8), col("cf", 46), A.add)
+    copy("s", r("lp", 0, 128), (r("nbf", 0, 192), r("cl", 0, 8)))
+    tr(r("lp", 128, 256), r("lp", 0, 128))
+    ts(r("dl", 0, 4), r("lp", 128, 256, 32), -256.0 * rank, A.add)
+    for k in range(2):
+        ts(r("ll", k, 4, 2), r("lp", 128 + 64 * k, 192 + 64 * k, 32), -256.0 * rank, A.add)
+    iota(r("d16", 64, 128), [[0, 4], [1, 16]], 0)
+    ts(r("d16", 0, 64), r("d16", 64, 128), P16, A.is_equal)
+    const(r("kk", 264, 268), 0.0)
+    iota(r("pat", 8, 40), [[1, 32]], 0)
+    for h in range(2):
+        act(r("ft", 64 + 32 * h, 96 + 32 * h), r("pat", 8, 40), F.Sign)
+    ts(r("gi", 0, 4), r("kk", 218, 228, 3), 2048.0 - 256.0 * (rank + 1), A.add)
+    ts(r("fi", 10, 14), r("gi", 0, 4), 5, A.arith_shift_right, 63, A.bitwise_and)
+    ts(r("gi", 4, 8), r("gi", 0, 4), 8, A.arith_shift_right, 7, A.bitwise_and)
+    copy("v", r("c01", 0, 4), r("fi", 10, 14))
+    copy("v", r("c01", 4, 8), r("gi", 4, 8))
+    copy("v", r("fr", 0, 64), r("ka", 0, 64))
+    ts(r("fr", 64, 128), r("fr", 0, 64), 31, A.bitwise_and)
+    ts(r("mk", 0, 64), r("fr", 64, 128), P32, A.is_equal)
+    ts(r("fr", 128, 192), r("fr", 0, 64), 2048.0 - 256.0 * (rank + 1), A.add)
+    ts(r("fr", 192, 256), r("fr", 128, 192), 3, A.arith_shift_right, 224, A.bitwise_and)
+    copy("v", r("flp", 0, 2), r("fa", 0, 2))
 
     for h in range(2):
-        quant(r("qb", 128 * h, 128 * h + 128), r("sb", 128 * h, 128 * h + 128), r("bb_t", 512 * h, 512 * h + 512))
+        quant("qb", "sb", 128 * h, 128 * h + 128, r("bb_t", 512 * h, 512 * h + 512))
     for i in range(4):
-        act(r("vb", i, 512, 4), r("iot", 0, 128), F.Identity, bias=col("v4", i), scale=0.0)
-    quant(r("qv", 0, 128), r("sv", 0, 128), r("vb", 0, 512))
-    mm(r("pf", 0, 256), r("qv", 0, 128), r("sv", 0, 128), r("qb", 0, 256), r("sb", 0, 256))
+        ts(r("vb", i, 512, 4), r("zb", 0, 128), col("v4", i), A.add, q="s")
+    quant("qv", "sv", 0, 128, r("vb", 0, 512))
+    mm("pf", 0, QV, QB)
     copy("s", r("fn", 0, 256), r("pf", 0, 256))
-    ts(col("cf", 27), col("cf", 26), col("cf", 2), A.add)
-    ts(r("frt", 0, 4), r("iot", 0, 64, 16), col("cf", 27), A.add)
-    act(r("d1z", 0, 64), (r("fn", 0, 256), r("frt", 0, 4)), F.Copy, scale=-1.0)
-    lin(col("cf", 47), col("cf", 43), 1.0, col("cf", 26))
-    ts(r("frt", 4, 8), r("iot", 0, 64, 16), col("cf", 47), A.add)
-    act(r("d1r", 6, 448, 7), (r("fn", 0, 256), r("frt", 4, 8)), F.Copy, scale=-1.0)
-    copy("s", r("d1r", 0, 448, 7), (r("ea", 0, 256), r("of", 0, 4)))
-    copy("v", r("d1r", 1, 448, 7), (r("ea", 0, 256), r("of", 4, 8)))
-    const(r("d0r", 0, 448), 1.0)
-    act(r("d0r", 0, 448, 7), r("iot", 0, 64), F.Copy, scale=0.0)
-    const(r("cf", 32, 35), 0.0)
-    const(r("cf", 32, 33, 1, 96, 128), -TINY)
-    const(r("cf", 33, 34, 1, 64, 128), -TINY)
-    const(r("cf", 34, 35, 1, 64, 128), -TINY)
-    const(r("cf", 34, 35, 1, 32, 64), -TINY)
-    ts(r("jj", 0, 64), r("jr", 0, 64), col("jo", 0), A.is_lt, -TINY, A.mult)
-    ts(r("jj", 64, 128), r("jr", 0, 64), col("jo", 1), A.is_lt, TINY, A.mult)
-    lin(r("kk", 18, 22), r("iot", 0, 4), 0.25, 0.0)
-    lin(r("kk", 0, 4), r("iot", 0, 4), 0.25, 16.0)
+    copy("s", r("ft", 0, 64), (r("fn", 0, 256), r("frt", 0, 4)))
+    tr(r("fn", 0, 64), r("ft", 0, 64))
+    const(r("fz", 0, 66), 0.0)
+    ts(r("fz", 32, 66, 33), r("fn", 0, 64, 32), -1.0, A.mult)
+    ts(r("cf", 36, 39), r("iot", 64, 256, 64), B64, A.add, 256.0, A.is_ge)
+    ts(r("cf", 32, 35), r("cf", 36, 39), -TINY, A.mult)
+    ts(r("kk", 18, 22), r("iot", 0, 4), 0.25, A.mult)
+    ts(r("kk", 0, 4), r("iot", 0, 4), 0.25, A.mult, 16.0, A.add)
     const(r("c4", 0, 128), 1.0)
     const(r("c4", 2, 128, 4), C05)
     const(r("c4", 3, 128, 4), 0.0)
     const(r("wm", 0, 96), 1.0)
     const(r("wm", 0, 96, 8), 0.0)
-    const(r("fr_", 0, 32), 7.0)
-    for c, u in ((0, 0), (1, 5), (16, 4), (17, 0)):
-        lin(r("fr_", c, c + 8 - c % 2, 2), r("iot", 0, 4), 8.0, 8.0 * u + 7)
-    for c, u in ((8, 9), (9, 11), (24, 10), (25, 9)):
-        const(col("fr_", c), 8.0 * u + 7)
+    iota(r("fr_", 0, 8), [[8, 4], [40, 2]], 7)
+    iota(r("fr_", 8, 16), [[0, 4], [16, 2]], 79)
+    iota(r("fr_", 16, 24), [[8, 4], [-32, 2]], 39)
+    iota(r("fr_", 24, 32), [[0, 4], [-8, 2]], 87)
     tr(r("fr_", 32, 64), r("fr_", 0, 32))
     copy("v", r("fo", 0, 2), r("fr_", 32, 34))
-    ts(r("dvo", 0, 6), r("iot", 0, 192, 32), col("cf", 2), A.add)
-    lin(col("cf", 4), col("cf", 2), -1.0, col("jo", 0))
-    for h in range(2):
-        lin(r("dv", 96 + 16 * h, 112 + 16 * h), r("iot", 32 * h, 32 * h + 16), 1.0, col("cf", 4))
-    copy("s", r("ol", 0, 256), r("iot", 0, 256))
+    ts(r("dv", 96, 128), (IOT, r("jo16", 0, 2)), UP, A.add, q="s")
+    iota(r("ol", 0, 256), [[1, 256]], int(UP))
+    iota(r("od", 0, 96), [[1, 96]], int(UP) + OWN0)
+    iota(r("ndv", 0, 224), [[1, 224]], int(UP) + LAND0)
+    iota(r("ndv", 224, 448), [[1, 224]], int(UP) + LAND0 + 224)
+    iota(r("wn", 0, 256), [[0, 256]], 0)
+    iota(r("xt", 128, 512), [[0, 384]], 0)
+    iota(r("pat", 40, 56), [[32, 8], [0, 2]], 0)
+    ts(r("d8", 0, 16), r("pat", 40, 56), P32, A.add)
 
     ts(r("fi", 4, 6), r("fi", 0, 2), 8, A.arith_shift_right)
-    copy("v", r("fa", 10, 12), r("fi", 4, 6))
-    ts(r("fa", 12, 14), r("fa", 10, 12), -256.0, A.mult, 0.5, A.add)
+    ts(r("fa", 12, 14), r("fi", 4, 6), -256.0, A.mult, 0.5, A.add)
     for h in range(2):
         act(junk(3 + h), FR, F.Sign, bias=col("fa", 12 + h), acc=col("ac", 8 + h))
     ts(r("fi", 6, 8), r("fi", 4, 6), float(7 - rank), A.add)
     ts(r("fi", 8, 10), r("fi", 6, 8), 7, A.bitwise_and)
-    ts(r("fa", 14, 16), r("fi", 8, 10), float(LC), A.mult, float(FAR0), A.add)
-    for k in range(2):
-        lin(r("nl", k, 192, 3), r("nbf", k, 192, 3), 1.0, -256.0 * rank)
+    ts(r("fa", 14, 16), r("fi", 8, 10), float(LC), A.mult, UP + FAR0, A.add)
     tt(r("ac", 10, 12), r("ac", 8, 10), r("ac", 4, 6), A.subtract)
-    ts(r("ac", 12, 14), r("ac", 10, 12), 0.5, A.mult)
-    tt(r("ac", 14, 16), r("ac", 12, 14), r("fa", 14, 16), A.add)
     for h in range(2):
-        times(r("sp", 128 + 32 * h, 160 + 32 * h), CONE, col("ac", 14 + h))
-    tr(r("ex", 512, 576), r("sp", 128, 192))
-    ts(r("ci", 5, 6), r("ci", 2, 3), 3.0, A.mult, 2.0, A.add)
-    ts(r("ci", 6, 7), r("ci", 5, 6), 15, A.bitwise_and)
-    copy("v", col("cf", 41), r("ci", 6, 7))
-    lin(col("cf", 48), col("cf", 41), 7.0, 6.0)
-    ts(r("frt", 8, 12), r("iot", 0, 448, 112), col("cf", 48), A.add)
-    ts(r("pm", 0, 4), r("iot", 0, 64, 16), col("cf", 41), A.add)
-    copy("s", r("nl", 2, 192, 3), (FL, r("pm", 0, 4)))
+        ts(col("ac", 14 + h), col("ac", 10 + h), 0.5, A.mult, col("fa", 14 + h), A.add)
+        ts(r("sp", 128 + 32 * h, 160 + 32 * h), CONE, col("ac", 14 + h), A.mult)
+    tr(FL, r("sp", 128, 192))
+    ts(r("fl2", 0, 2), r("iot", 0, 64, 32), P32, A.add)
+    copy("s", r("dv", 64, 96), (FL, r("fl2", 0, 2)))
 
-    dma([("y", r("rl", 21, 32), r("iot", 0, 11))])
+    dma([("y", r("rl", 21, 32), r("cc", 0, 11))])
     tr(r("rl2", 0, 32), r("rl", 0, 32))
     o = 16 * (rank % 2)
     for i in (32, 48):
@@ -536,65 +486,38 @@ def rank_program(g, core, T, topo):
     for a in range(4):
         copy("v", blk("rep", 0, 21, a), blk("rl2", 64, 85, rank // 2))
     pick(r("slc", 0, 336), r("sls", 0, 336), r("qx", 0, 256), r("sx", 0, 256), r("rep", 0, 21))
-    for s, l, arr in (("slc", "g0", "ac0"), ("sls", "h0", "as0")):
-        send_each([(d, r(s, LC * i, LC * i + LC), r(l, *slot(d, LC, FAR0))) for i, d in enumerate(peers)], arr, [r(l, FAR0, NEW0)])
-    w0 = 32 * ((rank + 1) % 8)
-    w1 = w0 or 128
-    iota(r("ndv", w1, 256), [[1, 256 - w1]], NEW0 + w1 - w0, 0)
-    iota(r("ndv", 0, w1), [[1, w1]], NEW0 + (256 - w0) % 256, 0)
-    const(r("np0", 0, 256), 0.0)
-    dma([("y", r("np0", 256 * i, 256 * i + 256), r("np0", 0, 256)) for i in range(1, 8)])
-    iota(r("od", 0, 96), [[1, 96]], P, 0)
-
-    copy("v", r("db", 0, 192), (r("nl", 0, 192), r("dbt", 0, 12)))
-    copy("s", r("dv", 0, 96), (r("db", 0, 192), r("dvo", 0, 6)))
-    dma([("y", r("junk", 0, 256), r("ea", 0, 256))])
-    const(r("ea", NEW0 + 224, NEW0 + 256), 0.0)
-    fill(r("xt", 0, 512), 0.0)
+    for s, l, arr in (("slc", "gq", "ac0"), ("sls", "gs", "as0")):
+        send_each([(d, r(s, LC * i, LC * i + LC), r(l, *slot(d, LC, FAR0))) for i, d in enumerate(peers)], arr, r(l, FAR0, LAND0))
     for b in range(4):
-        quant(r("qa", 128 * b, 128 * b + 128), r("sa", 128 * b, 128 * b + 128), r("at", 512 * b, 512 * b + 512))
-    quant(r("qw", 0, 128), r("sw", 0, 128), r("wt", 0, 512))
-    mm(r("py", 0, 256), r("qw", 0, 128), r("sw", 0, 128), r("qx", 0, 256), r("sx", 0, 256))
-    copy("s", r("yw", 0, 256), r("py", 0, 256))
-    for k in range(3):
-        tr(r("dt_", 64 * k, 64 * k + 64), r("nbf", k, 192, 3))
-    copy("v", r("dnb", 0, 12), r("dt_", 0, 192, 16))
-
-    def places(t):
-        copy("v", r("ndl", 0, 2), r("nd_", 16 * t + 8, 16 * t + 10))
-        scatter(r("ol", 0, 256), r("ndl", 0, 2), r("od", 32 * t, 32 * t + 32))
+        quant("qa", "sa", 128 * b, 128 * b + 128, r("at", 512 * b, 512 * b + 512))
+    quant("qw", "sw", 0, 128, r("wt", 0, 512))
+    mm("py", 0, QW, QX)
+    copy("s", r("yt", 0, 256), r("py", 0, 256))
 
     for t in range(R):
-        gq, gs, W, oz = "g%d" % t, "h%d" % t, NEW0 + 256 * t, 12 * t
-        if t:
-            win = r("er", 8 + 8 * t, 15 + 8 * t)
-            copy("v", r("es", 0, 128), (win, r("spo", 0, 8)))
-            copy("s", r("es", 128, 224), (win, r("spo", 8, 14)))
-            tr(r("ea", W - 256, W - 128), r("es", 0, 128))
-            tr(r("ea", W - 128, W - 32), r("es", 128, 224))
-        else:
-            mm(r("px", 0, 336), r("qu", 0, 128), r("su", 0, 128), r(gq, FAR0, NEW0), r(gs, FAR0, NEW0))
-            copy("s", r("ea", FAR0, NEW0), r("px", 0, 336))
-        if t:
-            copy("s", r("zs", 0, 64), (r("junk", 0, W), r("of", oz, oz + 4)))
-            tt(r("zs", 64, 128), (r("junk", 0, W), r("of", oz + 4, oz + 8)), r("zs", 0, 64), A.add)
-            tt(r("zs", 128, 192), (r("ea", 0, W - 32), r("of", oz + 8, oz + 12)), r("zs", 64, 128), A.add)
-            tt(r("zs", 192, 256), r("zs", 128, 192), r("d1z", 0, 64), A.add)
-            act(r("z", 0, 64), r("zs", 192, 256), F.Abs)
-        else:
-            scan(r("zr", 0, 448), r("d0r", 0, 448), r("d1r", 0, 448), 0.0, A.mult, A.add)
-            act(r("z", 0, 64), (r("zr", 0, 448), r("frt", 8, 12)), F.Abs)
-        exchange("z")
-        tr(r("zt", 0, 64), r("z", 0, 64))
-        ts(r("dd", 0, 64), r("z", 0, 64), col("zt", 0), A.subtract)
-        act(r("dd", 64, 128), r("z", 0, 64), F.Identity, bias=col("zt", 32), scale=-1.0)
+        W, at, po = LAND0 + 224 * t, OWN0 + 32 * t, 16 * t
+        ndl = r("po", po + 8, po + 10)
+        copy("s", r("dv", 0, 64), (r("ol", 0, 256), r("dl", 0, 4)))
+        tt(r("lg", 0, 64), (r("et", 0, 256), r("ll", 0, 4)), r("d16", 0, 64), A.mult)
+        scan(r("dz", 2, 130, 2), r("ft", 64, 128), r("lg", 0, 64), 0.0, A.mult, A.add)
+        win = (r("er", 48 + 8 * t, 55 + 8 * t), r("c01", 4, 8)) if t else (r("er", 0, 56), r("c01", 0, 4))
+        tt(r("tg", 0, 64), win, r("mk", 64 * (t % 2), 64 * (t % 2) + 64), A.mult)
         for h in range(2):
-            o = 256 * h
-            tt(r("mm_", o, o + 64), r("dd", 64 * h, 64 * h + 64), r("jj", 64 * h, 64 * h + 64), A.is_lt if h else A.is_gt)
+            tr(r("dz", 32 + 64 * h, 64 + 64 * h), r("tg", 32 * h, 32 * h + 32))
+        for h in range(2):
+            scan(r("zo", 40 * h, 40 * h + 33), r("dz", 32 + 64 * h, 65 + 64 * h), r("fz", 33 * h, 33 * h + 33), col("ok", h) if t else 0.0, A.add, A.add)
+            act(r("sp", 192 + 32 * h, 224 + 32 * h), CONE, F.Abs, scale=col("zo", 40 * h + 32))
+        tr(r("z", 0, 64), r("sp", 192, 256))
+        exchange("z")
+        for h in range(2):
+            o, zt = 256 * h, col("sp", 192 + 32 * h)
+            ts(r("dd", 64 * h, 64 * h + 64), r("z", 0, 64), -1.0, A.mult, zt, A.add, q="s")
+            tt(r("mm_", o, o + 64), r("dd", 64 * h, 64 * h + 64), r("jj", 64 * h, 64 * h + 64), A.is_lt)
             for d in range(1, 4):
-                ts(r("mm_", o + 64 * d, o + 64 * d + 64), r("z", 64 * d, 64 * d + 64), col("zt", 32 * h), A.subtract, col("cf", 31 + d), A.is_gt)
+                ts(r("mm_", o + 64 * d, o + 64 * d + 64), r("z", 64 * d, 64 * d + 64), zt, A.subtract, col("cf", 31 + d), A.is_gt)
             scan(r("cx", 128 * h, 128 * h + 128), r("mm_", o, o + 128), r("mm_", o + 128, o + 256), 0.0, A.add, A.add)
-        const(r("wn", 0, 256), 0.0)
+        if t:
+            const(r("wn", 64, 192), 0.0)
         for h in range(2):
             ts(r("so", h, 8, 2), r("kk", 0, 4), col("cx", 128 * h + 127), A.add, 4.0, A.mult)
         scatter(r("wn", 0, 1088), r("so", 0, 8), r("dv", 0, 128))
@@ -610,75 +533,53 @@ def rank_program(g, core, T, topo):
         copy("s", r("wx", 2, 96, 4, 0, 64), r("wt_", 0, 384, 16, 64, 128))
         copy("s", r("wx", 2, 96, 4, 64, 128), r("wt_", 0, 384, 16, 0, 64))
         scan(r("sm", 0, 96), r("wm", 0, 96), r("wx", 0, 96), 0.0, A.mult, A.add)
-        copy("v", r("po", 0, 16), (r("sm", 0, 96), r("fo", 0, 1)))
-        nd, na, n0 = r("sel", 16 * t + 8, 16 * t + 10), "nda%d" % t, 16 * t + 8
-        act(r("nd_", 16 * t, 16 * t + 16), (r("sm", 0, 96), r("fo", 0, 1)), F.Copy)
+        ts(r("po", po, po + 16), (r("sm", 0, 96), r("fo", 0, 1)), -UP, A.add)
+        ts(r("nd_", po, po + 16), (r("sm", 0, 96), r("fo", 0, 1)), -UP, A.add, q="s")
         if t < 2:
-            act(r("sel", 16 * t, 16 * t + 16), (r("sm", 0, 96), r("fo", 0, 1)), F.Copy, bias=256.0 * rank)
-            send_all(nd, lambda d: r(na, 2 * rank, 2 * rank + 2), "an%d" % t, [r(na, 2 * s, 2 * s + 2) for s in peers])
-            dma([("y", r(na, 2 * rank, 2 * rank + 2), nd)])
+            ts(r("sel", 2 * t, 2 * t + 2), ndl, 256.0 * rank, A.add)
+            send_all(r("sel", 2 * t, 2 * t + 2), "an", 16 * t, "an%d" % t)
         nq, ns = "nq%d" % t, "ns%d" % t
-        pick(r(nq, 0, 128), r(ns, 0, 128), r(gq, 0, W), r(gs, 0, W), r("po", 0, 8))
+        pick(r(nq, 0, 128), r(ns, 0, 128), r("gq", 0, W), r("gs", 0, W), r("po", po, po + 8))
         for b in range(4):
-            mm(r("ps", 512 * b, 512 * b + 128), r("qa", 128 * b, 128 * b + 128), r("sa", 128 * b, 128 * b + 128), r(nq, 0, 128), r(ns, 0, 128))
+            mm("ps", 512 * b, ("qa", "sa", 128 * b, 128 * b + 128), (nq, ns, 0, 128))
         for c in range(2):
-            ts(r("bo", c, 8, 2), r("kk", 18, 22), col("nd_", n0 + c), A.add, 4.0, A.mult)
+            ts(r("bo", c, 8, 2), r("kk", 18, 22), col("nd_", po + 8 + c), A.add, 4.0, A.mult)
         copy("s", r("bbs", 0, 128), (r("bb_t", 0, 1024), r("bo", 0, 8)))
-        if t == 2:
-            places(t)
+        scatter(r("ol", 0, 256), ndl, r("od", 32 * t, 32 * t + 32))
         for b in range(4):
             scan(r("sc4", 128 * b, 128 * b + 128), r("ps", 512 * b, 512 * b + 128), r("c4", 0, 128), 0.0, A.add, A.mult)
         for b in range(4):
             tt(r("xt", b, 128, 4), r("sc4", 128 * b + 2, 128 * b + 128, 4), r("bbs", 32 * b, 32 * b + 32), A.add)
-        if t == 2:
-            copy("s", r("og", 0, 256), (r("ol", 0, 256), r("d8", 0, 16)))
-        o0 = P + 32 * t
+        quant("gq", "gs", at, at + 128, r("xt", 0, 512))
+        new = ("gq", "gs", at, at + 128)
         if t < 2:
-            nq, ns, at = "g%d" % (t + 1), "h%d" % (t + 1), W + 224
-            quant(r(nq, at, at + 128), r(ns, at, at + 128), r("xt", 0, 512))
-            for i, bank in enumerate(("pe", "pf")):
-                mm(r(bank, 0, 128), r(nq, at, at + 128), r(ns, at, at + 128), r("qu", 0, 128), r("su", 0, 128))
-                for a in (2 * i, 2 * i + 1):
-                    copy("vs"[i], blk("ep", 4 + 4 * t, 5 + 4 * t, a), blk(bank, 0, 1, 0))
-            send_all(col("ep", 4 + 4 * t), lambda d: r("er", *slot(d, 1, 16 + 8 * t)), "ae%d" % t, [r("er", 16 + 8 * t, 23 + 8 * t)])
-            for n, arr in ((nq, "ac%d" % (t + 1)), (ns, "as%d" % (t + 1))):
-                send_all(r(n, at, at + 32), lambda d: r(n, *slot(d, 32, W)), arr, [r(n, W, at)], 1.5)
-            mm(r("px", 0, 128), r("qu", 0, 128), r("su", 0, 128), r(nq, at, at + 128), r(ns, at, at + 128))
-            copy("s", r("junk", at, at + 32), r("px", 0, 32))
-            dma([("y", r("ow", o0, o0 + 32), r(nq, at, at + 32)), ("y", r("os_", o0, o0 + 32), r(ns, at, at + 32))])
-        else:
-            nq, ns, at = "ow", "os_", o0
-            quant(r(nq, at, at + 128), r(ns, at, at + 128), r("xt", 0, 512))
-        mm(r("py", 0, 128), r("qw", 0, 128), r("sw", 0, 128), r(nq, at, at + 128), r(ns, at, at + 128))
-        copy("s", r("yw", o0, o0 + 32), r("py", 0, 32))
-        if t == 0:
-            dma([("y", r("g1", 0, NEW0), r("g0", 0, NEW0)), ("y", r("h1", 0, NEW0), r("h0", 0, NEW0))])
-            dma([("y", r("g2", 0, NEW0), r("g0", 0, NEW0)), ("y", r("h2", 0, NEW0), r("h0", 0, NEW0))])
-            lin(r("ndv", 256, 512), r("ndv", 0, 256), 1.0, 256.0)
-        dma([("y", T.nd[t:t + 1, 16 * c:16 * c + 16], r("nd_", n0 + c, n0 + c + 1, 1, 0, 16)) for c in range(2)])
+            mm("px", 0, QU, new)
+            tr(r("ec", 32 * t, 32 * t + 32), r("px", 0, 32))
+            send_all(col("ec", 32 * t), "er", 56 + 8 * t, "ae%d" % t)
+            for n, arr in (("gq", "ac%d" % (t + 1)), ("gs", "as%d" % (t + 1))):
+                send_all(r(n, at, at + 32), n, W, arr)
+            copy("s", r("nw", 0, 32), r("px", 0, 32))
+            scatter(r("et", 0, 256), ndl, r("nw", 0, 32))
+        mm("py", 0, QW, new)
+        copy("s", r("nw", 32, 64), r("py", 0, 32))
+        scatter(r("yt", 0, 256), ndl, r("nw", 32, 64))
+        dma([("y", T.nd[t:t + 1, 16 * c:16 * c + 16], r("nd_", po + 8 + c, po + 9 + c, 1, 0, 16)) for c in range(2)])
         if t < 2:
-            places(t)
-        if t == 1:
-            dma([("y", r("g2", NEW0, NEW0 + 256), r("g1", NEW0, NEW0 + 256)), ("y", r("h2", NEW0, NEW0 + 256), r("h1", NEW0, NEW0 + 256))])
-            ts(r("frf", 0, 16), r("iot", 0, 256, 16), 0.0, A.add)
-            ts(r("frf", 0, 16), r("frf", 0, 16), 224, A.bitwise_and)
-            ts(r("d8", 0, 16), r("frf", 0, 16), col("cf", 1), A.add)
-        if t < 2:
-            npn = r("np0", 0, 2048)
-            copy("v", r("nai", 0, 16), r(na, 0, 16))
-            scatter(npn, r("nai", 0, 16), r("ndv", 256 * t, 256 * t + 256))
-            tt(r("db", 0, 192), (npn, r("dnb", 0, 12)), r("db", 0, 192), A.max)
-            tr(r("dt_", 0, 192), r("db", 0, 192))
-            copy("v", r("of", 12 * t + 12, 12 * t + 24), r("dt_", 0, 192, 16))
-            copy("s", r("dv", 0, 96), (r("db", 0, 192), r("dvo", 0, 6)))
+            scatter(IOT, r("an", 16 * t, 16 * t + 14), r("ndv", 224 * t, 224 * t + 224))
+            tt(r("rel", 0, 64), (IOT, r("far16", 0, 4)), r("fr", 192, 256), A.subtract)
+            m = 64 * ((t + 1) % 2)
+            ts(r("mk", m, m + 64), r("rel", 0, 64), UP + W, A.subtract, P32, A.is_equal)
+            tr(r("rel", 64, 128), r("rel", 0, 64))
+            for h in range(2):
+                ts(col("ok", h), col("rel", 64 + 32 * h), UP + W, A.is_lt, col("zo", 40 * h + 31), A.mult)
+            tt(r("dv", 64, 96), (IOT, r("flp", 0, 2)), r("dv", 64, 96), A.max)
 
+    copy("s", r("og", 0, 256), (r("ol", 0, 256), r("d8", 0, 16)))
     tr(r("ogt", 0, 256), r("og", 0, 256))
-    copy("v", r("oo", 0, 16), r("ogt", 0, 256, 16))
-    pick(r("occ", 0, 256), r("ocs", 0, 256), r("ow", 0, 352), r("os_", 0, 352), r("oo", 0, 16))
+    ts(r("oo", 0, 16), r("ogt", 0, 256, 16), -UP, A.add)
+    pick(r("occ", 0, 256), r("ocs", 0, 256), r("gq", 0, FAR0), r("gs", 0, FAR0), r("oo", 0, 16))
     dma([("y", T.oc[:], r("occ", 0, 256))])
     dma([("y", T.osc[4 * k:4 * k + 4, :], r("ocs", 0, 256, 1, 32 * k, 32 * k + 4)) for k in range(4)])
-    copy("v", r("yt", 0, 128), (r("yw", 0, 352), r("oo", 0, 8)))
-    copy("s", r("yt", 128, 256), (r("yw", 0, 352), r("oo", 8, 16)))
     dma([("s", T.y[:], r("yt", 0, 256))])
     flush()
     for sem, c in cnt.items():

@@ -9,21 +9,21 @@ UP = 4096.0
 C05 = 13421773 * 2.0 ** -28
 TINY = 2.0 ** -110
 ORDER = """
-22 7 17s 21 8y 5 12y 4 2 15 9y 3s 23 28 11 1 27 13y 6s 10 16 0 19s 14 29 18 30 20 35 87s 31 128 52v 24 39 32 176v 36 25 34 33 71 178 38 46 40
-37v 217s 47 41 129 188 114 48 113 112v 43s 151 44s 49 42s 115v 45s 50 116 189 51 26 169 72s 165 153 190 55 130 154 58 56 195 59 111 57s 138 53v
-140 61s 124 126 60 63 117 199 54 125 64 67 66 65 141s 70v 118 69s 127s 83s 182 73 68 119 76s 75v 74s 77v 84 62s 120 142 152 78 79 187 89s 202
-167 139v 81 194 179 168v 80 236 206 155 82 86v 237 159 157 207 85s 148 170v 143 131 203 88 96s 181 166 198 93 97 90s 91v 92s 144 180s 98s 134
-94s 95v 150 145 204 160 100 105 102 104 101s 99s 171 103 109 107 172 110 106 108 205 215 147 146 122 149 135 132 162 200 173 240 209 208 196 234
-174 161 232 185 241 239 136 121 175 177s 210s 238 242 212s 243 244 245 247 235 123 246 248 211s 213s 218 249 220 250s 219 253 137 251 252s 221
-262 191 256 214 254s 222 223 255 224 225 133 263 227 258 266 264 259 260 257 265 226 193 216 230 186 183 261 267 228 268 269 164 270 201 271 273
-274 272 184v 163 282s 275 283 279v 277 276 281 280 284 285v 278 231 192 156 286 158 287 233 293 289 290 288 197 325 324s 229 292 299 298 296 294
-300 295 304 297 362 302 303 305 308 306 307 291 309 310 301 311 321 333 312 326 313 319 317 315 320 327 334 329 328 335 330 332 314 336 331 338
-337 341 318 339 342 340 343 347 346 356v 345 344 350 348s 357 349 352 358 322 316 351 354 360 353 359 355 361 363 364 365 367 369 366 368 377s
-379v 370s 376v 378 371 380 375 373s 374v 457 372v 381 382 383 384 388 387 385 394 393 389 390 395 392 397 391 419s 398 400 399 401 404 402 403
-405 396 406 416 407 386 414 408 428 412 410 421 415 422 429 424 423 430 409 431 426 425 432 433 434 413 436 427 435 437 420s 438 442 441 445 440v
-439s 451v 443s 446 444 447 453 452 448 454 449 455 450 456 458 459 460 411 462 464 461 463 471 465 472 469 473 467v 470s 468 474 466 475 323 476
-477 478v 480 479 501 488 417 502s 485 484 486 481 418 503 482 492 483 489 490 487 491 504 496 494 493 495 505 497 506 498 499 507 500 508 513y
-509s 511 510 512
+3 5y 10 11 2s 0 1 18 12 17 4 181v 192 50 46 49 20 9s 19 6y 182v 21 45 25 7 47 132 189 36 13 183 22 26s 185 8 133 29 51 134 14 119 23 30 117 116v
+142 24 52s 38 27 31 39 41 40 118v 144 188s 143 186s 35s 42 32s 120 37 54s 155 115 53s 28 145 135 43 55 157 121 130 172 173v 128 33 174v 34s 131 56
+148s 160 67s 147 122 62s 158 59s 44 48 203 123 146 149 138 66 57 58 124 175v 60 170 63 68s 93s 61s 171 71 162 72 70s 64 150 176 139 74 89 65 187s
+177 88 156 15 75 81s 164 80 78v 76 77s 161 83s 79 84 82v 16 73 178 207 151 165 85 69 129v 195 86 90 179v 159 201 166 153 91s 95 154 92 208 87 180
+94 190 245 211 125 106 99 105v 194 104s 103v 100s 97v 98s 102 101 96 209 163 246 205 107 108 111 110 196 247 109 114 197 136 184s 113 249 248 112
+141 210 212 252 250 126 213 204 253 215 251 140 137 271v 218s 216 265 254 237 219s 217 266 262 261s 259 260 263s 256 220 264 272 258 257s 275 255s
+127 223 221 274 269 224s 225v 193 273 268 222 200 226 267 276 152 228 230 229 227 244 270 198 278 232 277 231 279 235 233 202 283 280 282 281 199
+240 284s 289 292 285 288 294v 286v 293 291s 290v 287 239 236 295 238 296 297 298 332v 377 191v 167 301 333s 234 300 307 169 306 309 303 302 308
+304 305 311 299 344 310 312 313 315 314 316 317 168 318 334 241 319 335s 242 320 336 214 321 327 337 323 325 341 339s 340 328 338 342 345 346 322
+347 343 348 349 350 352 324 351 353v 326 365 354 371 355 358 364v 363s 361s 372 356 360 357 359s 366 362 243 374 368 373 367 369 375 329 370 376
+378 379 380 383 381 384 382 395 389v 391v 393 387v 392s 394 388 390s 386 385 330 396 206 399 398 397 401 402 408 407 404 405 409 403 406 433 412
+413 411 434s 414 400 417 416 415 418 419 435 410 420 430 436 421 437 428 422 438 426 424 429 442s 445v 440s 478 446 439 447 331 441 423 448 450 449
+427 453 451 454 452v 425 455 466 443 472 459v 461 463 460 464 462s 465 473 457 458s 467 456s 476 475 469 470 468 474 444 471 477 479 480 481 482
+484 483 485 496v 486s 489 490 492v 494 493s 495v 487 491s 488v 431v 497 522 498 499 523 500 501 506 507 509 504 432 502 508 505 503 524 512 510
+529 513 511 516 525 517 514 515 526 530 518 531 519 527 528 532 520 533 521 534s 536 539 535s 538s 537s
 """
 CODE, U8, BF, F32, I32, U16 = "float8_e4m3fn_x4", "uint8", "bfloat16", "float32", "int32", "uint16"
 
@@ -34,13 +34,12 @@ def _sbuf(dtype, **cols):
 
 SCRATCH = {"pe": ("psum", [128, 512], F32), "pf": ("psum", [128, 512], F32), "ps": ("psum", [128, 2048], F32), "py": ("psum", [128, 512], F32),
            "px": ("psum", [128, 512], F32)}
-SCRATCH.update(_sbuf(F32, nbf=192, iot=2048, jf=256, cf=64, jo=8, ka=256, kat=64, junk=2304, cq=768, cz=384, ac=32, fa=28, sp=256, ex=576, cc=128,
-                     lo=16, fn=256, z=256, dd=128, jj=128, c4=288, wn=1088, wt_=576, dv=128, kk=288, nd_=48, bbs=128, sc4=512, ndv=448, od=96,
-                     og=256, ogt=256, yt=256, ept=256, ep=8, ec=64, er=72, rl=32, rl2=96, lst=4, et=256, ol=256, mk=128, tg=64, lg=64, dz=132,
-                     fz=72, zo=80, ok=4, rel=128, jr=64, ft=128, lp=256, d16=128, nw=64, pat=64))
-SCRATCH.update(_sbuf(I32, nb32=48, ci=16, fi=16, gi=16, fr=256))
-SCRATCH.update(_sbuf(U16, nbt=12, far16=16, rep=24, so=8, po=48, sel=4, an=32, bo=8, frt=4, cl=8, dl=4, ll=4, c01=8, flp=2, fl2=2, jo16=2, fo=2,
-                     d8=16, oo=16))
+SCRATCH.update(_sbuf(F32, nbf=192, iot=2048, jf=256, cf=64, jo=8, ka=256, kat=64, junk=2304, cq=768, cz=384, ac=32, fa=28, sp=256, ex=576, cc=160,
+                     lo=24, fn=256, z=256, dd=128, jj=128, c4=288, wn=1088, wt_=576, dv=128, kk=288, nd_=48, bbs=128, sc4=512, an=16, od=96,
+                     og=256, ogt=256, yt=256, ept=256, ep=8, ec=64, er=96, rl2=96, et=256, ol=256, mk=128, tg=64, lg=64, dz=132,
+                     fz=72, zo=80, ok=8, rel=192, jr=64, ft=128, lp=256, d16=128, nw=64, pat=64))
+SCRATCH.update(_sbuf(I32, nb32=96, ci=16, fi=16, gi=24, fr=256))
+SCRATCH.update(_sbuf(U16, nbt=12, far16=16, rep=24, so=8, po=48, bo=8, frt=4, cl=8, dl=4, ll=4, c01=8, fl2=2, jo16=2, fo=2, d8=16, oo=16))
 SCRATCH.update(_sbuf(BF, xb=1024, bb_t=1024, at=2048, wt=512, u4=4, v4=4, ub=512, vb=512, mm_=512, xt=512, cx=256, zb=128))
 for _c, _s, _n in (("qx", "sx", 256), ("qb", "sb", 256), ("qu", "su", 128), ("qv", "sv", 128), ("qa", "sa", 512), ("qw", "sw", 128), ("slc", "sls", 336),
                    ("gq", "gs", 1232), ("nq0", "ns0", 128), ("nq1", "ns1", 128), ("nq2", "ns2", 128), ("occ", "ocs", 256)):
@@ -88,7 +87,7 @@ def rank_program(g, core, T, topo):
             s = span(x)
             bank = SCRATCH[x[0]][0] == "psum"
             for y, t, w2, i, q2 in log.get(x[0], []):
-                if (w or w2 or (bank and q2 != q)) and s[0] < t[1] and t[0] < s[1] and s[2] < t[3] and t[2] < s[3] and clash(x, y):
+                if (w or w2 or bank) and s[0] < t[1] and t[0] < s[1] and s[2] < t[3] and t[2] < s[3] and clash(x, y):
                     deps.add(i)
         return deps
 
@@ -158,7 +157,7 @@ def rank_program(g, core, T, topo):
 
     def copy(q, out, in_):
         i, rd = src(in_)
-        flex = all(SCRATCH[k][2] in (F32, BF) for k in (out[0], rd[0][0])) and SCRATCH[rd[0][0]][0] == "sbuf"
+        flex = all(SCRATCH[k][2] in (F32, BF) for k in (out[0], rd[0][0]))
         put(q, lambda e: g.vector.tensor_copy(ap(out), i) if e == "v" else g.scalar.activation(ap(out), i, F.Copy), rd, [out], alt="vs" if flex else "")
 
     def scatter(win, off, in_):
@@ -182,6 +181,11 @@ def rank_program(g, core, T, topo):
         mul, add = (1.0, a) if op0 == A.add else (a, 0.0 if op1 is None else b)
         put(q, lambda e: g.vector.tensor_scalar(ap(out), i, a, b, op0, *([] if op1 is None else [op1])) if e == "v" else
             g.scalar.activation(ap(out), i, F.Copy if isinstance(add, float) else F.Identity, bias=add, scale=mul), rd + ra + rb, [out], alt="vs" if both else "")
+
+    def size(out, c):
+        i = r("cc", 64, 96)
+        put("s", lambda e: g.vector.tensor_scalar(ap(out), ap(i), ap(c), ap(c), A.mult, A.max) if e == "v" else
+            g.scalar.activation(ap(out), ap(i), F.Abs, scale=ap(c)), [i, c], [out], alt="vs")
 
     def tt(out, in0, in1, op):
         i, rd = src(in0)
@@ -209,7 +213,8 @@ def rank_program(g, core, T, topo):
 
     def pick(qo, so, win, wins, off):
         put("v", lambda e: g.vector.tensor_copy(ap(qo).bitcast(dt.uint32), ap(win).bitcast(dt.uint32).indirect(ap(off))), [win, off], [qo])
-        put("s", lambda e: g.scalar.activation(ap(so), ap(wins).indirect(ap(off)), F.Copy), [wins, off], [so])
+        put("s", lambda e: g.vector.tensor_copy(ap(so), ap(wins).indirect(ap(off))) if e == "v" else
+            g.scalar.activation(ap(so), ap(wins).indirect(ap(off)), F.Copy), [wins, off], [so], alt="vs")
 
     def side(x):
         return ap(x).bitcast(dt.uint8) if SCRATCH[x[0]][2] == CODE else ap(x)
@@ -259,11 +264,12 @@ def rank_program(g, core, T, topo):
         return q, q + w
 
     def exchange(n, o=0, w=64):
-        for a in range(4):
-            b = (a + 1) % 4
-            copy("vs"[a % 2], r(n, o + w, o + 2 * w, 1, 32 * a, 32 * a + 32), r(n, o, o + w, 1, 32 * b, 32 * b + 32))
-        copy("v", r(n, o + 2 * w, o + 4 * w, 1, 0, 64), r(n, o, o + 2 * w, 1, 64, 128))
-        copy("s", r(n, o + 2 * w, o + 4 * w, 1, 64, 128), r(n, o, o + 2 * w, 1, 0, 64))
+        for d in (1, 3):
+            for a in range(4):
+                b = (a + d) % 4
+                copy("vs"[a % 2], r(n, o + d * w, o + d * w + w, 1, 32 * a, 32 * a + 32), r(n, o, o + w, 1, 32 * b, 32 * b + 32))
+        copy("v", r(n, o + 2 * w, o + 3 * w, 1, 0, 64), r(n, o, o + w, 1, 64, 128))
+        copy("s", r(n, o + 2 * w, o + 3 * w, 1, 64, 128), r(n, o, o + w, 1, 0, 64))
 
     def col(n, c):
         return r(n, c, c + 1)
@@ -277,30 +283,24 @@ def rank_program(g, core, T, topo):
     QX, QU, QV, QW, QB = ("qx", "sx", 0, 256), ("qu", "su", 0, 128), ("qv", "sv", 0, 128), ("qw", "sw", 0, 128), ("qb", "sb", 0, 256)
     IOT = r("iot", 0, 2048)
 
-    mv = []
-    for gr in range(8):
-        a = gr // 2
-        q = "ys"[gr % 2]
-        mv.append((q, r("nb32", 0, 48 - 12 * a, 1, 16 * gr, 16 * gr + 16), T.nb[:, 12 * a:48]))
-        if a:
-            mv.append((q, r("nb32", 48 - 12 * a, 48, 1, 16 * gr, 16 * gr + 16), T.nb[:, 0:12 * a]))
-    dma(mv)
+    dma([("ys"[k % 2], r("nb32", 48 * (k // 2), 48 * (k // 2) + 48, 1, 16 * (k % 2), 16 * (k % 2) + 16), T.nb[:]) for k in range(4)])
     dma([("y", r("xb", 0, 1024), T.x[:])])
     dma([("s", r("u4", 0, 4), T.u[:, 0:4])])
     dma([("s", r("v4", 0, 4), T.v[:, 0:4])])
     dma([("y", r("bb_t", 0, 1024), T.bb[:])])
-    for h in range(2):
-        dma([("y", r("at", 1024 * h, 1024 * h + 1024), T.a[:, 1024 * h:1024 * h + 1024])])
+    dma([("y", r("at", 0, 2048), T.a[:])])
     dma([("y", r("wt", 0, 512), T.w[:])])
 
     C4096, CM128, CONE = r("cc", 0, 32), r("cc", 32, 64), r("cc", 96, 128)
+    CBIG, NEAR = r("cc", 128, 160), 0.25 + 1.0 / 1024
     PP, P32, P16, B64, PI, PO = col("cf", 0), col("cf", 1), col("cf", 2), col("cf", 26), col("cf", 43), col("cf", 45)
     fill(r("zb", 0, 128), 0.0)
     iota(col("ci", 0), [[0, 1]], 0, 1)
     iota(r("iot", 0, 256), [[1, 256]], 0)
     iota(r("kk", 24, 72), [[0, 16], [1, 3]], 0)
     iota(r("iot", 1536, 2048), [[1, 512]], 1536)
-    iota(r("lo", 8, 11), [[4096, 3]], 0)
+    iota(r("lo", 8, 14), [[-2, 2], [-32, 3]], 0)
+    iota(col("lo", 14), [[0, 1]], 254)
     ts(col("ci", 1), col("ci", 0), 31, A.bitwise_and)
     ts(col("ci", 2), col("ci", 0), 15, A.bitwise_and)
     copy("v", r("cf", 0, 3), r("ci", 0, 3))
@@ -321,16 +321,24 @@ def rank_program(g, core, T, topo):
     ts(col("cf", 3), PP, 2.0, A.mult, P32, A.subtract)
     ts(r("jo", 2, 4), r("iot", 0, 64, 32), col("cf", 3), A.add, 1.0 / 512, A.mult)
 
-    tt(r("kk", 168, 216), r("nb32", 0, 48), r("kk", 72, 120), A.mult)
+    for a in range(4):
+        tt(blk("kk", 168, 216, a), blk("nb32", 12 * a, 12 * a + 48, 0), blk("kk", 72, 120, 0), A.mult)
     scan(r("kk", 216, 264), r("kk", 120, 168), r("kk", 168, 216), 0.0, A.mult, A.add)
     copy("v", r("far16", 0, 16), r("kk", 218, 264, 3))
     tt(r("ka", 0, 256), (IOT, r("far16", 0, 16)), r("jf", 0, 256), A.add)
-    const(C4096, 4096.0)
+    const(C4096, -4096.0)
+    const(CBIG, -2.0 ** 21)
     const(CM128, -128.0)
     const(CONE, 1.0)
-    tr(r("kat", 0, 64), r("ka", 0, 64))
-    tt(r("jo", 4, 6), r("jo", 2, 4), r("kat", 0, 64, 32), A.subtract)
-    ts(junk(0), r("ka", 0, 256), col("jo", 4), A.add)
+    const(r("cc", 64, 96), -1.0)
+    ts(col("ci", 9), col("ci", 0), 4, A.arith_shift_right, 1, A.bitwise_and)
+    copy("v", col("cf", 4), col("ci", 9))
+    ts(col("cf", 5), col("cf", 4), -1.0, A.add)
+    ts(r("kat", 2, 4), r("kk", 218, 230, 6), col("cf", 5), A.mult)
+    ts(r("kat", 4, 6), r("kk", 221, 233, 6), col("cf", 4), A.mult)
+    tt(r("jo", 4, 6), r("kat", 2, 4), r("kat", 4, 6), A.subtract)
+    tt(r("kat", 0, 64, 32), r("jo", 2, 4), r("jo", 4, 6), A.subtract)
+    ts(junk(0), r("ka", 0, 256), col("kat", 0), A.subtract, NEAR, A.add)
     act(junk(6), r("ka", 0, 256), F.Sign, bias=col("kat", 32), scale=-1.0, acc=col("ac", 1))
     ts(col("ac", 17), col("kat", 32), -0.5, A.add)
     act(junk(7), r("ka", 0, 256), F.Sign, bias=col("ac", 17), scale=-1.0, acc=col("ac", 18))
@@ -339,11 +347,12 @@ def rank_program(g, core, T, topo):
     put("v", lambda e: g.vector.tensor_reduce(ap(col("ac", 0)), ap(junk(0)), AxisListType.X, A.min, apply_absolute_value=True), [junk(0)], [col("ac", 0)])
     copy("v", r("fi", 0, 2), r("fa", 0, 2))
     ts(r("fi", 2, 4), r("fi", 0, 2), 255, A.bitwise_and)
-    ts(col("ac", 6), col("ac", 0), col("jo", 2), A.not_equal)
-    ts(col("ac", 7), col("ac", 1), col("ac", 18), A.subtract, 1.0, A.not_equal)
+    ts(col("ac", 21), col("jo", 4), -1.0, A.mult, 2.0 ** 21 * NEAR, A.add)
+    ts(col("ac", 20), col("jo", 5), -1.0, A.mult, -4096.0, A.add)
+    ts(col("ac", 7), col("ac", 1), 4096.0, A.mult, col("ac", 20), A.add)
     copy("v", r("fa", 4, 6), r("fi", 2, 4))
-    for h in range(2):
-        ts(r("sp", 32 * h, 32 * h + 32), C4096, col("ac", 6 + h), A.mult, col("fa", h), A.add, q="vs"[h])
+    ts(r("sp", 0, 32), CBIG, col("ac", 0), A.mult, col("ac", 21), A.add)
+    ts(r("sp", 32, 64), C4096, col("ac", 18), A.mult, col("ac", 7), A.add, q="s")
     ts(col("cf", 17), PP, P16, A.subtract, -16.0, A.mult)
     ts(col("cf", 16), col("cf", 17), 0.5, A.add)
     tr(r("ex", 0, 64), r("sp", 0, 64))
@@ -352,28 +361,24 @@ def rank_program(g, core, T, topo):
     for h in range(2):
         act(junk(1 + h), FR, F.Sign, bias=col("fa", 2 + h), acc=col("ac", 4 + h))
     act(junk(8), FR, F.Sign, bias=col("cf", 16), acc=col("ac", 19))
-    ts(r("fa", 6, 8), r("ac", 6, 8), 1048576.0, A.mult)
+    for h in range(2):
+        ts(col("fa", 6 + h), col("sp", 32 * h), col("fa", h), A.subtract, 256.0, A.mult)
     tt(r("fa", 8, 10), r("fa", 6, 8), r("fa", 4, 6), A.add)
     for h in range(2):
         ts(r("sp", 64 + 32 * h, 96 + 32 * h), CM128, col("ac", 4 + h), A.mult, col("fa", 8 + h), A.add, q="vs"[h])
-    ts(col("cf", 18), P16, 256.0, A.mult)
+    ts(col("cf", 18), P16, -2.0, A.mult)
     tr(r("ex", 256, 320), r("sp", 64, 128))
-    ts(r("lo", 0, 3), r("lo", 8, 11), col("cf", 18), A.add)
+    ts(r("lo", 16, 23), r("lo", 8, 15), col("cf", 18), A.add)
     exchange("ex", 256)
-    ts(col("cf", 19), col("ac", 19), -128.0, A.mult)
-    ts(r("lo", 3, 6), r("lo", 0, 3), col("cf", 19), A.add)
-    ts(r("lo", 11, 14), r("lo", 3, 6), 256.0, A.add)
-    ts(r("cf", 21, 24), r("lo", 3, 6), -255.0, A.mult, -32512.0, A.add)
-    ts(col("lo", 14), col("lo", 3), -1.0, A.mult)
-    ts(col("lo", 15), col("lo", 3), 33024.0, A.add)
-    act(junk(5), CR2, F.Relu, bias=col("lo", 14))
+    ts(r("lo", 0, 7), r("lo", 16, 23), col("ac", 19), A.add, -128.0, A.mult)
+    ts(r("cf", 21, 24), r("lo", 0, 3), -255.0, A.mult, -32512.0, A.add)
+    act(junk(5), CR2, F.Relu, bias=col("lo", 3), scale=-1.0)
     act(r("cq", 0, 256), junk(5), F.Relu, bias=256.0, scale=-1.0, acc=col("ac", 16))
     for c in (1, 2):
-        ts(r("cq", 256 * c, 256 * c + 256), CR2, col("lo", 3 + c), A.max, col("lo", 11 + c), A.min)
-    ts(col("lst", 0), col("ac", 16), -1.0, A.mult, col("lo", 15), A.add, q="s")
+        ts(r("cq", 256 * c, 256 * c + 256), CR2, col("lo", c), A.max, col("lo", 3 + c), A.min)
+    ts(r("cz", 381, 384, 3), col("ac", 16), col("lo", 6), A.add, q="s")
     for c in (1, 2):
-        scan(r("cz", 128 * c, 128 * c + 128), r("cq", 256 * c, 256 * c + 128), r("cq", 256 * c + 128, 256 * c + 256), 0.0, A.add, A.add)
-        ts(col("lst", c), col("cz", 128 * c + 127), col("cf", 21 + c), A.add)
+        scan(r("cz", c, 384, 3), r("cq", 256 * c, 256 * c + 128), r("cq", 256 * c + 128, 256 * c + 256), col("cf", 21 + c), A.add, A.add)
 
     quant("qx", "sx", 0, 256, r("xb", 0, 1024))
     for i in range(4):
@@ -383,7 +388,7 @@ def rank_program(g, core, T, topo):
     tr(r("ept", 0, 256), r("pe", 0, 256))
     copy("s", r("ep", 0, 8), r("ept", 0, 256, 32))
     send_all(r("ep", 0, 8), "er", 0, "aer")
-    send_all(r("lst", 0, 3), "rl", 0, "arl")
+    send_all(r("cz", 381, 384), "er", 56, "arl")
     mm("px", 0, QU, QX)
     copy("s", r("et", 0, 256), r("px", 0, 256))
     dma([("y", r("gq", 0, 256), r("qx", 0, 256)), ("y", r("gs", 0, 256), r("sx", 0, 256))])
@@ -397,8 +402,9 @@ def rank_program(g, core, T, topo):
     ts(r("frt", 0, 4), r("iot", 0, 64, 16), B64, A.add, PI, A.add)
     copy("s", r("jr", 0, 64), (IOT, r("frt", 0, 4)))
     for h in range(2):
-        ts(r("jj", 64 * h, 64 * h + 64), r("jr", 0, 64), col("jo", h), A.is_lt, TINY, A.mult)
-    copy("v", r("nbt", 0, 12), r("nb32", 0, 12))
+        ts(r("jj", 64 * h, 64 * h + 64), r("jr", 0, 64), col("jo", h), A.is_lt, -2.0 ** -24, A.mult)
+    for a in range(4):
+        copy("v", blk("nbt", 0, 12, a), blk("nb32", 12 * a, 12 * a + 12, 0))
     copy("s", r("nbf", 0, 192), (IOT, r("nbt", 0, 12)))
     iota(r("pat", 0, 8), [[1, 2], [96, 2], [48, 2]], 0)
     ts(col("cf", 46), PI, 3.0, A.mult)
@@ -410,21 +416,19 @@ def rank_program(g, core, T, topo):
         ts(r("ll", k, 4, 2), r("lp", 128 + 64 * k, 192 + 64 * k, 32), -256.0 * rank, A.add)
     iota(r("d16", 64, 128), [[0, 4], [1, 16]], 0)
     ts(r("d16", 0, 64), r("d16", 64, 128), P16, A.is_equal)
-    const(r("kk", 264, 268), 0.0)
     iota(r("pat", 8, 40), [[1, 32]], 0)
     for h in range(2):
         act(r("ft", 64 + 32 * h, 96 + 32 * h), r("pat", 8, 40), F.Sign)
     ts(r("gi", 0, 4), r("kk", 218, 228, 3), 2048.0 - 256.0 * (rank + 1), A.add)
-    ts(r("fi", 10, 14), r("gi", 0, 4), 5, A.arith_shift_right, 63, A.bitwise_and)
-    ts(r("gi", 4, 8), r("gi", 0, 4), 8, A.arith_shift_right, 7, A.bitwise_and)
-    copy("v", r("c01", 0, 4), r("fi", 10, 14))
-    copy("v", r("c01", 4, 8), r("gi", 4, 8))
+    ts(r("gi", 16, 20), r("gi", 0, 4), 5, A.arith_shift_right, 63, A.bitwise_and)
+    ts(r("gi", 20, 24), r("gi", 0, 4), 8, A.arith_shift_right, 7, A.bitwise_and)
+    copy("v", r("c01", 0, 8), r("gi", 16, 24))
     copy("v", r("fr", 0, 64), r("ka", 0, 64))
     ts(r("fr", 64, 128), r("fr", 0, 64), 31, A.bitwise_and)
     ts(r("mk", 0, 64), r("fr", 64, 128), P32, A.is_equal)
-    ts(r("fr", 128, 192), r("fr", 0, 64), 2048.0 - 256.0 * (rank + 1), A.add)
-    ts(r("fr", 192, 256), r("fr", 128, 192), 3, A.arith_shift_right, 224, A.bitwise_and)
-    copy("v", r("flp", 0, 2), r("fa", 0, 2))
+    ts(r("fr", 128, 192), r("fr", 0, 64), 255, A.bitwise_and)
+    ts(r("fr", 192, 256), r("fr", 128, 192), UP, A.add)
+    ts(r("cf", 50, 52), r("iot", 0, 448, 224), UP + LAND0, A.add, P32, A.add)
 
     for h in range(2):
         quant("qb", "sb", 128 * h, 128 * h + 128, r("bb_t", 512 * h, 512 * h + 512))
@@ -435,8 +439,10 @@ def rank_program(g, core, T, topo):
     copy("s", r("fn", 0, 256), r("pf", 0, 256))
     copy("s", r("ft", 0, 64), (r("fn", 0, 256), r("frt", 0, 4)))
     tr(r("fn", 0, 64), r("ft", 0, 64))
-    const(r("fz", 0, 66), 0.0)
-    ts(r("fz", 32, 66, 33), r("fn", 0, 64, 32), -1.0, A.mult)
+    const(r("fz", 0, 68), 0.0)
+    const(r("fz", 33, 68, 34), 2.0 ** -120)
+    const(r("dz", 65, 130, 64), 0.0)
+    ts(r("fz", 32, 68, 34), r("fn", 0, 64, 32), -1.0, A.mult)
     ts(r("cf", 36, 39), r("iot", 64, 256, 64), B64, A.add, 256.0, A.is_ge)
     ts(r("cf", 32, 35), r("cf", 36, 39), -TINY, A.mult)
     ts(r("kk", 18, 22), r("iot", 0, 4), 0.25, A.mult)
@@ -455,8 +461,6 @@ def rank_program(g, core, T, topo):
     ts(r("dv", 96, 128), (IOT, r("jo16", 0, 2)), UP, A.add, q="s")
     iota(r("ol", 0, 256), [[1, 256]], int(UP))
     iota(r("od", 0, 96), [[1, 96]], int(UP) + OWN0)
-    iota(r("ndv", 0, 224), [[1, 224]], int(UP) + LAND0)
-    iota(r("ndv", 224, 448), [[1, 224]], int(UP) + LAND0 + 224)
     iota(r("wn", 0, 256), [[0, 256]], 0)
     iota(r("xt", 128, 512), [[0, 384]], 0)
     iota(r("pat", 40, 56), [[32, 8], [0, 2]], 0)
@@ -469,6 +473,7 @@ def rank_program(g, core, T, topo):
     ts(r("fi", 6, 8), r("fi", 4, 6), float(7 - rank), A.add)
     ts(r("fi", 8, 10), r("fi", 6, 8), 7, A.bitwise_and)
     ts(r("fa", 14, 16), r("fi", 8, 10), float(LC), A.mult, UP + FAR0, A.add)
+    ts(r("fa", 16, 18), r("fi", 8, 10), 32.0, A.mult)
     tt(r("ac", 10, 12), r("ac", 8, 10), r("ac", 4, 6), A.subtract)
     for h in range(2):
         ts(col("ac", 14 + h), col("ac", 10 + h), 0.5, A.mult, col("fa", 14 + h), A.add)
@@ -477,14 +482,13 @@ def rank_program(g, core, T, topo):
     ts(r("fl2", 0, 2), r("iot", 0, 64, 32), P32, A.add)
     copy("s", r("dv", 64, 96), (FL, r("fl2", 0, 2)))
 
-    dma([("y", r("rl", 21, 32), r("cc", 0, 11))])
-    tr(r("rl2", 0, 32), r("rl", 0, 32))
+    tr(r("rl2", 0, 32), r("er", 45, 77))
     o = 16 * (rank % 2)
     for i in (32, 48):
-        ts(r("rl2", i, i + 16), r("rl2", o, o + 16), 255.0, A.min)
+        copy("vs"[i // 48], r("rl2", i, i + 16), r("rl2", o, o + 16))
     tr(r("rl2", 64, 96), r("rl2", 32, 64))
     for a in range(4):
-        copy("v", blk("rep", 0, 21, a), blk("rl2", 64, 85, rank // 2))
+        ts(blk("rep", 0, 21, a), blk("rl2", 75, 96, rank // 2), 255.0, A.min)
     pick(r("slc", 0, 336), r("sls", 0, 336), r("qx", 0, 256), r("sx", 0, 256), r("rep", 0, 21))
     for s, l, arr in (("slc", "gq", "ac0"), ("sls", "gs", "as0")):
         send_each([(d, r(s, LC * i, LC * i + LC), r(l, *slot(d, LC, FAR0))) for i, d in enumerate(peers)], arr, r(l, FAR0, LAND0))
@@ -500,19 +504,19 @@ def rank_program(g, core, T, topo):
         copy("s", r("dv", 0, 64), (r("ol", 0, 256), r("dl", 0, 4)))
         tt(r("lg", 0, 64), (r("et", 0, 256), r("ll", 0, 4)), r("d16", 0, 64), A.mult)
         scan(r("dz", 2, 130, 2), r("ft", 64, 128), r("lg", 0, 64), 0.0, A.mult, A.add)
-        win = (r("er", 48 + 8 * t, 55 + 8 * t), r("c01", 4, 8)) if t else (r("er", 0, 56), r("c01", 0, 4))
+        win = (r("er", 72 + 8 * t, 79 + 8 * t), r("c01", 4, 8)) if t else (r("er", 0, 56), r("c01", 0, 4))
         tt(r("tg", 0, 64), win, r("mk", 64 * (t % 2), 64 * (t % 2) + 64), A.mult)
         for h in range(2):
             tr(r("dz", 32 + 64 * h, 64 + 64 * h), r("tg", 32 * h, 32 * h + 32))
         for h in range(2):
-            scan(r("zo", 40 * h, 40 * h + 33), r("dz", 32 + 64 * h, 65 + 64 * h), r("fz", 33 * h, 33 * h + 33), col("ok", h) if t else 0.0, A.add, A.add)
-            act(r("sp", 192 + 32 * h, 224 + 32 * h), CONE, F.Abs, scale=col("zo", 40 * h + 32))
+            scan(r("zo", 40 * h, 40 * h + 34), r("dz", 32 + 64 * h, 66 + 64 * h), r("fz", 34 * h, 34 * h + 34), col("ok", h) if t else 0.0, A.add, A.add)
+            size(r("sp", 192 + 32 * h, 224 + 32 * h), col("zo", 40 * h + 33))
         tr(r("z", 0, 64), r("sp", 192, 256))
         exchange("z")
         for h in range(2):
             o, zt = 256 * h, col("sp", 192 + 32 * h)
-            ts(r("dd", 64 * h, 64 * h + 64), r("z", 0, 64), -1.0, A.mult, zt, A.add, q="s")
-            tt(r("mm_", o, o + 64), r("dd", 64 * h, 64 * h + 64), r("jj", 64 * h, 64 * h + 64), A.is_lt)
+            ts(r("dd", 64 * h, 64 * h + 64), r("jj", 64 * h, 64 * h + 64), zt, A.mult, zt, A.add, q="s")
+            tt(r("mm_", o, o + 64), r("z", 0, 64), r("dd", 64 * h, 64 * h + 64), A.is_gt)
             for d in range(1, 4):
                 ts(r("mm_", o + 64 * d, o + 64 * d + 64), r("z", 64 * d, 64 * d + 64), zt, A.subtract, col("cf", 31 + d), A.is_gt)
             scan(r("cx", 128 * h, 128 * h + 128), r("mm_", o, o + 128), r("mm_", o + 128, o + 256), 0.0, A.add, A.add)
@@ -536,8 +540,7 @@ def rank_program(g, core, T, topo):
         ts(r("po", po, po + 16), (r("sm", 0, 96), r("fo", 0, 1)), -UP, A.add)
         ts(r("nd_", po, po + 16), (r("sm", 0, 96), r("fo", 0, 1)), -UP, A.add, q="s")
         if t < 2:
-            ts(r("sel", 2 * t, 2 * t + 2), ndl, 256.0 * rank, A.add)
-            send_all(r("sel", 2 * t, 2 * t + 2), "an", 16 * t, "an%d" % t)
+            send_all(col("sm", 79), "an", 8 * t, "an%d" % t)
         nq, ns = "nq%d" % t, "ns%d" % t
         pick(r(nq, 0, 128), r(ns, 0, 128), r("gq", 0, W), r("gs", 0, W), r("po", po, po + 8))
         for b in range(4):
@@ -555,7 +558,7 @@ def rank_program(g, core, T, topo):
         if t < 2:
             mm("px", 0, QU, new)
             tr(r("ec", 32 * t, 32 * t + 32), r("px", 0, 32))
-            send_all(col("ec", 32 * t), "er", 56 + 8 * t, "ae%d" % t)
+            send_all(col("ec", 32 * t), "er", 80 + 8 * t, "ae%d" % t)
             for n, arr in (("gq", "ac%d" % (t + 1)), ("gs", "as%d" % (t + 1))):
                 send_all(r(n, at, at + 32), n, W, arr)
             copy("s", r("nw", 0, 32), r("px", 0, 32))
@@ -563,21 +566,26 @@ def rank_program(g, core, T, topo):
         mm("py", 0, QW, new)
         copy("s", r("nw", 32, 64), r("py", 0, 32))
         scatter(r("yt", 0, 256), ndl, r("nw", 32, 64))
-        dma([("y", T.nd[t:t + 1, 16 * c:16 * c + 16], r("nd_", po + 8 + c, po + 9 + c, 1, 0, 16)) for c in range(2)])
+        ts(col("ok", 4 + t), col("sm", 79), -UP, A.add, q="s")
+        dma([("y", T.nd[t:t + 1, :], r("ok", 4 + t, 5 + t, 1, 0, 32))])
         if t < 2:
-            scatter(IOT, r("an", 16 * t, 16 * t + 14), r("ndv", 224 * t, 224 * t + 224))
-            tt(r("rel", 0, 64), (IOT, r("far16", 0, 4)), r("fr", 192, 256), A.subtract)
-            m = 64 * ((t + 1) % 2)
-            ts(r("mk", m, m + 64), r("rel", 0, 64), UP + W, A.subtract, P32, A.is_equal)
+            m = r("mk", 64 * ((t + 1) % 2), 64 * ((t + 1) % 2) + 64)
+            tt(m, (r("an", 8 * t, 8 * t + 7), r("c01", 4, 8)), r("fr", 192, 256), A.is_equal)
+            ts(r("rel", 0, 64), m, col("cf", 50 + t), A.mult)
             tr(r("rel", 64, 128), r("rel", 0, 64))
+            scan(r("rel", 128, 192), r("ft", 64, 128), r("rel", 64, 128), 0.0, A.mult, A.add)
             for h in range(2):
-                ts(col("ok", h), col("rel", 64 + 32 * h), UP + W, A.is_lt, col("zo", 40 * h + 31), A.mult)
-            tt(r("dv", 64, 96), (IOT, r("flp", 0, 2)), r("dv", 64, 96), A.max)
+                v = col("rel", 159 + 32 * h)
+                ts(col("ok", h), v, 0.5, A.is_lt, col("zo", 40 * h + 31), A.mult)
+                ts(r("sp", 128 + 32 * h, 160 + 32 * h), CONE, v, A.mult, col("fa", 16 + h), A.add)
+            tr(FL, r("sp", 128, 192))
+            tt(r("dv", 64, 96), (FL, r("fl2", 0, 2)), r("dv", 64, 96), A.max)
 
-    copy("s", r("og", 0, 256), (r("ol", 0, 256), r("d8", 0, 16)))
-    tr(r("ogt", 0, 256), r("og", 0, 256))
-    ts(r("oo", 0, 16), r("ogt", 0, 256, 16), -UP, A.add)
-    pick(r("occ", 0, 256), r("ocs", 0, 256), r("gq", 0, FAR0), r("gs", 0, FAR0), r("oo", 0, 16))
+    for c in (0, 128):
+        copy("s", r("og", c, c + 128), (r("ol", 0, 256), r("d8", c // 16, c // 16 + 8)))
+        tr(r("ogt", c, c + 128), r("og", c, c + 128))
+        ts(r("oo", c // 16, c // 16 + 8), r("ogt", c, c + 128, 16), -UP, A.add)
+        pick(r("occ", c, c + 128), r("ocs", c, c + 128), r("gq", 0, FAR0), r("gs", 0, FAR0), r("oo", c // 16, c // 16 + 8))
     dma([("y", T.oc[:], r("occ", 0, 256))])
     dma([("y", T.osc[4 * k:4 * k + 4, :], r("ocs", 0, 256, 1, 32 * k, 32 * k + 4)) for k in range(4)])
     dma([("s", T.y[:], r("yt", 0, 256))])

@@ -4,26 +4,26 @@ from concourse.mybir import dt, AluOpType, AxisListType, ActivationFunctionType
 A = AluOpType
 F = ActivationFunctionType
 P, K, R, LC = 256, 32, 3, 48
-OWN0, FAR0, LAND0 = 256, 448, 784
+OWN0, FAR0, LAND0 = 256, 512, 848
 UP = 4096.0
 C05 = 13421773 * 2.0 ** -28
 TINY = 2.0 ** -110
 ORDER = """
-3 5y 10 11 2s 0 1 18 12 17 4 181v 192 50 46 49 20 9s 19 6y 182v 21 45 25 7 47 132 189 36 13 183 22 26s 185 8 133 29 51 134 14 119 23 30 117 116v
-142 24 52s 38 27 31 39 41 40 118v 144 188s 143 186s 35s 42 32s 120 37 54s 155 115 53s 28 145 135 43 55 157 121 130 172 173v 128 33 174v 34s 131 56
-148s 160 67s 147 122 62s 158 59s 44 48 203 123 146 149 138 66 57 58 124 175v 60 170 63 68s 93s 61s 171 71 162 72 70s 64 150 176 139 74 89 65 187s
-177 88 156 15 75 81s 164 80 78v 76 77s 161 83s 79 84 82v 16 73 178 207 151 165 85 69 129v 195 86 90 179v 159 201 166 153 91s 95 154 92 208 87 180
-94 190 245 211 125 106 99 105v 194 104s 103v 100s 97v 98s 102 101 96 209 163 246 205 107 108 111 110 196 247 109 114 197 136 184s 113 249 248 112
-141 210 212 252 250 126 213 204 253 215 251 140 137 271v 218s 216 265 254 237 219s 217 266 262 261s 259 260 263s 256 220 264 272 258 257s 275 255s
-127 223 221 274 269 224s 225v 193 273 268 222 200 226 267 276 152 228 230 229 227 244 270 198 278 232 277 231 279 235 233 202 283 280 282 281 199
-240 284s 289 292 285 288 294v 286v 293 291s 290v 287 239 236 295 238 296 297 298 332v 377 191v 167 301 333s 234 300 307 169 306 309 303 302 308
-304 305 311 299 344 310 312 313 315 314 316 317 168 318 334 241 319 335s 242 320 336 214 321 327 337 323 325 341 339s 340 328 338 342 345 346 322
-347 343 348 349 350 352 324 351 353v 326 365 354 371 355 358 364v 363s 361s 372 356 360 357 359s 366 362 243 374 368 373 367 369 375 329 370 376
-378 379 380 383 381 384 382 395 389v 391v 393 387v 392s 394 388 390s 386 385 330 396 206 399 398 397 401 402 408 407 404 405 409 403 406 433 412
-413 411 434s 414 400 417 416 415 418 419 435 410 420 430 436 421 437 428 422 438 426 424 429 442s 445v 440s 478 446 439 447 331 441 423 448 450 449
-427 453 451 454 452v 425 455 466 443 472 459v 461 463 460 464 462s 465 473 457 458s 467 456s 476 475 469 470 468 474 444 471 477 479 480 481 482
-484 483 485 496v 486s 489 490 492v 494 493s 495v 487 491s 488v 431v 497 522 498 499 523 500 501 506 507 509 504 432 502 508 505 503 524 512 510
-529 513 511 516 525 517 514 515 526 530 518 531 519 527 528 532 520 533 521 534s 536 539 535s 538s 537s
+1y 24 4s 0s 45v 25 2 3y 5 28 26 7 6 183 27 176 29 56v 173 159 11y 161 30 53 8y 10 49 141 48 50 52v 40 31 58 44 37s 32s 16 35s 36s 111 39 33 41 34 42
+38v 62 60 61 63 46 112 43 64 65 20 47 15y 51s 54 113 66 110 160 109 114 115 143 21y 59 196 122 67 166 70 9 68 198 182 197 69 187 71s 72s 55 73 116
+13y 117 178 139 19y 136s 74 83 18 12 199 14 17y 181 77 145 146 76 75 84 80 151 79v 78 82 81 86 153 144 158 132 123 135 140 85 152 156 133 22 154 89
+88 147 134 87 137 201 155 91 92 157 93 102 208 126 101 192 23 94 100v 125 97v 99v 127 98v 118 231 169v 148 96 95 162s 184 233 185 163s 107 108 149 90
+103 105 202 104 150 57 200 119 232 106 234 120 204 138 235 164s 205 165s 167s 129s 230 206 128s 236 179 238 191 188 207 237v 124s 189 251 130s 172s
+239v 227 193 240 241 257 245 246 247 250 248 242 244 243 252 260 228 249 254 121 210 211 258 261 212 255 174 209 253 259 213 215 216 131s 175 214 142
+256 262 168 263 180 218 190 264 217 265 225 268 267 266 269 221 177 219 280v 278v 270 271 273s 275s 272v 274v 186 171v 277s 279 276 281 223 283 284
+366 282 222 226 287 220 286 170v 224 291 296 300 293 194 285 288 297 290 299 289 295 298 203 294 304 292 303 322 301 302 305 229 323 306 195 311v 307
+324s 319 308 325 326 317 318 328 330s 309 327 334 316 335 329 336 337 331 338 310 341 339 340v 342 332 343 345 360 344 354 314 347 346 355 348 357
+363 349 352 364 353 350 351 361 358 356 362 367 333 359 365 368 369 370 372 373 371 374 379v 380s 385v 378 312 376 382 377 384v 313 383 375s 381 386
+387 320 472v 391 315 321 392 396 395 394 393 397 388 401 405 400 404 403 402 399 409 408 389 398 438 407 406 410 390 428 411 429s 416 412 422v 430
+423 427 413 431 439 414 434 415 435s 433s 424 425v 441 440 442 436 432 443 437 446 447 471 465 444 445v 448 452 449 459 451 453 456 450 454 460 457
+455 466 458 462 463 469 468 467 461 470 464 474 473 475 478 479 477 476 481s 480s 489v 483 482 485 484v 488v 490v 419 420 487s 486 491 421 417 493
+492 426 418 494 495 517 504 496 502v 505 497 501 500 518 503 498 506 507 499 509 508 519 510 511 512 524 520 525 513 526 522 521 523 527 514 515 516
+529 528 531s 534y 530s 532 533
 """
 CODE, U8, BF, F32, I32, U16 = "float8_e4m3fn_x4", "uint8", "bfloat16", "float32", "int32", "uint16"
 
@@ -32,20 +32,22 @@ def _sbuf(dtype, **cols):
     return {n: ("sbuf", [128, c], dtype) for n, c in cols.items()}
 
 
-SCRATCH = {"pe": ("psum", [128, 512], F32), "pf": ("psum", [128, 512], F32), "ps": ("psum", [128, 2048], F32), "py": ("psum", [128, 512], F32),
+SCRATCH = {"pe": ("psum", [128, 512], F32), "ps": ("psum", [128, 2560], F32), "py": ("psum", [128, 512], F32),
            "px": ("psum", [128, 512], F32)}
-SCRATCH.update(_sbuf(F32, nbf=192, iot=2048, jf=256, cf=64, jo=8, ka=256, kat=64, junk=2304, cq=768, cz=384, ac=32, fa=28, sp=256, ex=576, cc=160,
-                     lo=24, fn=256, z=256, dd=128, jj=128, c4=288, wn=1088, wt_=576, dv=128, kk=288, nd_=48, bbs=128, sc4=512, an=16, od=96,
-                     og=256, ogt=256, yt=256, ept=256, ep=8, ec=64, er=96, rl2=96, et=256, ol=256, mk=128, tg=64, lg=64, dz=132,
-                     fz=72, zo=80, ok=8, rel=192, jr=64, ft=128, lp=256, d16=128, nw=64, pat=64))
-SCRATCH.update(_sbuf(I32, nb32=96, ci=16, fi=16, gi=24, fr=256))
-SCRATCH.update(_sbuf(U16, nbt=12, far16=16, rep=24, so=8, po=48, bo=8, frt=4, cl=8, dl=4, ll=4, c01=8, fl2=2, jo16=2, fo=2, d8=16, oo=16))
-SCRATCH.update(_sbuf(BF, xb=1024, bb_t=1024, at=2048, wt=512, u4=4, v4=4, ub=512, vb=512, mm_=512, xt=512, cx=256, zb=128))
-for _c, _s, _n in (("qx", "sx", 256), ("qb", "sb", 256), ("qu", "su", 128), ("qv", "sv", 128), ("qa", "sa", 512), ("qw", "sw", 128), ("slc", "sls", 336),
-                   ("gq", "gs", 1232), ("nq0", "ns0", 128), ("nq1", "ns1", 128), ("nq2", "ns2", 128), ("occ", "ocs", 256)):
+SCRATCH.update(_sbuf(F32, tf=32, g1=16, s2=192, iot=2048, jf=256, cf=64, jo=8, ka=256, junk=2304, cq=768, cz=384, ac=32, fa=28, sp=256, ex=576, cc=160,
+                     lo=24, z=256, dd=128, jj=128, c4=288, wn=1600, wt_=480, dv=128, kk=8, bbs=256, sc4=768, an=16, od=96,
+                     og=256, ogt=256, yt=256, ept=256, ep=8, ec=64, er=96, rl2=96, et=256, ol=256, mk=128, tg=64, lg=64,
+                     fz=72, zo=80, ok=8, rel=192, ft=128, d16=128, nw=64, pat=64))
+SCRATCH.update(_sbuf(I32, ci=16, fi=16, gi=32, fr=256))
+SCRATCH.update(_sbuf(U16, go=4, dl=4, odd=2, far16=16, rep=24, so=8, po=48, c01=12, fl2=2, fo=2, d8=16, oo=16))
+SCRATCH.update(_sbuf(BF, xb=1024, bt=1024, bb_t=1024, at=2048, wt=512, u4=4, ub=520, m2=320, mm_=512, xt=512, cx=256, zb=128))
+for _c, _s, _n in (("qx", "sx", 256), ("qb", "sb", 256), ("qu", "su", 130), ("qa", "sa", 512), ("qw", "sw", 128), ("slc", "sls", 336),
+                   ("gq", "gs", 1296), ("xq0", "xs0", 128), ("xq1", "xs1", 128), ("sq0", "ss0", 32), ("sq1", "ss1", 32),
+                   ("nq0", "ns0", 128), ("nq1", "ns1", 128), ("nq2", "ns2", 128), ("occ", "ocs", 256)):
     SCRATCH.update({_c: ("sbuf", [128, _n], CODE), _s: ("sbuf", [128, _n], U8)})
+SCRATCH.update({"rl3": ("sbuf", [128, 4, 16], F32), "dz": ("sbuf", [128, 2, 64], F32), "nb32": ("sbuf", [128, 3, 48], I32)})
 SEMAPHORES = ["cv", "cs", "ct", "cg"] + ["q%d" % i for i in range(40)] + ["aer", "arl", "ac0", "as0", "an0", "an1", "ae0", "ae1", "ac1", "as1", "ac2", "as2"]
-PARTS = {"wm": ("c4", 128), "fr_": ("c4", 224), "wx": ("wt_", 384), "sm": ("wt_", 480)}
+PARTS = {"wm": ("c4", 128), "fr_": ("c4", 224), "wx": ("wt_", 320), "sm": ("wt_", 400)}
 
 
 def r(name, c0, c1, step=1, p0=0, p1=128):
@@ -62,6 +64,9 @@ def rank_program(g, core, T, topo):
     cnt, known, log, pool, snaps, ops = {}, {q: {} for q in eng}, {}, [0], {}, []
 
     def ap(x):
+        if len(SCRATCH[x[0]][1]) == 3:
+            w = SCRATCH[x[0]][1][2]
+            return T[x[0]][x[4]:x[5], x[1] // w, x[1] % w:x[2] - x[1] // w * w:x[3]]
         return T[x[0]][x[4]:x[5], x[1]:x[2]:x[3]] if x[3] != 1 else T[x[0]][x[4]:x[5], x[1]:x[2]]
 
     def span(x):
@@ -196,7 +201,7 @@ def rank_program(g, core, T, topo):
         put("v", lambda e: g.vector.tensor_tensor_scan(ap(out), ap(d0), ap(d1), a, op0, op1), [d0, d1] + ra, [out])
 
     def tr(out, in_):
-        put("v", lambda e: g.vector.transpose(ap(out), ap(in_)), [in_], [out])
+        return put("v", lambda e: g.vector.transpose(ap(out), ap(in_)), [in_], [out])
 
     def fill(out, val):
         put("v", lambda e: g.vector.memset(ap(out), val), [], [out])
@@ -263,13 +268,14 @@ def rank_program(g, core, T, topo):
         q = base + w * ((rank - d - 1) % 8)
         return q, q + w
 
-    def exchange(n, o=0, w=64):
-        for d in (1, 3):
-            for a in range(4):
-                b = (a + d) % 4
-                copy("vs"[a % 2], r(n, o + d * w, o + d * w + w, 1, 32 * a, 32 * a + 32), r(n, o, o + w, 1, 32 * b, 32 * b + 32))
-        copy("v", r(n, o + 2 * w, o + 3 * w, 1, 0, 64), r(n, o, o + w, 1, 64, 128))
-        copy("s", r(n, o + 2 * w, o + 3 * w, 1, 64, 128), r(n, o, o + w, 1, 0, 64))
+    def exchange(n, o, src, nv):
+        tr(r(n, o, o + 64), src)
+        for k, (d, p, q, w) in enumerate([(2, 0, 64, 64), (2, 64, 0, 64)] + [(d, 32 * a, 32 * ((a + d) % 4), 32) for d in (3, 1) for a in range(4)]):
+            out = r(n, o + 64 * d, o + 64 * d + 64, 1, p, p + w)
+            if k < nv:
+                tr(out, r(src[0], src[1], src[2], 1, q, q + w))
+            else:
+                copy("s", out, r(n, o, o + 64, 1, q, q + w))
 
     def col(n, c):
         return r(n, c, c + 1)
@@ -280,110 +286,95 @@ def rank_program(g, core, T, topo):
     def junk(i):
         return r("junk", 256 * i, 256 * i + 256)
 
-    QX, QU, QV, QW, QB = ("qx", "sx", 0, 256), ("qu", "su", 0, 128), ("qv", "sv", 0, 128), ("qw", "sw", 0, 128), ("qb", "sb", 0, 256)
+    QX, QU, QW = ("qx", "sx", 0, 256), ("qu", "su", 0, 128), ("qw", "sw", 0, 128)
     IOT = r("iot", 0, 2048)
 
-    dma([("ys"[k % 2], r("nb32", 48 * (k // 2), 48 * (k // 2) + 48, 1, 16 * (k % 2), 16 * (k % 2) + 16), T.nb[:]) for k in range(4)])
+    def table(k, c0, on):
+        moves = []
+        for p in (0, 16):
+            q = 0
+            while q < 16:
+                s, row = divmod(3 * q + k, 16)
+                n = len(range(row, 16, 3))
+                moves.append(("ys"[len(moves) % 2], r("nb32", c0, c0 + 46 - on * p // 16, 1, p + q, p + q + n), T.nb[row:16:3, s + on * p // 16:s + 46]))
+                q += n
+        return moves
+
+    dma(table(2, 0, 0))
     dma([("y", r("xb", 0, 1024), T.x[:])])
     dma([("s", r("u4", 0, 4), T.u[:, 0:4])])
-    dma([("s", r("v4", 0, 4), T.v[:, 0:4])])
+    dma([("s", r("ub", 512, 520), T.v[:, 0:8])])
     dma([("y", r("bb_t", 0, 1024), T.bb[:])])
+    dma(table(0, 48, 3) + table(1, 96, 3))
     dma([("y", r("at", 0, 2048), T.a[:])])
     dma([("y", r("wt", 0, 512), T.w[:])])
 
-    C4096, CM128, CONE = r("cc", 0, 32), r("cc", 32, 64), r("cc", 96, 128)
-    CBIG, NEAR = r("cc", 128, 160), 0.25 + 1.0 / 1024
-    PP, P32, P16, B64, PI, PO = col("cf", 0), col("cf", 1), col("cf", 2), col("cf", 26), col("cf", 43), col("cf", 45)
+    C2048, CHALF, CONE, CBIG = r("cc", 0, 32), r("cc", 32, 64), r("cc", 96, 128), r("cc", 128, 160)
+    PP, P32, P16, B64, G16 = col("cf", 0), col("cf", 1), col("cf", 2), col("cf", 26), col("cf", 43)
+    TURN = 2048.0 - 256.0 * (rank + 1)
     fill(r("zb", 0, 128), 0.0)
     iota(col("ci", 0), [[0, 1]], 0, 1)
     iota(r("iot", 0, 256), [[1, 256]], 0)
-    iota(r("kk", 24, 72), [[0, 16], [1, 3]], 0)
-    iota(r("iot", 1536, 2048), [[1, 512]], 1536)
-    iota(r("lo", 8, 14), [[-2, 2], [-32, 3]], 0)
-    iota(col("lo", 14), [[0, 1]], 254)
+    iota(r("iot", 1792, 2048), [[1, 256]], 1792)
     ts(col("ci", 1), col("ci", 0), 31, A.bitwise_and)
     ts(col("ci", 2), col("ci", 0), 15, A.bitwise_and)
     copy("v", r("cf", 0, 3), r("ci", 0, 3))
-    ts(col("ci", 3), col("ci", 2), 11.0, A.mult)
-    ts(col("ci", 4), col("ci", 3), 5, A.arith_shift_right)
-    ts(col("cf", 40), col("ci", 4), -3.0, A.mult, P16, A.add)
-    ts(r("kk", 72, 120), r("kk", 24, 72), col("cf", 40), A.add, 2.0, A.is_equal)
-    act(r("kk", 120, 168), r("kk", 24, 72), F.Sign)
     ts(B64, PP, P32, A.subtract, 2.0, A.mult)
-    ts(r("iot", 256, 512), r("iot", 0, 256), 256.0, A.add)
-    ts(r("iot", 512, 1024), r("iot", 0, 512), 512.0, A.add, q="s")
-    ts(r("iot", 1024, 1536), r("iot", 0, 512), 1024.0, A.add, q="s")
-    ts(r("gi", 8, 12), r("iot", 0, 256, 64), B64, A.add)
-    ts(r("gi", 12, 16), r("gi", 8, 12), 255, A.bitwise_and)
-    ts(r("cf", 28, 32), r("gi", 12, 16), 1.0 / 512, A.mult)
-    for d in range(4):
-        ts(r("jf", 64 * d, 64 * d + 64), r("iot", 0, 64), 1.0 / 512, A.mult, col("cf", 28 + d), A.add)
+    for c in range(256, 1792, 256):
+        ts(r("iot", c, c + 256), r("iot", 0, 256), float(c), A.add)
+    ts(r("jf", 0, 256), r("iot", 0, 256), 1.0 / 512, A.mult, 1.0 / 1024, A.add, q="s")
+    ts(G16, P32, P16, A.subtract, B64, A.add)
+    ts(col("ci", 3), col("ci", 0), 1, A.bitwise_and)
+    ts(col("cf", 4), col("ci", 3), 32.0, A.mult, G16, A.add)
+    ts(col("go", 0), col("cf", 4), 1.0 / 16, A.mult)
+    ts(col("go", 2), B64, 1.0 / 16, A.mult, P16, A.add)
     ts(col("cf", 3), PP, 2.0, A.mult, P32, A.subtract)
-    ts(r("jo", 2, 4), r("iot", 0, 64, 32), col("cf", 3), A.add, 1.0 / 512, A.mult)
-
-    for a in range(4):
-        tt(blk("kk", 168, 216, a), blk("nb32", 12 * a, 12 * a + 48, 0), blk("kk", 72, 120, 0), A.mult)
-    scan(r("kk", 216, 264), r("kk", 120, 168), r("kk", 168, 216), 0.0, A.mult, A.add)
-    copy("v", r("far16", 0, 16), r("kk", 218, 264, 3))
-    tt(r("ka", 0, 256), (IOT, r("far16", 0, 16)), r("jf", 0, 256), A.add)
-    const(C4096, -4096.0)
+    const(r("tf", 18, 32), 0.0)
+    ts(r("tf", 16, 18), r("iot", 0, 64, 32), col("cf", 3), A.add, 1.0 / 512, A.mult)
+    const(r("tf", 20, 22), TURN)
+    const(col("tf", 22), 0.5 + 2.0 ** 21 * (0.25 + 1.0 / 1024))
+    const(col("tf", 23), 0.5)
+    const(col("tf", 24), -2.0 ** 19)
+    ts(col("tf", 26), col("tf", 16), -0.25, A.add)
+    const(r("m2", 256, 320), 0.0)
+    const(C2048, 2048.0)
     const(CBIG, -2.0 ** 21)
-    const(CM128, -128.0)
+    const(CHALF, 0.5)
     const(CONE, 1.0)
     const(r("cc", 64, 96), -1.0)
-    ts(col("ci", 9), col("ci", 0), 4, A.arith_shift_right, 1, A.bitwise_and)
-    copy("v", col("cf", 4), col("ci", 9))
-    ts(col("cf", 5), col("cf", 4), -1.0, A.add)
-    ts(r("kat", 2, 4), r("kk", 218, 230, 6), col("cf", 5), A.mult)
-    ts(r("kat", 4, 6), r("kk", 221, 233, 6), col("cf", 4), A.mult)
-    tt(r("jo", 4, 6), r("kat", 2, 4), r("kat", 4, 6), A.subtract)
-    tt(r("kat", 0, 64, 32), r("jo", 2, 4), r("jo", 4, 6), A.subtract)
-    ts(junk(0), r("ka", 0, 256), col("kat", 0), A.subtract, NEAR, A.add)
-    act(junk(6), r("ka", 0, 256), F.Sign, bias=col("kat", 32), scale=-1.0, acc=col("ac", 1))
-    ts(col("ac", 17), col("kat", 32), -0.5, A.add)
-    act(junk(7), r("ka", 0, 256), F.Sign, bias=col("ac", 17), scale=-1.0, acc=col("ac", 18))
-    ts(r("fa", 0, 2), r("jo", 4, 6), -1.0, A.mult)
-    ts(r("fa", 2, 4), r("jo", 4, 6), 0.5, A.add)
-    put("v", lambda e: g.vector.tensor_reduce(ap(col("ac", 0)), ap(junk(0)), AxisListType.X, A.min, apply_absolute_value=True), [junk(0)], [col("ac", 0)])
-    copy("v", r("fi", 0, 2), r("fa", 0, 2))
-    ts(r("fi", 2, 4), r("fi", 0, 2), 255, A.bitwise_and)
-    ts(col("ac", 21), col("jo", 4), -1.0, A.mult, 2.0 ** 21 * NEAR, A.add)
-    ts(col("ac", 20), col("jo", 5), -1.0, A.mult, -4096.0, A.add)
-    ts(col("ac", 7), col("ac", 1), 4096.0, A.mult, col("ac", 20), A.add)
-    copy("v", r("fa", 4, 6), r("fi", 2, 4))
-    ts(r("sp", 0, 32), CBIG, col("ac", 0), A.mult, col("ac", 21), A.add)
-    ts(r("sp", 32, 64), C4096, col("ac", 18), A.mult, col("ac", 7), A.add, q="s")
-    ts(col("cf", 17), PP, P16, A.subtract, -16.0, A.mult)
-    ts(col("cf", 16), col("cf", 17), 0.5, A.add)
-    tr(r("ex", 0, 64), r("sp", 0, 64))
-    exchange("ex")
+    ts(col("cf", 16), PP, P16, A.subtract, 16.0, A.mult)
+    ts(r("lo", 16, 19), r("iot", 0, 48, 16), P16, A.add, 2.0, A.mult)
+
+    for a in range(4):
+        copy("v", blk("far16", 0, 16, a), r("nb32", 0, 46, 3, 0, 32))
+    copy("v", r("tf", 0, 16), r("far16", 0, 16))
+    tt(r("ka", 0, 256), (IOT, r("far16", 0, 16)), r("jf", 0, 256), A.add)
+    tt(r("g1", 0, 16), (r("tf", 0, 16), col("go", 0)), r("tf", 16, 32), A.add)
+    act(junk(0), r("ka", 0, 256), F.Abs, bias=col("g1", 10), scale=-1.0)
+    act(junk(7), r("ka", 0, 256), F.Sign, bias=col("g1", 3), scale=-1.0, acc=col("ac", 18))
+    act(junk(6), r("ka", 0, 256), F.Sign, bias=col("g1", 1), scale=-1.0, acc=col("ac", 1))
+    scan(r("junk", 256, 384), r("junk", 0, 128), r("junk", 128, 256), 1.0, A.min, A.min)
+    ts(col("ac", 7), col("ac", 18), -2048.0, A.mult, col("g1", 7), A.add)
+    ts(r("sp", 0, 32), CBIG, col("junk", 383), A.mult, col("g1", 6), A.add)
+    ts(r("sp", 32, 64), C2048, col("ac", 1), A.mult, col("ac", 7), A.add, q="s")
+    exchange("ex", 0, r("sp", 0, 64), 2)
     FR, CR2, FL = r("ex", 0, 256), r("ex", 256, 512), r("ex", 512, 576)
-    for h in range(2):
-        act(junk(1 + h), FR, F.Sign, bias=col("fa", 2 + h), acc=col("ac", 4 + h))
-    act(junk(8), FR, F.Sign, bias=col("cf", 16), acc=col("ac", 19))
-    for h in range(2):
-        ts(col("fa", 6 + h), col("sp", 32 * h), col("fa", h), A.subtract, 256.0, A.mult)
-    tt(r("fa", 8, 10), r("fa", 6, 8), r("fa", 4, 6), A.add)
-    for h in range(2):
-        ts(r("sp", 64 + 32 * h, 96 + 32 * h), CM128, col("ac", 4 + h), A.mult, col("fa", 8 + h), A.add, q="vs"[h])
-    ts(col("cf", 18), P16, -2.0, A.mult)
-    tr(r("ex", 256, 320), r("sp", 64, 128))
-    ts(r("lo", 16, 23), r("lo", 8, 15), col("cf", 18), A.add)
-    exchange("ex", 256)
-    ts(r("lo", 0, 7), r("lo", 16, 23), col("ac", 19), A.add, -128.0, A.mult)
-    ts(r("cf", 21, 24), r("lo", 0, 3), -255.0, A.mult, -32512.0, A.add)
-    act(junk(5), CR2, F.Relu, bias=col("lo", 3), scale=-1.0)
-    act(r("cq", 0, 256), junk(5), F.Relu, bias=256.0, scale=-1.0, acc=col("ac", 16))
-    for c in (1, 2):
-        ts(r("cq", 256 * c, 256 * c + 256), CR2, col("lo", c), A.max, col("lo", 3 + c), A.min)
-    ts(r("cz", 381, 384, 3), col("ac", 16), col("lo", 6), A.add, q="s")
-    for c in (1, 2):
-        scan(r("cz", c, 384, 3), r("cq", 256 * c, 256 * c + 128), r("cq", 256 * c + 128, 256 * c + 256), col("cf", 21 + c), A.add, A.add)
+    ts(r("m2", 0, 256), FR, col("g1", 2), A.is_lt, 4096.0, A.mult)
+    act(junk(2), FR, F.Sign, bias=col("g1", 3), scale=-1.0, acc=col("ac", 5))
+    act(junk(8), FR, F.Sign, bias=col("cf", 16), scale=-1.0, acc=col("ac", 19))
+    scan(r("s2", 0, 160), r("m2", 0, 320, 2), r("m2", 1, 320, 2), col("g1", 8), A.add, A.add)
+    ts(r("s2", 160, 192), C2048, col("ac", 5), A.mult, col("g1", 3), A.add, q="s")
+    ts(col("ac", 4), col("s2", 159), col("g1", 2), A.subtract, 1.0 / 2048, A.mult)
+    exchange("ex", 256, r("s2", 128, 192), 1)
+    ts(r("lo", 0, 3), r("lo", 16, 19), col("ac", 19), A.add, -2048.0, A.mult)
+    for c in range(3):
+        act(r("cq", 256 * c, 256 * c + 256), CR2, F.Abs, bias=col("lo", c))
+        scan(r("cz", c, 384, 3), r("cq", 256 * c, 256 * c + 128), r("cq", 256 * c + 128, 256 * c + 256), 4096.0, A.min, A.min)
 
     quant("qx", "sx", 0, 256, r("xb", 0, 1024))
     for i in range(4):
         ts(r("ub", i, 512, 4), r("zb", 0, 128), col("u4", i), A.add, q="s")
-    quant("qu", "su", 0, 128, r("ub", 0, 512))
+    quant("qu", "su", 0, 130, r("ub", 0, 520))
     mm("pe", 0, QU, QX)
     tr(r("ept", 0, 256), r("pe", 0, 256))
     copy("s", r("ep", 0, 8), r("ept", 0, 256, 32))
@@ -393,102 +384,86 @@ def rank_program(g, core, T, topo):
     copy("s", r("et", 0, 256), r("px", 0, 256))
     dma([("y", r("gq", 0, 256), r("qx", 0, 256)), ("y", r("gs", 0, 256), r("sx", 0, 256))])
 
-    ts(col("ci", 7), col("ci", 3), 10.0, A.add)
-    ts(col("ci", 8), col("ci", 7), 15, A.bitwise_and)
-    copy("v", PI, col("ci", 8))
-    ts(PO, P32, P16, A.subtract, PI, A.add)
-    ts(r("jo", 0, 2), r("iot", 0, 64, 32), B64, A.add, PO, A.add)
-    copy("v", r("jo16", 0, 2), r("jo", 0, 2))
-    ts(r("frt", 0, 4), r("iot", 0, 64, 16), B64, A.add, PI, A.add)
-    copy("s", r("jr", 0, 64), (IOT, r("frt", 0, 4)))
-    for h in range(2):
-        ts(r("jj", 64 * h, 64 * h + 64), r("jr", 0, 64), col("jo", h), A.is_lt, -2.0 ** -24, A.mult)
+    dma([("y", r(n % t, 96, 128), r(s, 0, 32)) for t in range(R) for n, s in (("nq%d", "qx"), ("ns%d", "sx"))])
+
     for a in range(4):
-        copy("v", blk("nbt", 0, 12, a), blk("nb32", 12 * a, 12 * a + 12, 0))
-    copy("s", r("nbf", 0, 192), (IOT, r("nbt", 0, 12)))
-    iota(r("pat", 0, 8), [[1, 2], [96, 2], [48, 2]], 0)
-    ts(col("cf", 46), PI, 3.0, A.mult)
-    ts(r("cl", 0, 8), r("pat", 0, 8), col("cf", 46), A.add)
-    copy("s", r("lp", 0, 128), (r("nbf", 0, 192), r("cl", 0, 8)))
-    tr(r("lp", 128, 256), r("lp", 0, 128))
-    ts(r("dl", 0, 4), r("lp", 128, 256, 32), -256.0 * rank, A.add)
-    for k in range(2):
-        ts(r("ll", k, 4, 2), r("lp", 128 + 64 * k, 192 + 64 * k, 32), -256.0 * rank, A.add)
+        put("v", lambda e, a=a: g.vector.tensor_scalar(ap(blk("dl", 0, 4, a)), T.nb32[0:32, 1:3, 12 * a:12 * a + 7:6], -256.0 * rank, None, A.add),
+            [r("nb32", 48, 144, 1, 0, 32)], [blk("dl", 0, 4, a)])
+    ts(r("jo", 0, 2), r("iot", 0, 64, 32), P32, A.add)
+    for h in range(2):
+        ts(r("jj", 64 * h, 64 * h + 64), r("iot", 0, 64), col("jo", h), A.is_lt, -2.0 ** -24, A.mult)
     iota(r("d16", 64, 128), [[0, 4], [1, 16]], 0)
     ts(r("d16", 0, 64), r("d16", 64, 128), P16, A.is_equal)
-    iota(r("pat", 8, 40), [[1, 32]], 0)
-    for h in range(2):
-        act(r("ft", 64 + 32 * h, 96 + 32 * h), r("pat", 8, 40), F.Sign)
-    ts(r("gi", 0, 4), r("kk", 218, 228, 3), 2048.0 - 256.0 * (rank + 1), A.add)
+    const(r("ft", 64, 128), 1.0)
+    const(r("ft", 64, 128, 32), 0.0)
+    ts(r("gi", 0, 16), (r("tf", 0, 32), col("go", 2)), TURN, A.add)
     ts(r("gi", 16, 20), r("gi", 0, 4), 5, A.arith_shift_right, 63, A.bitwise_and)
     ts(r("gi", 20, 24), r("gi", 0, 4), 8, A.arith_shift_right, 7, A.bitwise_and)
-    copy("v", r("c01", 0, 8), r("gi", 16, 24))
-    copy("v", r("fr", 0, 64), r("ka", 0, 64))
-    ts(r("fr", 64, 128), r("fr", 0, 64), 31, A.bitwise_and)
+    ts(r("gi", 24, 28), r("gi", 0, 4), 255, A.bitwise_and)
+    copy("v", r("c01", 0, 12), r("gi", 16, 28))
+    copy("v", r("fr", 192, 256), (r("iot", 0, 256), r("c01", 8, 12)))
+    ts(r("fr", 64, 128), r("fr", 192, 256), 31, A.bitwise_and)
     ts(r("mk", 0, 64), r("fr", 64, 128), P32, A.is_equal)
-    ts(r("fr", 128, 192), r("fr", 0, 64), 255, A.bitwise_and)
-    ts(r("fr", 192, 256), r("fr", 128, 192), UP, A.add)
     ts(r("cf", 50, 52), r("iot", 0, 448, 224), UP + LAND0, A.add, P32, A.add)
 
     for h in range(2):
         quant("qb", "sb", 128 * h, 128 * h + 128, r("bb_t", 512 * h, 512 * h + 512))
-    for i in range(4):
-        ts(r("vb", i, 512, 4), r("zb", 0, 128), col("v4", i), A.add, q="s")
-    quant("qv", "sv", 0, 128, r("vb", 0, 512))
-    mm("pf", 0, QV, QB)
-    copy("s", r("fn", 0, 256), r("pf", 0, 256))
-    copy("s", r("ft", 0, 64), (r("fn", 0, 256), r("frt", 0, 4)))
-    tr(r("fn", 0, 64), r("ft", 0, 64))
+    for j in range(5):
+        mm("ps", 512 * j, ("qb", "sb", 32 * j, 32 * j + 128), ("qu", "su", 2, 130))
     const(r("fz", 0, 68), 0.0)
     const(r("fz", 33, 68, 34), 2.0 ** -120)
-    const(r("dz", 65, 130, 64), 0.0)
-    ts(r("fz", 32, 68, 34), r("fn", 0, 64, 32), -1.0, A.mult)
+    put("v", lambda e: g.vector.memset(T.dz[:, :, 63], 0.0), [], [r("dz", 63, 128, 64)])
+    for a in (0, 2, 1, 3):
+        ts(r("fz", 32, 68, 34, 32 * a, 32 * a + 32), r("ps", 512 * a + 126, 512 * a + 639, 512, 32 * a, 32 * a + 32), -1.0, A.mult)
     ts(r("cf", 36, 39), r("iot", 64, 256, 64), B64, A.add, 256.0, A.is_ge)
     ts(r("cf", 32, 35), r("cf", 36, 39), -TINY, A.mult)
-    ts(r("kk", 18, 22), r("iot", 0, 4), 0.25, A.mult)
-    ts(r("kk", 0, 4), r("iot", 0, 4), 0.25, A.mult, 16.0, A.add)
-    const(r("c4", 0, 128), 1.0)
-    const(r("c4", 2, 128, 4), C05)
-    const(r("c4", 3, 128, 4), 0.0)
-    const(r("wm", 0, 96), 1.0)
-    const(r("wm", 0, 96, 8), 0.0)
-    iota(r("fr_", 0, 8), [[8, 4], [40, 2]], 7)
-    iota(r("fr_", 8, 16), [[0, 4], [16, 2]], 79)
-    iota(r("fr_", 16, 24), [[8, 4], [-32, 2]], 39)
-    iota(r("fr_", 24, 32), [[0, 4], [-8, 2]], 87)
+    for b in range(4):
+        copy("s", r("bt", 256 * b, 256 * b + 256), r("bb_t", b, 1024, 4))
+    ts(r("kk", 4, 7), r("iot", 0, 3), 1.0 / 3, A.mult, 0.01, A.add)
+    const(col("kk", 7), 256.01)
+    const(r("c4", 0, 96), 1.0)
+    const(r("c4", 0, 96, 3), 0.0)
+    const(r("sc4", 1, 768, 6), 0.0)
+    const(r("bbs", 0, 256, 2), C05)
+    ts(r("odd", 0, 2), r("lo", 16, 18), 1.0, A.add)
+    const(r("wm", 0, 80), 1.0)
+    const(r("wm", 0, 80, 8), 0.0)
+    iota(r("fr_", 0, 6), [[8, 3], [32, 2]], 7)
+    iota(r("fr_", 6, 16), [[0, 5], [16, 2]], 63)
+    iota(r("fr_", 16, 22), [[8, 3], [-24, 2]], 31)
+    iota(r("fr_", 22, 32), [[0, 5], [-8, 2]], 71)
     tr(r("fr_", 32, 64), r("fr_", 0, 32))
     copy("v", r("fo", 0, 2), r("fr_", 32, 34))
-    ts(r("dv", 96, 128), (IOT, r("jo16", 0, 2)), UP, A.add, q="s")
     iota(r("ol", 0, 256), [[1, 256]], int(UP))
-    iota(r("od", 0, 96), [[1, 96]], int(UP) + OWN0)
-    iota(r("wn", 0, 256), [[0, 256]], 0)
-    iota(r("xt", 128, 512), [[0, 384]], 0)
+    for h in range(2):
+        ts(r("dv", 96 + 16 * h, 112 + 16 * h), r("ol", 32 * h, 32 * h + 16), G16, A.add, q="s")
+    iota(r("od", 0, 96), [[64, 3], [2, 32]], int(UP) + OWN0 + 1)
+    iota(r("wn", 48, 176), [[0, 128]], 0)
+    iota(r("wn", 784, 976, 3), [[0, 64]], 0)
+    iota(r("xt", 256, 512), [[0, 256]], 0)
     iota(r("pat", 40, 56), [[32, 8], [0, 2]], 0)
     ts(r("d8", 0, 16), r("pat", 40, 56), P32, A.add)
 
-    ts(r("fi", 4, 6), r("fi", 0, 2), 8, A.arith_shift_right)
-    ts(r("fa", 12, 14), r("fi", 4, 6), -256.0, A.mult, 0.5, A.add)
+    copy("v", r("fi", 0, 4), r("g1", 2, 6))
+    ts(r("fi", 4, 6), r("fi", 0, 2), 7 * P, A.bitwise_and)
+    ts(r("fi", 6, 8), r("fi", 2, 4), 8, A.arith_shift_right, 7, A.bitwise_and)
+    copy("v", r("fa", 10, 14), r("fi", 4, 8))
     for h in range(2):
-        act(junk(3 + h), FR, F.Sign, bias=col("fa", 12 + h), acc=col("ac", 8 + h))
-    ts(r("fi", 6, 8), r("fi", 4, 6), float(7 - rank), A.add)
-    ts(r("fi", 8, 10), r("fi", 6, 8), 7, A.bitwise_and)
-    ts(r("fa", 14, 16), r("fi", 8, 10), float(LC), A.mult, UP + FAR0, A.add)
-    ts(r("fa", 16, 18), r("fi", 8, 10), 32.0, A.mult)
-    tt(r("ac", 10, 12), r("ac", 8, 10), r("ac", 4, 6), A.subtract)
+        act(junk(3 + h), FR, F.Sign, bias=col("fa", 10 + h), scale=-1.0, acc=col("ac", 8 + h))
+    ts(r("fa", 14, 16), r("fa", 12, 14), float(LC), A.mult, UP + FAR0, A.add, q="s")
+    ts(r("fa", 16, 18), r("fa", 12, 14), 32.0, A.mult, q="s")
+    tt(r("ac", 10, 12), r("ac", 4, 6), r("ac", 8, 10), A.subtract)
     for h in range(2):
-        ts(col("ac", 14 + h), col("ac", 10 + h), 0.5, A.mult, col("fa", 14 + h), A.add)
-        ts(r("sp", 128 + 32 * h, 160 + 32 * h), CONE, col("ac", 14 + h), A.mult)
+        ts(r("sp", 128 + 32 * h, 160 + 32 * h), CHALF, col("ac", 10 + h), A.mult, col("fa", 14 + h), A.add)
     tr(FL, r("sp", 128, 192))
-    ts(r("fl2", 0, 2), r("iot", 0, 64, 32), P32, A.add)
+    copy("v", r("fl2", 0, 2), r("jo", 0, 2))
     copy("s", r("dv", 64, 96), (FL, r("fl2", 0, 2)))
 
-    tr(r("rl2", 0, 32), r("er", 45, 77))
-    o = 16 * (rank % 2)
-    for i in (32, 48):
-        copy("vs"[i // 48], r("rl2", i, i + 16), r("rl2", o, o + 16))
-    tr(r("rl2", 64, 96), r("rl2", 32, 64))
+    for i in (0, 2):
+        put("v", lambda e, i=i: g.vector.transpose(T.rl3[:, i:i + 2, :], ap(r("er", 45, 77))), [r("er", 45, 77)], [r("rl3", 16 * i, 16 * i + 32)])
+    put("v", lambda e: g.vector.transpose(ap(r("rl2", 64, 96)), T.rl3[:, rank % 2:4:2, :]), [r("rl3", 0, 64)], [r("rl2", 64, 96)])
     for a in range(4):
-        ts(blk("rep", 0, 21, a), blk("rl2", 75, 96, rank // 2), 255.0, A.min)
+        ts(blk("rep", 0, 21, a), blk("rl2", 75, 96, rank // 2), -256.0 * rank, A.add, 255.0, A.min)
     pick(r("slc", 0, 336), r("sls", 0, 336), r("qx", 0, 256), r("sx", 0, 256), r("rep", 0, 21))
     for s, l, arr in (("slc", "gq", "ac0"), ("sls", "gs", "as0")):
         send_each([(d, r(s, LC * i, LC * i + LC), r(l, *slot(d, LC, FAR0))) for i, d in enumerate(peers)], arr, r(l, FAR0, LAND0))
@@ -499,20 +474,19 @@ def rank_program(g, core, T, topo):
     copy("s", r("yt", 0, 256), r("py", 0, 256))
 
     for t in range(R):
-        W, at, po = LAND0 + 224 * t, OWN0 + 32 * t, 16 * t
-        ndl = r("po", po + 8, po + 10)
+        W, at, po = LAND0 + 224 * t, OWN0 + 64 * t, 16 * t
+        ndl = r("po", po + 6, po + 8)
         copy("s", r("dv", 0, 64), (r("ol", 0, 256), r("dl", 0, 4)))
-        tt(r("lg", 0, 64), (r("et", 0, 256), r("ll", 0, 4)), r("d16", 0, 64), A.mult)
-        scan(r("dz", 2, 130, 2), r("ft", 64, 128), r("lg", 0, 64), 0.0, A.mult, A.add)
+        tt(r("lg", 0, 64), (r("et", 0, 256), r("dl", 0, 4)), r("d16", 0, 64), A.mult)
+        for h in range(2):
+            scan(r("dz", 47 + 64 * h, 63 + 64 * h), r("lg", 16 * h, 16 * h + 16), r("lg", 32 + 16 * h, 48 + 16 * h), 0.0, A.add, A.add)
         win = (r("er", 72 + 8 * t, 79 + 8 * t), r("c01", 4, 8)) if t else (r("er", 0, 56), r("c01", 0, 4))
         tt(r("tg", 0, 64), win, r("mk", 64 * (t % 2), 64 * (t % 2) + 64), A.mult)
+        put("v", lambda e: g.vector.transpose(T.dz[:, :, 30:62], ap(r("tg", 0, 64))), [r("tg", 0, 64)], [r("dz", 30, 62), r("dz", 94, 126)])
         for h in range(2):
-            tr(r("dz", 32 + 64 * h, 64 + 64 * h), r("tg", 32 * h, 32 * h + 32))
-        for h in range(2):
-            scan(r("zo", 40 * h, 40 * h + 34), r("dz", 32 + 64 * h, 66 + 64 * h), r("fz", 34 * h, 34 * h + 34), col("ok", h) if t else 0.0, A.add, A.add)
+            scan(r("zo", 40 * h, 40 * h + 34), r("dz", 30 + 64 * h, 64 + 64 * h), r("fz", 34 * h, 34 * h + 34), col("ok", h) if t else 0.0, A.add, A.add)
             size(r("sp", 192 + 32 * h, 224 + 32 * h), col("zo", 40 * h + 33))
-        tr(r("z", 0, 64), r("sp", 192, 256))
-        exchange("z")
+        exchange("z", 0, r("sp", 192, 256), 4)
         for h in range(2):
             o, zt = 256 * h, col("sp", 192 + 32 * h)
             ts(r("dd", 64 * h, 64 * h + 64), r("jj", 64 * h, 64 * h + 64), zt, A.mult, zt, A.add, q="s")
@@ -521,52 +495,53 @@ def rank_program(g, core, T, topo):
                 ts(r("mm_", o + 64 * d, o + 64 * d + 64), r("z", 64 * d, 64 * d + 64), zt, A.subtract, col("cf", 31 + d), A.is_gt)
             scan(r("cx", 128 * h, 128 * h + 128), r("mm_", o, o + 128), r("mm_", o + 128, o + 256), 0.0, A.add, A.add)
         if t:
-            const(r("wn", 64, 192), 0.0)
+            const(r("wn", 64, 160), 0.0)
+            const(r("wn", 832, 928, 3), 0.0)
         for h in range(2):
-            ts(r("so", h, 8, 2), r("kk", 0, 4), col("cx", 128 * h + 127), A.add, 4.0, A.mult)
-        scatter(r("wn", 0, 1088), r("so", 0, 8), r("dv", 0, 128))
-        tr(r("wt_", 0, 128), r("wn", 64, 192))
-        tr(r("wt_", 128, 288), r("wn", 48, 208))
-        tr(r("wt_", 288, 320), r("wn", 67, 192, 4))
-        tr(r("wt_", 320, 384), r("wn", 3, 256, 4))
-        copy("v", r("wx", 0, 96, 4), r("wt_", 0, 384, 16))
+            ts(r("so", h, 8, 2), r("kk", 4, 8), col("cx", 128 * h + 127), A.add, 3.0, A.mult)
+        scatter(r("wn", 64, 1600), r("so", 0, 8), r("dv", 0, 128))
+        tr(r("wt_", 0, 96), r("wn", 64, 160))
+        tr(r("wt_", 96, 224), r("wn", 48, 176))
+        tr(r("wt_", 224, 256), r("wn", 832, 928, 3))
+        tr(r("wt_", 256, 320), r("wn", 784, 976, 3))
+        copy("v", r("wx", 0, 80, 4), r("wt_", 0, 320, 16))
         for d in (1, 3):
             for a in range(4):
                 b = (a + d) % 4
-                copy("vs"[a % 2], r("wx", d, 96, 4, 32 * a, 32 * a + 32), r("wt_", 0, 384, 16, 32 * b, 32 * b + 32))
-        copy("s", r("wx", 2, 96, 4, 0, 64), r("wt_", 0, 384, 16, 64, 128))
-        copy("s", r("wx", 2, 96, 4, 64, 128), r("wt_", 0, 384, 16, 0, 64))
-        scan(r("sm", 0, 96), r("wm", 0, 96), r("wx", 0, 96), 0.0, A.mult, A.add)
-        ts(r("po", po, po + 16), (r("sm", 0, 96), r("fo", 0, 1)), -UP, A.add)
-        ts(r("nd_", po, po + 16), (r("sm", 0, 96), r("fo", 0, 1)), -UP, A.add, q="s")
+                copy("vs"[a % 2], r("wx", d, 80, 4, 32 * a, 32 * a + 32), r("wt_", 0, 320, 16, 32 * b, 32 * b + 32))
+        copy("s", r("wx", 2, 80, 4, 0, 64), r("wt_", 0, 320, 16, 64, 128))
+        copy("s", r("wx", 2, 80, 4, 64, 128), r("wt_", 0, 320, 16, 0, 64))
+        scan(r("sm", 0, 80), r("wm", 0, 80), r("wx", 0, 80), 0.0, A.mult, A.add)
+        ts(r("po", po, po + 16), (r("sm", 0, 80), r("fo", 0, 1)), -UP, A.add)
+        ts(col("ok", 4 + t), col("sm", 63), -UP, A.add, q="s")
         if t < 2:
-            send_all(col("sm", 79), "an", 8 * t, "an%d" % t)
+            send_all(col("ok", 4 + t), "an", 8 * t, "an%d" % t)
         nq, ns = "nq%d" % t, "ns%d" % t
-        pick(r(nq, 0, 128), r(ns, 0, 128), r("gq", 0, W), r("gs", 0, W), r("po", po, po + 8))
+        pick(r(nq, 0, 96), r(ns, 0, 96), r("gq", 0, W), r("gs", 0, W), r("po", po, po + 6))
         for b in range(4):
             mm("ps", 512 * b, ("qa", "sa", 128 * b, 128 * b + 128), (nq, ns, 0, 128))
-        for c in range(2):
-            ts(r("bo", c, 8, 2), r("kk", 18, 22), col("nd_", po + 8 + c), A.add, 4.0, A.mult)
-        copy("s", r("bbs", 0, 128), (r("bb_t", 0, 1024), r("bo", 0, 8)))
+        for b in range(4):
+            copy("s", r("bbs", 64 * b + 1, 64 * b + 64, 2), (r("bt", 256 * b, 256 * b + 256), ndl))
         scatter(r("ol", 0, 256), ndl, r("od", 32 * t, 32 * t + 32))
         for b in range(4):
-            scan(r("sc4", 128 * b, 128 * b + 128), r("ps", 512 * b, 512 * b + 128), r("c4", 0, 128), 0.0, A.add, A.mult)
+            scan(r("sc4", 192 * b, 192 * b + 192, 2), r("c4", 0, 96), r("ps", 512 * b, 512 * b + 96), 0.0, A.mult, A.add)
         for b in range(4):
-            tt(r("xt", b, 128, 4), r("sc4", 128 * b + 2, 128 * b + 128, 4), r("bbs", 32 * b, 32 * b + 32), A.add)
-        quant("gq", "gs", at, at + 128, r("xt", 0, 512))
-        new = ("gq", "gs", at, at + 128)
+            scan(r("xt", b, 256, 4), r("sc4", 192 * b + 1, 192 * b + 192, 3), r("bbs", 64 * b, 64 * b + 64), 0.0, A.mult, A.add)
+        new = ("xq%d" % t, "xs%d" % t, 0, 128) if t < 2 else ("gq", "gs", at, at + 128)
+        quant(*new, r("xt", 0, 512))
         if t < 2:
             mm("px", 0, QU, new)
-            tr(r("ec", 32 * t, 32 * t + 32), r("px", 0, 32))
+            tr(r("ec", 32 * t, 32 * t + 32), r("px", 1, 64, 2))
             send_all(col("ec", 32 * t), "er", 80 + 8 * t, "ae%d" % t)
-            for n, arr in (("gq", "ac%d" % (t + 1)), ("gs", "as%d" % (t + 1))):
-                send_all(r(n, at, at + 32), n, W, arr)
-            copy("s", r("nw", 0, 32), r("px", 0, 32))
+            pick(r("sq%d" % t, 0, 32), r("ss%d" % t, 0, 32), r(new[0], 0, 64), r(new[1], 0, 64), r("odd", 0, 2))
+            for s, n, arr in (("sq%d" % t, "gq", "ac%d" % (t + 1)), ("ss%d" % t, "gs", "as%d" % (t + 1))):
+                send_all(r(s, 0, 32), n, W, arr)
+            quant("gq", "gs", at, at + 128, r("xt", 0, 512))
+            copy("s", r("nw", 0, 32), r("px", 1, 64, 2))
             scatter(r("et", 0, 256), ndl, r("nw", 0, 32))
         mm("py", 0, QW, new)
-        copy("s", r("nw", 32, 64), r("py", 0, 32))
+        copy("s", r("nw", 32, 64), r("py", 1, 64, 2))
         scatter(r("yt", 0, 256), ndl, r("nw", 32, 64))
-        ts(col("ok", 4 + t), col("sm", 79), -UP, A.add, q="s")
         dma([("y", T.nd[t:t + 1, :], r("ok", 4 + t, 5 + t, 1, 0, 32))])
         if t < 2:
             m = r("mk", 64 * ((t + 1) % 2), 64 * ((t + 1) % 2) + 64)
@@ -586,7 +561,7 @@ def rank_program(g, core, T, topo):
         tr(r("ogt", c, c + 128), r("og", c, c + 128))
         ts(r("oo", c // 16, c // 16 + 8), r("ogt", c, c + 128, 16), -UP, A.add)
         pick(r("occ", c, c + 128), r("ocs", c, c + 128), r("gq", 0, FAR0), r("gs", 0, FAR0), r("oo", c // 16, c // 16 + 8))
-    dma([("y", T.oc[:], r("occ", 0, 256))])
+        dma([("y", T.oc[:, 4 * c:4 * c + 512], r("occ", c, c + 128))])
     dma([("y", T.osc[4 * k:4 * k + 4, :], r("ocs", 0, 256, 1, 32 * k, 32 * k + 4)) for k in range(4)])
     dma([("s", T.y[:], r("yt", 0, 256))])
     flush()

from concourse.bass import DstId, RemoteDMATransfer
from concourse.mybir import dt, AluOpType, AxisListType, ActivationFunctionType

A = AluOpType
F = ActivationFunctionType
P, K, R, LC = 256, 32, 3, 48
OWN0, FAR0, LAND0 = 256, 512, 848
UP = 4096.0
C05 = 13421773 * 2.0 ** -28
TINY = 2.0 ** -110
ORDER = """
1y 24 4s 0s 45v 25 2 3y 5 28 26 7 6 183 27 176 29 56v 173 159 11y 161 30 53 8y 10 49 141 48 50 52v 40 31 58 44 37s 32s 16 35s 36s 111 39 33 41 34 42
38v 62 60 61 63 46 112 43 64 65 20 47 15y 51s 54 113 66 110 160 109 114 115 143 21y 59 196 122 67 166 70 9 68 198 182 197 69 187 71s 72s 55 73 116
13y 117 178 139 19y 136s 74 83 18 12 199 14 17y 181 77 145 146 76 75 84 80 151 79v 78 82 81 86 153 144 158 132 123 135 140 85 152 156 133 22 154 89
88 147 134 87 137 201 155 91 92 157 93 102 208 126 101 192 23 94 100v 125 97v 99v 127 98v 118 231 169v 148 96 95 162s 184 233 185 163s 107 108 149 90
103 105 202 104 150 57 200 119 232 106 234 120 204 138 235 164s 205 165s 167s 129s 230 206 128s 236 179 238 191 188 207 237v 124s 189 251 130s 172s
239v 227 193 240 241 257 245 246 247 250 248 242 244 243 252 260 228 249 254 121 210 211 258 261 212 255 174 209 253 259 213 215 216 131s 175 214 142
256 262 168 263 180 218 190 264 217 265 225 268 267 266 269 221 177 219 280v 278v 270 271 273s 275s 272v 274v 186 171v 277s 279 276 281 223 283 284
366 282 222 226 287 220 286 170v 224 291 296 300 293 194 285 288 297 290 299 289 295 298 203 294 304 292 303 322 301 302 305 229 323 306 195 311v 307
324s 319 308 325 326 317 318 328 330s 309 327 334 316 335 329 336 337 331 338 310 341 339 340v 342 332 343 345 360 344 354 314 347 346 355 348 357
363 349 352 364 353 350 351 361 358 356 362 367 333 359 365 368 369 370 372 373 371 374 379v 380s 385v 378 312 376 382 377 384v 313 383 375s 381 386
387 320 472v 391 315 321 392 396 395 394 393 397 388 401 405 400 404 403 402 399 409 408 389 398 438 407 406 410 390 428 411 429s 416 412 422v 430
423 427 413 431 439 414 434 415 435s 433s 424 425v 441 440 442 436 432 443 437 446 447 471 465 444 445v 448 452 449 459 451 453 456 450 454 460 457
455 466 458 462 463 469 468 467 461 470 464 474 473 475 478 479 477 476 481s 480s 489v 483 482 485 484v 488v 490v 419 420 487s 486 491 421 417 493
492 426 418 494 495 517 504 496 502v 505 497 501 500 518 503 498 506 507 499 509 508 519 510 511 512 524 520 525 513 526 522 521 523 527 514 515 516
529 528 531s 534y 530s 532 533
"""
CODE, U8, BF, F32, I32, U16 = "float8_e4m3fn_x4", "uint8", "bfloat16", "float32", "int32", "uint16"


def _sbuf(dtype, **cols):
    return {n: ("sbuf", [128, c], dtype) for n, c in cols.items()}


SCRATCH = {"pe": ("psum", [128, 512], F32), "ps": ("psum", [128, 2560], F32), "py": ("psum", [128, 512], F32),
           "px": ("psum", [128, 512], F32)}
SCRATCH.update(_sbuf(F32, tf=32, g1=16, s2=192, iot=2048, jf=256, cf=64, jo=8, ka=256, junk=2304, cq=768, cz=384, ac=32, fa=28, sp=256, ex=576, cc=160,
                     lo=24, z=256, dd=128, jj=128, c4=288, wn=1600, wt_=480, dv=128, kk=8, bbs=256, sc4=768, an=16, od=96,
                     og=256, ogt=256, yt=256, ept=256, ep=8, ec=64, er=96, rl2=96, et=256, ol=256, mk=128, tg=64, lg=64,
                     fz=72, zo=80, ok=8, rel=192, ft=128, d16=128, nw=64, pat=64))
SCRATCH.update(_sbuf(I32, ci=16, fi=16, gi=32, fr=256))
SCRATCH.update(_sbuf(U16, go=4, dl=4, odd=2, far16=16, rep=24, so=8, po=48, c01=12, fl2=2, fo=2, d8=16, oo=16))
SCRATCH.update(_sbuf(BF, xb=1024, bt=1024, bb_t=1024, at=2048, wt=512, u4=4, ub=520, m2=320, mm_=512, xt=512, cx=256, zb=128))
for _c, _s, _n in (("qx", "sx", 256), ("qb", "sb", 256), ("qu", "su", 130), ("qa", "sa", 512), ("qw", "sw", 128), ("slc", "sls", 336),
                   ("gq", "gs", 1296), ("xq0", "xs0", 128), ("xq1", "xs1", 128), ("sq0", "ss0", 32), ("sq1", "ss1", 32),
                   ("nq0", "ns0", 128), ("nq1", "ns1", 128), ("nq2", "ns2", 128), ("occ", "ocs", 256)):
    SCRATCH.update({_c: ("sbuf", [128, _n], CODE), _s: ("sbuf", [128, _n], U8)})
SCRATCH.update({"rl3": ("sbuf", [128, 4, 16], F32), "dz": ("sbuf", [128, 2, 64], F32), "nb32": ("sbuf", [128, 3, 48], I32)})
SEMAPHORES = ["cv", "cs", "ct", "cg"] + ["q%d" % i for i in range(40)] + ["aer", "arl", "ac0", "as0", "an0", "an1", "ae0", "ae1", "ac1", "as1", "ac2", "as2"]
PARTS = {"wm": ("c4", 128), "fr_": ("c4", 224), "wx": ("wt_", 320), "sm": ("wt_", 400)}


def r(name, c0, c1, step=1, p0=0, p1=128):
    name, o = PARTS.get(name, (name, 0))
    return (name, c0 + o, c1 + o, step, p0, p1)


def rank_program(g, core, T, topo):
    rank = T.rank_of(core)
    if rank is None:
        return
    eng = {"v": g.vector, "s": g.scalar, "t": g.tensor, "g": g, "y": g.sync}
    csem = {"v": "cv", "s": "cs", "t": "ct", "g": "cg"}
    cnt, known, log, pool, snaps, ops = {}, {q: {} for q in eng}, {}, [0], {}, []

    def ap(x):
        if len(SCRATCH[x[0]][1]) == 3:
            w = SCRATCH[x[0]][1][2]
            return T[x[0]][x[4]:x[5], x[1] // w, x[1] % w:x[2] - x[1] // w * w:x[3]]
        return T[x[0]][x[4]:x[5], x[1]:x[2]:x[3]] if x[3] != 1 else T[x[0]][x[4]:x[5], x[1]:x[2]]

    def span(x):
        if SCRATCH[x[0]][0] == "psum":
            return x[1] // 512 * 512, (x[2] + 511) // 512 * 512, 0, 128
        return x[1], x[2], x[4], x[5]

    def learn(q, tok):
        k, (sem, c) = known[q], tok
        if k.get(sem, 0) >= c:
            return
        k[sem] = c
        for n, m in snaps.get(tok, {}).items():
            if k.get(n, 0) < m:
                k[n] = m

    def clash(a, b):
        return not (a[3] == b[3] and a[3] > 1 and (a[1] - b[1]) % a[3])

    def meets(reads, writes, q):
        deps = set()
        for x, w in [(x, 0) for x in reads] + [(x, 1) for x in writes]:
            s = span(x)
            bank = SCRATCH[x[0]][0] == "psum"
            for y, t, w2, i, q2 in log.get(x[0], []):
                if (w or w2 or bank) and s[0] < t[1] and t[0] < s[1] and s[2] < t[3] and t[2] < s[3] and clash(x, y):
                    deps.add(i)
        return deps

    def note(q, reads, writes, i):
        for x in writes:
            s = span(x)
            if x[3] == 1:
                log[x[0]] = [e for e in log.get(x[0], []) if not (s[0] <= e[1][0] and e[1][1] <= s[1] and s[2] <= e[1][2] and e[1][3] <= s[3])]
            log.setdefault(x[0], []).append((x, s, 1, i, q))
        for x in reads:
            log.setdefault(x[0], []).append((x, span(x), 0, i, q))

    def put(q, fn, reads, writes, sem=None, inc=1, deps=(), alt=""):
        i = len(ops)
        ops.append({"q": q, "fn": fn, "deps": meets(reads, writes, q) | set(deps), "sem": sem, "inc": inc, "alt": alt, "peers": [i]})
        note(q, reads, writes, i)
        return i

    def width(x):
        return -(-(x[2] - x[1]) // x[3])

    def flush():
        for i, o in enumerate(ops):
            for k in list(o["deps"]):
                o["deps"] |= set(ops[k]["peers"])
            o["deps"].discard(i)
        out = [int(x.rstrip("vsy")) for x in ORDER.split()] or list(range(len(ops)))
        for x in ORDER.split():
            if x[-1] in "vsy":
                ops[int(x[:-1])]["q"] = x[-1]
        tok = {}
        for i in out:
            o = ops[i]
            q = o["q"]
            need = {}
            if q == "g" and o["sem"] is None and "cg" in cnt:
                need["cg"] = cnt["cg"]
            for k in o["deps"]:
                need[tok[k][0]] = max(need.get(tok[k][0], 0), tok[k][1])
            if q != "r":
                for sem, c in sorted(need.items(), key=lambda e: -sum(snaps.get(e, {}).values())):
                    if known[q].get(sem, 0) < c:
                        eng[q].wait_ge(T.sem[sem], c)
                        learn(q, (sem, c))
            sem = o["sem"] or csem[q]
            cnt[sem] = cnt.get(sem, 0) + 1 if o["sem"] is None else o["inc"]
            tok[i] = (sem, cnt[sem])
            if q != "r":
                s = snaps.setdefault(tok[i], {})
                for n, m in known[q].items():
                    s[n] = max(s.get(n, 0), m)
                c = o["fn"](q)
                if o["sem"] is None:
                    c.then_inc(T.sem[sem], 1)

    def newsem():
        pool[0] += 1
        return "q%d" % (pool[0] - 1)

    def src(x):
        if len(x) == 2:
            return ap(x[0]).indirect(ap(x[1])), [x[0], x[1]]
        return ap(x), [x]

    def sc(x):
        return (ap(x), [x]) if isinstance(x, tuple) else (x, [])

    def copy(q, out, in_):
        i, rd = src(in_)
        flex = all(SCRATCH[k][2] in (F32, BF) for k in (out[0], rd[0][0]))
        put(q, lambda e: g.vector.tensor_copy(ap(out), i) if e == "v" else g.scalar.activation(ap(out), i, F.Copy), rd, [out], alt="vs" if flex else "")

    def scatter(win, off, in_):
        put("v", lambda e: g.vector.tensor_copy(ap(win).indirect(ap(off)), ap(in_)), [in_, off], [win])

    def act(out, in_, func, bias=0.0, scale=1.0, acc=None):
        i, rd = src(in_)
        b, rb = sc(bias)
        s, rs = sc(scale)
        put("s", lambda e: g.scalar.activation(ap(out), i, func, bias=b, scale=s, accum_out=acc and ap(acc)), rd + rb + rs, [out] + ([acc] if acc else []))

    def const(out, val):
        i = r("zb", 0, width(out), 1, out[4], out[5])
        put("s", lambda e: g.vector.memset(ap(out), val) if e == "v" else g.scalar.activation(ap(out), ap(i), F.Copy, bias=val, scale=0.0), [i], [out], alt="vs")

    def ts(out, in_, s1, op0, s2=None, op1=None, q="v"):
        i, rd = src(in_)
        a, ra = sc(s1)
        b, rb = sc(s2)
        both = all(SCRATCH[x[0]][2] in (F32, BF) for x in (out, rd[0])) and (op0, op1) in ((A.add, None), (A.mult, None), (A.mult, A.add))
        mul, add = (1.0, a) if op0 == A.add else (a, 0.0 if op1 is None else b)
        put(q, lambda e: g.vector.tensor_scalar(ap(out), i, a, b, op0, *([] if op1 is None else [op1])) if e == "v" else
            g.scalar.activation(ap(out), i, F.Copy if isinstance(add, float) else F.Identity, bias=add, scale=mul), rd + ra + rb, [out], alt="vs" if both else "")

    def size(out, c):
        i = r("cc", 64, 96)
        put("s", lambda e: g.vector.tensor_scalar(ap(out), ap(i), ap(c), ap(c), A.mult, A.max) if e == "v" else
            g.scalar.activation(ap(out), ap(i), F.Abs, scale=ap(c)), [i, c], [out], alt="vs")

    def tt(out, in0, in1, op):
        i, rd = src(in0)
        put("v", lambda e: g.vector.tensor_tensor(ap(out), i, ap(in1), op), rd + [in1], [out])

    def scan(out, d0, d1, initial, op0, op1):
        a, ra = sc(initial)
        put("v", lambda e: g.vector.tensor_tensor_scan(ap(out), ap(d0), ap(d1), a, op0, op1), [d0, d1] + ra, [out])

    def tr(out, in_):
        return put("v", lambda e: g.vector.transpose(ap(out), ap(in_)), [in_], [out])

    def fill(out, val):
        put("v", lambda e: g.vector.memset(ap(out), val), [], [out])

    def quant(q, s, c0, c1, in_):
        put("v", lambda e: g.vector.quantize_mx(ap(r(q, c0, c1)), ap(r(s, c0, c1)), ap(in_)), [in_], [r(q, c0, c1), r(s, c0, c1)])

    def mm(bank, at, w, x):
        out, rd = r(bank, at, at + x[3] - x[2]), [r(w[0], w[2], w[3]), r(w[1], w[2], w[3]), r(x[0], x[2], x[3]), r(x[1], x[2], x[3])]
        put("t", lambda e: g.tensor.matmul_mx(ap(out), ap(rd[0]), ap(rd[1]), ap(rd[2]), ap(rd[3]), True, True), rd, [out])

    def iota(out, pattern, base, cm=0):
        put("g", lambda e: g.iota(ap(out), pattern, base, cm, allow_small_or_imprecise_dtypes=SCRATCH[out[0]][2] != I32), [], [out])

    def pick(qo, so, win, wins, off):
        put("v", lambda e: g.vector.tensor_copy(ap(qo).bitcast(dt.uint32), ap(win).bitcast(dt.uint32).indirect(ap(off))), [win, off], [qo])
        put("s", lambda e: g.vector.tensor_copy(ap(so), ap(wins).indirect(ap(off))) if e == "v" else
            g.scalar.activation(ap(so), ap(wins).indirect(ap(off)), F.Copy), [wins, off], [so], alt="vs")

    def side(x):
        return ap(x).bitcast(dt.uint8) if SCRATCH[x[0]][2] == CODE else ap(x)

    def dma(moves):
        sem = newsem()
        made = []
        for q, out, in_ in moves:
            wr = [out] if isinstance(out, tuple) else []
            rd = [in_] if isinstance(in_, tuple) else []
            o, i = side(out) if wr else out, side(in_) if rd else in_
            made.append(put(q, lambda e, o=o, i=i: eng[e].dma_start(o, i).then_inc(T.sem[sem], 16), rd, wr, sem, 16 * len(moves), alt="ys"))
        for k in made:
            ops[k]["peers"] = made

    peers = [(rank + 1 + i) % 8 for i in range(7)]
    ids = {}
    for d in peers:
        rid, pid, _ = topo.addr(T.cores[d])
        ids[d] = DstId(rid=rid, pnc=pid)
    full = topo.engines(core, T.cores[peers[0]])
    across = [d for d in peers if topo.die(T.cores[d]) != topo.die(core)]
    masks = {}
    for d in peers:
        e = topo.engines(core, T.cores[d])
        lane = e[0::2] if d in across else e[1::2]
        k = (across if d in across else [s for s in peers if s not in across]).index(d)
        masks[d] = sum(1 << x for x in lane[2 * k:2 * k + 2])

    def issue(trs, reads, total):
        sem = newsem()
        return put("g", lambda e: g.remote_dma_fused(trs, local_sem=T.sem[sem]), reads, [], sem, total)

    def send_each(moves, arr, region):
        i = issue([RemoteDMATransfer(dst_ids=[ids[d]], dma_engine_mask=masks[d], remote_sem=T.sem[arr], srcs=[side(s)], dsts=[side(l)]) for d, s, l in moves],
                  [m[1] for m in moves], 2 * len(moves))
        put("r", None, [], [region], arr, 2 * 7, [i])

    def send_all(s, name, base, arr):
        w = width(s)
        i = issue([RemoteDMATransfer(dst_ids=[ids[d] for d in peers], dma_engine_mask=sum(1 << x for x in full), remote_sem=T.sem[arr], srcs=[side(s)],
                                     dsts=[side(r(name, *slot(d, w, base))) for d in peers])], [s], len(full))
        put("r", None, [], [r(name, base, base + 7 * w)], arr, len(full) * 7, [i])

    def slot(d, w, base):
        q = base + w * ((rank - d - 1) % 8)
        return q, q + w

    def exchange(n, o, src, nv):
        tr(r(n, o, o + 64), src)
        for k, (d, p, q, w) in enumerate([(2, 0, 64, 64), (2, 64, 0, 64)] + [(d, 32 * a, 32 * ((a + d) % 4), 32) for d in (3, 1) for a in range(4)]):
            out = r(n, o + 64 * d, o + 64 * d + 64, 1, p, p + w)
            if k < nv:
                tr(out, r(src[0], src[1], src[2], 1, q, q + w))
            else:
                copy("s", out, r(n, o, o + 64, 1, q, q + w))

    def col(n, c):
        return r(n, c, c + 1)

    def blk(n, c0, c1, a):
        return r(n, c0, c1, 1, 32 * a, 32 * a + 32)

    def junk(i):
        return r("junk", 256 * i, 256 * i + 256)

    QX, QU, QW = ("qx", "sx", 0, 256), ("qu", "su", 0, 128), ("qw", "sw", 0, 128)
    IOT = r("iot", 0, 2048)

    def table(k, c0, on):
        moves = []
        for p in (0, 16):
            q = 0
            while q < 16:
                s, row = divmod(3 * q + k, 16)
                n = len(range(row, 16, 3))
                moves.append(("ys"[len(moves) % 2], r("nb32", c0, c0 + 46 - on * p // 16, 1, p + q, p + q + n), T.nb[row:16:3, s + on * p // 16:s + 46]))
                q += n
        return moves

    dma(table(2, 0, 0))
    dma([("y", r("xb", 0, 1024), T.x[:])])
    dma([("s", r("u4", 0, 4), T.u[:, 0:4])])
    dma([("s", r("ub", 512, 520), T.v[:, 0:8])])
    dma([("y", r("bb_t", 0, 1024), T.bb[:])])
    dma(table(0, 48, 3) + table(1, 96, 3))
    dma([("y", r("at", 0, 2048), T.a[:])])
    dma([("y", r("wt", 0, 512), T.w[:])])

    C2048, CHALF, CONE, CBIG = r("cc", 0, 32), r("cc", 32, 64), r("cc", 96, 128), r("cc", 128, 160)
    PP, P32, P16, B64, G16 = col("cf", 0), col("cf", 1), col("cf", 2), col("cf", 26), col("cf", 43)
    TURN = 2048.0 - 256.0 * (rank + 1)
    fill(r("zb", 0, 128), 0.0)
    iota(col("ci", 0), [[0, 1]], 0, 1)
    iota(r("iot", 0, 256), [[1, 256]], 0)
    iota(r("iot", 1792, 2048), [[1, 256]], 1792)
    ts(col("ci", 1), col("ci", 0), 31, A.bitwise_and)
    ts(col("ci", 2), col("ci", 0), 15, A.bitwise_and)
    copy("v", r("cf", 0, 3), r("ci", 0, 3))
    ts(B64, PP, P32, A.subtract, 2.0, A.mult)
    for c in range(256, 1792, 256):
        ts(r("iot", c, c + 256), r("iot", 0, 256), float(c), A.add)
    ts(r("jf", 0, 256), r("iot", 0, 256), 1.0 / 512, A.mult, 1.0 / 1024, A.add, q="s")
    ts(G16, P32, P16, A.subtract, B64, A.add)
    ts(col("ci", 3), col("ci", 0), 1, A.bitwise_and)
    ts(col("cf", 4), col("ci", 3), 32.0, A.mult, G16, A.add)
    ts(col("go", 0), col("cf", 4), 1.0 / 16, A.mult)
    ts(col("go", 2), B64, 1.0 / 16, A.mult, P16, A.add)
    ts(col("cf", 3), PP, 2.0, A.mult, P32, A.subtract)
    const(r("tf", 18, 32), 0.0)
    ts(r("tf", 16, 18), r("iot", 0, 64, 32), col("cf", 3), A.add, 1.0 / 512, A.mult)
    const(r("tf", 20, 22), TURN)
    const(col("tf", 22), 0.5 + 2.0 ** 21 * (0.25 + 1.0 / 1024))
    const(col("tf", 23), 0.5)
    const(col("tf", 24), -2.0 ** 19)
    ts(col("tf", 26), col("tf", 16), -0.25, A.add)
    const(r("m2", 256, 320), 0.0)
    const(C2048, 2048.0)
    const(CBIG, -2.0 ** 21)
    const(CHALF, 0.5)
    const(CONE, 1.0)
    const(r("cc", 64, 96), -1.0)
    ts(col("cf", 16), PP, P16, A.subtract, 16.0, A.mult)
    ts(r("lo", 16, 19), r("iot", 0, 48, 16), P16, A.add, 2.0, A.mult)

    for a in range(4):
        copy("v", blk("far16", 0, 16, a), r("nb32", 0, 46, 3, 0, 32))
    copy("v", r("tf", 0, 16), r("far16", 0, 16))
    tt(r("ka", 0, 256), (IOT, r("far16", 0, 16)), r("jf", 0, 256), A.add)
    tt(r("g1", 0, 16), (r("tf", 0, 16), col("go", 0)), r("tf", 16, 32), A.add)
    act(junk(0), r("ka", 0, 256), F.Abs, bias=col("g1", 10), scale=-1.0)
    act(junk(7), r("ka", 0, 256), F.Sign, bias=col("g1", 3), scale=-1.0, acc=col("ac", 18))
    act(junk(6), r("ka", 0, 256), F.Sign, bias=col("g1", 1), scale=-1.0, acc=col("ac", 1))
    scan(r("junk", 256, 384), r("junk", 0, 128), r("junk", 128, 256), 1.0, A.min, A.min)
    ts(col("ac", 7), col("ac", 18), -2048.0, A.mult, col("g1", 7), A.add)
    ts(r("sp", 0, 32), CBIG, col("junk", 383), A.mult, col("g1", 6), A.add)
    ts(r("sp", 32, 64), C2048, col("ac", 1), A.mult, col("ac", 7), A.add, q="s")
    exchange("ex", 0, r("sp", 0, 64), 2)
    FR, CR2, FL = r("ex", 0, 256), r("ex", 256, 512), r("ex", 512, 576)
    ts(r("m2", 0, 256), FR, col("g1", 2), A.is_lt, 4096.0, A.mult)
    act(junk(2), FR, F.Sign, bias=col("g1", 3), scale=-1.0, acc=col("ac", 5))
    act(junk(8), FR, F.Sign, bias=col("cf", 16), scale=-1.0, acc=col("ac", 19))
    scan(r("s2", 0, 160), r("m2", 0, 320, 2), r("m2", 1, 320, 2), col("g1", 8), A.add, A.add)
    ts(r("s2", 160, 192), C2048, col("ac", 5), A.mult, col("g1", 3), A.add, q="s")
    ts(col("ac", 4), col("s2", 159), col("g1", 2), A.subtract, 1.0 / 2048, A.mult)
    exchange("ex", 256, r("s2", 128, 192), 1)
    ts(r("lo", 0, 3), r("lo", 16, 19), col("ac", 19), A.add, -2048.0, A.mult)
    for c in range(3):
        act(r("cq", 256 * c, 256 * c + 256), CR2, F.Abs, bias=col("lo", c))
        scan(r("cz", c, 384, 3), r("cq", 256 * c, 256 * c + 128), r("cq", 256 * c + 128, 256 * c + 256), 4096.0, A.min, A.min)

    quant("qx", "sx", 0, 256, r("xb", 0, 1024))
    for i in range(4):
        ts(r("ub", i, 512, 4), r("zb", 0, 128), col("u4", i), A.add, q="s")
    quant("qu", "su", 0, 130, r("ub", 0, 520))
    mm("pe", 0, QU, QX)
    tr(r("ept", 0, 256), r("pe", 0, 256))
    copy("s", r("ep", 0, 8), r("ept", 0, 256, 32))
    send_all(r("ep", 0, 8), "er", 0, "aer")
    send_all(r("cz", 381, 384), "er", 56, "arl")
    mm("px", 0, QU, QX)
    copy("s", r("et", 0, 256), r("px", 0, 256))
    dma([("y", r("gq", 0, 256), r("qx", 0, 256)), ("y", r("gs", 0, 256), r("sx", 0, 256))])

    dma([("y", r(n % t, 96, 128), r(s, 0, 32)) for t in range(R) for n, s in (("nq%d", "qx"), ("ns%d", "sx"))])

    for a in range(4):
        put("v", lambda e, a=a: g.vector.tensor_scalar(ap(blk("dl", 0, 4, a)), T.nb32[0:32, 1:3, 12 * a:12 * a + 7:6], -256.0 * rank, None, A.add),
            [r("nb32", 48, 144, 1, 0, 32)], [blk("dl", 0, 4, a)])
    ts(r("jo", 0, 2), r("iot", 0, 64, 32), P32, A.add)
    for h in range(2):
        ts(r("jj", 64 * h, 64 * h + 64), r("iot", 0, 64), col("jo", h), A.is_lt, -2.0 ** -24, A.mult)
    iota(r("d16", 64, 128), [[0, 4], [1, 16]], 0)
    ts(r("d16", 0, 64), r("d16", 64, 128), P16, A.is_equal)
    const(r("ft", 64, 128), 1.0)
    const(r("ft", 64, 128, 32), 0.0)
    ts(r("gi", 0, 16), (r("tf", 0, 32), col("go", 2)), TURN, A.add)
    ts(r("gi", 16, 20), r("gi", 0, 4), 5, A.arith_shift_right, 63, A.bitwise_and)
    ts(r("gi", 20, 24), r("gi", 0, 4), 8, A.arith_shift_right, 7, A.bitwise_and)
    ts(r("gi", 24, 28), r("gi", 0, 4), 255, A.bitwise_and)
    copy("v", r("c01", 0, 12), r("gi", 16, 28))
    copy("v", r("fr", 192, 256), (r("iot", 0, 256), r("c01", 8, 12)))
    ts(r("fr", 64, 128), r("fr", 192, 256), 31, A.bitwise_and)
    ts(r("mk", 0, 64), r("fr", 64, 128), P32, A.is_equal)
    ts(r("cf", 50, 52), r("iot", 0, 448, 224), UP + LAND0, A.add, P32, A.add)

    for h in range(2):
        quant("qb", "sb", 128 * h, 128 * h + 128, r("bb_t", 512 * h, 512 * h + 512))
    for j in range(5):
        mm("ps", 512 * j, ("qb", "sb", 32 * j, 32 * j + 128), ("qu", "su", 2, 130))
    const(r("fz", 0, 68), 0.0)
    const(r("fz", 33, 68, 34), 2.0 ** -120)
    put("v", lambda e: g.vector.memset(T.dz[:, :, 63], 0.0), [], [r("dz", 63, 128, 64)])
    for a in (0, 2, 1, 3):
        ts(r("fz", 32, 68, 34, 32 * a, 32 * a + 32), r("ps", 512 * a + 126, 512 * a + 639, 512, 32 * a, 32 * a + 32), -1.0, A.mult)
    ts(r("cf", 36, 39), r("iot", 64, 256, 64), B64, A.add, 256.0, A.is_ge)
    ts(r("cf", 32, 35), r("cf", 36, 39), -TINY, A.mult)
    for b in range(4):
        copy("s", r("bt", 256 * b, 256 * b + 256), r("bb_t", b, 1024, 4))
    ts(r("kk", 4, 7), r("iot", 0, 3), 1.0 / 3, A.mult, 0.01, A.add)
    const(col("kk", 7), 256.01)
    const(r("c4", 0, 96), 1.0)
    const(r("c4", 0, 96, 3), 0.0)
    const(r("sc4", 1, 768, 6), 0.0)
    const(r("bbs", 0, 256, 2), C05)
    ts(r("odd", 0, 2), r("lo", 16, 18), 1.0, A.add)
    const(r("wm", 0, 80), 1.0)
    const(r("wm", 0, 80, 8), 0.0)
    iota(r("fr_", 0, 6), [[8, 3], [32, 2]], 7)
    iota(r("fr_", 6, 16), [[0, 5], [16, 2]], 63)
    iota(r("fr_", 16, 22), [[8, 3], [-24, 2]], 31)
    iota(r("fr_", 22, 32), [[0, 5], [-8, 2]], 71)
    tr(r("fr_", 32, 64), r("fr_", 0, 32))
    copy("v", r("fo", 0, 2), r("fr_", 32, 34))
    iota(r("ol", 0, 256), [[1, 256]], int(UP))
    for h in range(2):
        ts(r("dv", 96 + 16 * h, 112 + 16 * h), r("ol", 32 * h, 32 * h + 16), G16, A.add, q="s")
    iota(r("od", 0, 96), [[64, 3], [2, 32]], int(UP) + OWN0 + 1)
    iota(r("wn", 48, 176), [[0, 128]], 0)
    iota(r("wn", 784, 976, 3), [[0, 64]], 0)
    iota(r("xt", 256, 512), [[0, 256]], 0)
    iota(r("pat", 40, 56), [[32, 8], [0, 2]], 0)
    ts(r("d8", 0, 16), r("pat", 40, 56), P32, A.add)

    copy("v", r("fi", 0, 4), r("g1", 2, 6))
    ts(r("fi", 4, 6), r("fi", 0, 2), 7 * P, A.bitwise_and)
    ts(r("fi", 6, 8), r("fi", 2, 4), 8, A.arith_shift_right, 7, A.bitwise_and)
    copy("v", r("fa", 10, 14), r("fi", 4, 8))
    for h in range(2):
        act(junk(3 + h), FR, F.Sign, bias=col("fa", 10 + h), scale=-1.0, acc=col("ac", 8 + h))
    ts(r("fa", 14, 16), r("fa", 12, 14), float(LC), A.mult, UP + FAR0, A.add, q="s")
    ts(r("fa", 16, 18), r("fa", 12, 14), 32.0, A.mult, q="s")
    tt(r("ac", 10, 12), r("ac", 4, 6), r("ac", 8, 10), A.subtract)
    for h in range(2):
        ts(r("sp", 128 + 32 * h, 160 + 32 * h), CHALF, col("ac", 10 + h), A.mult, col("fa", 14 + h), A.add)
    tr(FL, r("sp", 128, 192))
    copy("v", r("fl2", 0, 2), r("jo", 0, 2))
    copy("s", r("dv", 64, 96), (FL, r("fl2", 0, 2)))

    for i in (0, 2):
        put("v", lambda e, i=i: g.vector.transpose(T.rl3[:, i:i + 2, :], ap(r("er", 45, 77))), [r("er", 45, 77)], [r("rl3", 16 * i, 16 * i + 32)])
    put("v", lambda e: g.vector.transpose(ap(r("rl2", 64, 96)), T.rl3[:, rank % 2:4:2, :]), [r("rl3", 0, 64)], [r("rl2", 64, 96)])
    for a in range(4):
        ts(blk("rep", 0, 21, a), blk("rl2", 75, 96, rank // 2), -256.0 * rank, A.add, 255.0, A.min)
    pick(r("slc", 0, 336), r("sls", 0, 336), r("qx", 0, 256), r("sx", 0, 256), r("rep", 0, 21))
    for s, l, arr in (("slc", "gq", "ac0"), ("sls", "gs", "as0")):
        send_each([(d, r(s, LC * i, LC * i + LC), r(l, *slot(d, LC, FAR0))) for i, d in enumerate(peers)], arr, r(l, FAR0, LAND0))
    for b in range(4):
        quant("qa", "sa", 128 * b, 128 * b + 128, r("at", 512 * b, 512 * b + 512))
    quant("qw", "sw", 0, 128, r("wt", 0, 512))
    mm("py", 0, QW, QX)
    copy("s", r("yt", 0, 256), r("py", 0, 256))

    for t in range(R):
        W, at, po = LAND0 + 224 * t, OWN0 + 64 * t, 16 * t
        ndl = r("po", po + 6, po + 8)
        copy("s", r("dv", 0, 64), (r("ol", 0, 256), r("dl", 0, 4)))
        tt(r("lg", 0, 64), (r("et", 0, 256), r("dl", 0, 4)), r("d16", 0, 64), A.mult)
        for h in range(2):
            scan(r("dz", 47 + 64 * h, 63 + 64 * h), r("lg", 16 * h, 16 * h + 16), r("lg", 32 + 16 * h, 48 + 16 * h), 0.0, A.add, A.add)
        win = (r("er", 72 + 8 * t, 79 + 8 * t), r("c01", 4, 8)) if t else (r("er", 0, 56), r("c01", 0, 4))
        tt(r("tg", 0, 64), win, r("mk", 64 * (t % 2), 64 * (t % 2) + 64), A.mult)
        put("v", lambda e: g.vector.transpose(T.dz[:, :, 30:62], ap(r("tg", 0, 64))), [r("tg", 0, 64)], [r("dz", 30, 62), r("dz", 94, 126)])
        for h in range(2):
            scan(r("zo", 40 * h, 40 * h + 34), r("dz", 30 + 64 * h, 64 + 64 * h), r("fz", 34 * h, 34 * h + 34), col("ok", h) if t else 0.0, A.add, A.add)
            size(r("sp", 192 + 32 * h, 224 + 32 * h), col("zo", 40 * h + 33))
        exchange("z", 0, r("sp", 192, 256), 4)
        for h in range(2):
            o, zt = 256 * h, col("sp", 192 + 32 * h)
            ts(r("dd", 64 * h, 64 * h + 64), r("jj", 64 * h, 64 * h + 64), zt, A.mult, zt, A.add, q="s")
            tt(r("mm_", o, o + 64), r("z", 0, 64), r("dd", 64 * h, 64 * h + 64), A.is_gt)
            for d in range(1, 4):
                ts(r("mm_", o + 64 * d, o + 64 * d + 64), r("z", 64 * d, 64 * d + 64), zt, A.subtract, col("cf", 31 + d), A.is_gt)
            scan(r("cx", 128 * h, 128 * h + 128), r("mm_", o, o + 128), r("mm_", o + 128, o + 256), 0.0, A.add, A.add)
        if t:
            const(r("wn", 64, 160), 0.0)
            const(r("wn", 832, 928, 3), 0.0)
        for h in range(2):
            ts(r("so", h, 8, 2), r("kk", 4, 8), col("cx", 128 * h + 127), A.add, 3.0, A.mult)
        scatter(r("wn", 64, 1600), r("so", 0, 8), r("dv", 0, 128))
        tr(r("wt_", 0, 96), r("wn", 64, 160))
        tr(r("wt_", 96, 224), r("wn", 48, 176))
        tr(r("wt_", 224, 256), r("wn", 832, 928, 3))
        tr(r("wt_", 256, 320), r("wn", 784, 976, 3))
        copy("v", r("wx", 0, 80, 4), r("wt_", 0, 320, 16))
        for d in (1, 3):
            for a in range(4):
                b = (a + d) % 4
                copy("vs"[a % 2], r("wx", d, 80, 4, 32 * a, 32 * a + 32), r("wt_", 0, 320, 16, 32 * b, 32 * b + 32))
        copy("s", r("wx", 2, 80, 4, 0, 64), r("wt_", 0, 320, 16, 64, 128))
        copy("s", r("wx", 2, 80, 4, 64, 128), r("wt_", 0, 320, 16, 0, 64))
        scan(r("sm", 0, 80), r("wm", 0, 80), r("wx", 0, 80), 0.0, A.mult, A.add)
        ts(r("po", po, po + 16), (r("sm", 0, 80), r("fo", 0, 1)), -UP, A.add)
        ts(col("ok", 4 + t), col("sm", 63), -UP, A.add, q="s")
        if t < 2:
            send_all(col("ok", 4 + t), "an", 8 * t, "an%d" % t)
        nq, ns = "nq%d" % t, "ns%d" % t
        pick(r(nq, 0, 96), r(ns, 0, 96), r("gq", 0, W), r("gs", 0, W), r("po", po, po + 6))
        for b in range(4):
            mm("ps", 512 * b, ("qa", "sa", 128 * b, 128 * b + 128), (nq, ns, 0, 128))
        for b in range(4):
            copy("s", r("bbs", 64 * b + 1, 64 * b + 64, 2), (r("bt", 256 * b, 256 * b + 256), ndl))
        scatter(r("ol", 0, 256), ndl, r("od", 32 * t, 32 * t + 32))
        for b in range(4):
            scan(r("sc4", 192 * b, 192 * b + 192, 2), r("c4", 0, 96), r("ps", 512 * b, 512 * b + 96), 0.0, A.mult, A.add)
        for b in range(4):
            scan(r("xt", b, 256, 4), r("sc4", 192 * b + 1, 192 * b + 192, 3), r("bbs", 64 * b, 64 * b + 64), 0.0, A.mult, A.add)
        new = ("xq%d" % t, "xs%d" % t, 0, 128) if t < 2 else ("gq", "gs", at, at + 128)
        quant(*new, r("xt", 0, 512))
        if t < 2:
            mm("px", 0, QU, new)
            tr(r("ec", 32 * t, 32 * t + 32), r("px", 1, 64, 2))
            send_all(col("ec", 32 * t), "er", 80 + 8 * t, "ae%d" % t)
            pick(r("sq%d" % t, 0, 32), r("ss%d" % t, 0, 32), r(new[0], 0, 64), r(new[1], 0, 64), r("odd", 0, 2))
            for s, n, arr in (("sq%d" % t, "gq", "ac%d" % (t + 1)), ("ss%d" % t, "gs", "as%d" % (t + 1))):
                send_all(r(s, 0, 32), n, W, arr)
            quant("gq", "gs", at, at + 128, r("xt", 0, 512))
            copy("s", r("nw", 0, 32), r("px", 1, 64, 2))
            scatter(r("et", 0, 256), ndl, r("nw", 0, 32))
        mm("py", 0, QW, new)
        copy("s", r("nw", 32, 64), r("py", 1, 64, 2))
        scatter(r("yt", 0, 256), ndl, r("nw", 32, 64))
        dma([("y", T.nd[t:t + 1, :], r("ok", 4 + t, 5 + t, 1, 0, 32))])
        if t < 2:
            m = r("mk", 64 * ((t + 1) % 2), 64 * ((t + 1) % 2) + 64)
            tt(m, (r("an", 8 * t, 8 * t + 7), r("c01", 4, 8)), r("fr", 192, 256), A.is_equal)
            ts(r("rel", 0, 64), m, col("cf", 50 + t), A.mult)
            tr(r("rel", 64, 128), r("rel", 0, 64))
            scan(r("rel", 128, 192), r("ft", 64, 128), r("rel", 64, 128), 0.0, A.mult, A.add)
            for h in range(2):
                v = col("rel", 159 + 32 * h)
                ts(col("ok", h), v, 0.5, A.is_lt, col("zo", 40 * h + 31), A.mult)
                ts(r("sp", 128 + 32 * h, 160 + 32 * h), CONE, v, A.mult, col("fa", 16 + h), A.add)
            tr(FL, r("sp", 128, 192))
            tt(r("dv", 64, 96), (FL, r("fl2", 0, 2)), r("dv", 64, 96), A.max)

    for c in (0, 128):
        copy("s", r("og", c, c + 128), (r("ol", 0, 256), r("d8", c // 16, c // 16 + 8)))
        tr(r("ogt", c, c + 128), r("og", c, c + 128))
        ts(r("oo", c // 16, c // 16 + 8), r("ogt", c, c + 128, 16), -UP, A.add)
        pick(r("occ", c, c + 128), r("ocs", c, c + 128), r("gq", 0, FAR0), r("gs", 0, FAR0), r("oo", c // 16, c // 16 + 8))
        dma([("y", T.oc[:, 4 * c:4 * c + 512], r("occ", c, c + 128))])
    dma([("y", T.osc[4 * k:4 * k + 4, :], r("ocs", 0, 256, 1, 32 * k, 32 * k + 4)) for k in range(4)])
    dma([("s", T.y[:], r("yt", 0, 256))])
    flush()
    for sem, c in cnt.items():
        if known["g"].get(sem, 0) < c:
            g.wait_ge(T.sem[sem], c)
